import numpy as np, ml_dtypes
CORES = [24,25,26,27,28,29,30,31]
N = 8
BF = ml_dtypes.bfloat16
W, S, P, M, RO = 4096, 128, 32, 4, 5
DIST = (1, 3, 6)
ST = 16 // M
def rho(d, h):
    return (((d * (2 * h + 1)) >> 1) + 613 * h) & (W - 1)
def lay(a):
    n = a.shape[-1]; return np.ascontiguousarray(a.reshape(N, 8, S // 16, 16, n).transpose(0, 1, 3, 2, 4)).reshape(N, 128, -1)
def unlay(a, n):
    return np.ascontiguousarray(a.astype(np.int64).reshape(N, 8, 16, S // 16, n).transpose(0, 1, 3, 2, 4)).reshape(N, 8, S, n)
def records(x):
    return np.ascontiguousarray(x.astype(np.int16).transpose(0, 1, 3, 2)).reshape(N * 8 * W, 16)
def heard(rec, d, h):
    return rec[np.arange(N * 8).reshape(N, 8, 1, 1) * W + rho(d, h)]
def apart(u, v):
    return np.add.reduce(np.abs(u - v), axis=-1, dtype=np.int64)
def pack(x, d, h, th, a):
    return {"X": np.ascontiguousarray(x.reshape(N, 128, W)).astype(np.float32).astype(BF), "D": lay(d).astype(np.int32), "H": lay(h).astype(np.int32),
            "th": lay(th[..., None]).astype(np.int32), "A": lay(a[..., None]).astype(np.int32)}
def runs(rng, stay):
    new = rng.random((N, 8, S, P)) >= stay; new[..., 0] = True
    i = np.maximum.accumulate(np.where(new, np.arange(P), 0), axis=-1)
    return np.take_along_axis(rng.integers(0, 16, (N, 8, S, P)), i, -1)
def setup_inputs(rng):
    x = rng.integers(-128, 128, (N, 8, 16, W)); d = rng.integers(0, W, (N, 8, S, P))
    h = runs(rng, rng.choice(np.array([0.3, 0.6, 0.8, 0.95]), (N, 8, S, 1)))
    return pack(x, d, h, rng.integers(1000, 1900, (N, 8, S)), rng.integers(0, 64, (N, 8, S)))
def setup_inputs_spread(rng):
    x = np.floor(rng.integers(-128, 128, (N, 8, 16, W)) * np.exp2(-rng.integers(0, 7, (N, 8, 1, W)).astype(np.float64))).astype(np.int64)
    d = np.floor(W * rng.random((N, 8, S, P)) ** rng.integers(1, 5, (N, 8, S, 1))).astype(np.int64); d = np.minimum(d, W - 1)
    h = runs(rng, rng.random((N, 8, S, 1)))
    th = np.minimum(np.floor(np.exp2(12 * np.sqrt(rng.random((N, 8, S))))).astype(np.int64) - 1, 4079)
    return pack(x, d, h, th, rng.integers(0, 64, (N, 8, S)))
def setup_inputs_ends(rng):
    kind = rng.integers(0, 10, (N, 8, 1, W)); top = np.where(kind < 3, 0, np.where(kind < 6, 1, rng.integers(0, 2, (N, 8, 16, W))))
    x = np.where(top == 1, 127, -128); x = x + np.where((kind == 9) & (rng.random((N, 8, 16, W)) < 0.5), 1 - 2 * top, 0)
    end = (W - 1) * rng.integers(0, 2, (N, 8, S, P))
    d = np.where(rng.random((N, 8, S, P)) < 0.8, end, rng.integers(0, W, (N, 8, S, P)))
    h = 15 * (runs(rng, 0.8) & 1); th = 4079 * rng.integers(0, 2, (N, 8, S)); a = 63 * rng.integers(0, 2, (N, 8, S))
    six = np.arange(16); c0 = rho(0, six); c1 = rho(W - 1, six); both = np.concatenate([c0, c1])
    last = int(np.argmax(rho(np.arange(W), 15) == W - 1)); d[:, :, S - 2, P - 1] = last; h[:, :, S - 2, P - 1] = 15
    chain = [0, W - 1, 0]
    for j in range(RO): chain.append((13 * chain[-1] + 4080) & (W - 1))
    far = rho(np.array(chain)[:, None], six[None, :]).reshape(-1)
    x[N - 1, 7][:, far] = 127; x[N - 1, 7][:, W - 1] = 127
    x[N - 2, 7][:, both] = -128
    for m in (1, 2, M - 1): x[N - 2, 7][:, [c0[ST * m], c1[ST * m]]] = 127
    for l in (0, S - 1):
        for q in [(N - 1 + j) % N for j in DIST]:
            x[q, 7][:, [c0[15], c1[15]]] = -128; d[q, 7, l] = end[q, 7, l]; h[q, 7, l] = 15; th[q, 7, l] = 4079; a[q, 7, l] = 63
        d[N - 1, 7, l] = end[N - 1, 7, l]; d[N - 1, 7, l, 0] = 0; h[N - 1, 7, l] = 15; th[N - 1, 7, l] = 0; a[N - 1, 7, l] = 63
    for l in (1, S - 3):
        for q in (N - 2, N - 1): d[q, 7, l] = end[q, 7, l]; h[q, 7, l] = 15; th[q, 7, l] = 4079; a[q, 7, l] = 0
    x[0, 7][:, W - 1] = -128; x[0, 7][:, 0] = 127
    for q in (0, N - 1): d[q, 7, S - 2, :P - 1] = 0; h[q, 7, S - 2, :P - 1] = 0; th[q, 7, S - 2] = 4079; a[q, 7, S - 2] = 0
    x[N - 1, 6][:, both] = 127; x[0, 6][:, both] = -128; x[N - 1, 6, 15, c1[ST]] = 126
    for l in (0, S - 1):
        for q in (0, N - 1): d[q, 6, l] = 0; d[q, 6, l, P - 1] = W - 1; h[q, 6, l] = 15; th[q, 6, l] = 4079; a[q, 6, l] = 0
    return pack(x, d, h, th, a)
def setup_inputs_corners(rng):
    k = np.arange(P); x = rng.integers(-128, 128, (N, 8, 16, W)); x[..., 0::2] = rng.integers(-4, 5, (N, 8, 16, W // 2))
    u = rng.integers(0, 16, (N, 8, S, 1)); v = rng.integers(0, 16, (N, 8, S, 1)); c = rng.integers(0, P, (N, 8, S, 1)); e = c + rng.integers(1, P, (N, 8, S, 1)); full = np.zeros((N, 8, S, P), np.int64)
    h = np.choose(rng.integers(0, 6, (N, 8, S, 1)) + full, [u + full, np.where(k % 2 == 0, u, v) + full, (u + k) & 15, np.where(k < c, u, v) + full, np.where((k >= c) & (k < e), v, u) + full, runs(rng, 0.7)])
    first = rng.choice(np.array([0, 0, 1, P // 2, P // 2 + 1, P - 2, P - 1, P - 1, P]), (1, 8, S, 1)) + np.zeros((N, 1, 1, 1), np.int64)
    loud = np.where(k < first, 0, np.where(k == first, 1, rng.integers(0, 2, (N, 8, S, P))))
    d = rng.integers(0, W, (N, 8, S, P)); d = np.where((rho(d, h) & 1) != loud, d ^ 2, d)
    a = rng.choice(np.array([0, 1, 30, 31, 32, 62, 63]), (N, 8, S))
    s = heard(records(x), d, h); far = apart(s, s[(np.arange(N) + DIST[0]) % N])
    at = np.take_along_axis(far, np.minimum(first, P - 1), -1)[..., 0]
    exact = np.minimum(np.maximum(at - (a & 31) - rng.integers(0, 2, (N, 8, S)), 0), 4079)
    w = rng.random((N, 8, S)); th = np.where(w < 0.45, rng.integers(300, 600, (N, 8, S)), np.where(w < 0.9, exact, np.where(w < 0.95, 0, 4079)))
    return pack(x, d, h, th, a)
def setup_inputs_alike(rng):
    x = np.take_along_axis(rng.integers(0, 2, (N, 8, 16, 7)), np.broadcast_to(rng.integers(0, 7, (N, 8, 1, W)), (N, 8, 16, W)), 3); x[:, 3] = x[0:1, 3]
    d = rng.integers(0, W, (N, 8, S, P)); h = runs(rng, 0.7)
    d[:, 5] = d[:, 5, :, :1]; d[:, :, ::2] = d[0:1, :, ::2]; h[:, :, ::4] = h[0:1, :, ::4]
    return pack(x, d, h, rng.integers(0, 10, (N, 8, S)), rng.choice(np.array([0, 1, 2, 32, 33, 63]), (N, 8, S)))
def setup_inputs_crowds(rng):
    x = rng.integers(-128, 128, (N, 8, 16, W)); d = rng.integers(0, W, (N, 8, S, P)); h = runs(rng, 0.7)
    th = rng.integers(1000, 1900, (N, 8, S)); a = rng.integers(0, 64, (N, 8, S)); o = [int(g) for g in rng.permutation(8)]
    for g in (o[0], o[1], o[4], o[5]): h[:, g] = rng.integers(0, 16, (N, S, 1)); th[:, g] = 0
    for g in (o[3], o[4]):
        x[:, g] = (32 * rng.permutation(8)[:N, None] - 128 + rng.integers(0, 16, (N, 16)))[..., None]; th[:, g] = 0
    still = np.zeros((N, 8, S), bool); still[:, o[2]] = True; still[int(rng.integers(0, 2))::2, o[5]] = True
    still[:, o[6]] = True; still[np.arange(N), o[6], rng.integers(0, S, N)] = False; th[:, o[6]] = 0
    return pack(x, d, h, np.where(still, 4079, th), np.where(still, rng.choice(np.array([1, 31, 63]), (N, 8, S)), a))
def check_inputs(d):
    bad = []
    for k, lo, hi in (("X", -128, 127), ("D", 0, W - 1), ("H", 0, 15), ("th", 0, 4079), ("A", 0, 63)):
        v = np.asarray(d[k]).astype(np.float64)
        if not (np.min(v) >= lo and np.max(v) <= hi): bad.append("range of " + k)
        elif np.any(v != np.floor(v)): bad.append("whole numbers of " + k)
    return bad
def reference(X, D, H, th, A):
    rec = records(X.astype(np.float32).reshape(N, 8, 16, W))
    d = unlay(D, P); h = unlay(H, P); lim = unlay(th, 1); a = unlay(A, 1); k = np.arange(P)
    for rnd in range(RO):
        x = heard(rec, d, h); y = x[(np.arange(N) + DIST[rnd % 3]) % N]; e = apart(x, y)
        over = e > lim + (a & 31); some = np.any(over, axis=-1, keepdims=True); p = np.argmax(over, axis=-1)[..., None]
        hp = np.take_along_axis(h, p, -1); ep = np.take_along_axis(e, p, -1)
        same = h == hp; c = np.add.accumulate(np.where(same, 0, 1), axis=-1)
        run = same & (c == np.take_along_axis(c, p, -1)) & some
        old = np.add.reduce(np.where(run, e, 0), axis=-1, keepdims=True)
        hm = (hp + 1 + ST * np.arange(M) + (ep & (ST - 1))) & 15
        em = np.stack([np.add.reduce(np.where(run, apart(heard(rec, d, hm[..., m:m + 1]), y), 0), axis=-1) for m in range(M)], axis=-1)
        best = np.argmin(em, axis=-1)[..., None]
        better = some & (np.take_along_axis(em, best, -1) < old); mut = some & ~better
        h = np.where(run & better, np.take_along_axis(hm, best, -1), np.where(run & mut & (k >= p), hm[..., :1], h))
        d = np.where(mut & (k == p), (13 * d + e) & (W - 1), d)
        a = a + np.where(mut, 1, 0)
    return {"yD": lay(d).astype(np.float32), "yH": lay(h).astype(np.float32), "yA": lay(a).astype(np.float32)}

@@ -1,0 +1,535 @@
+from concourse.bass import DstId, RemoteDMATransfer
+from concourse.mybir import dt, AluOpType, AxisListType, ActivationFunctionType
+
+A = AluOpType
+F = ActivationFunctionType
+RO = 5
+DIST = (1, 3, 6)
+COPIES = 7
+VCOPIES = 6
+MAGIC = 50331648.0
+WIN = [16384, 20480, 24576, 28672]
+VT = (0, 1)
+ORDER = (0, 2, 1, 3)
+XP = 4
+XV = (3,)
+VPN = 4
+SPN = 4
+PEADD = True
+
+SCRATCH = {"Xw": ("sbuf", [128, 4096 * COPIES], "bfloat16"),
+           "Dl": ("sbuf", [128, 256], "int32"), "Hl": ("sbuf", [128, 256], "int32"),
+           "tl": ("sbuf", [128, 8], "int32"), "Al": ("sbuf", [128, 8], "int32"), "thm": ("sbuf", [128, 8], "float32")}
+for _t in range(3):
+    SCRATCH["x%d" % _t] = ("sbuf", [128, 4096], "bfloat16")
+for _t in range(RO):
+    SCRATCH["y%d" % _t] = ("sbuf", [128, 4096], "bfloat16")
+for _n in ("ones", "Ib", "Bt", "Bb", "Ss", "nIb", "I16", "keep"):
+    SCRATCH[_n] = ("sbuf", [128, 128], "bfloat16")
+for _n in ("Ih", "Bh", "V1", "Tri"):
+    SCRATCH[_n] = ("sbuf", [128, 128], "float16")
+SCRATCH["I4"] = ("sbuf", [128, 384], "float16")
+SCRATCH["B4"] = ("sbuf", [128, 16], "float16")
+SCRATCH["B16"] = ("sbuf", [128, 4], "float16")
+for _n in ("selt", "sel", "sel2", "seln"):
+    SCRATCH[_n] = ("sbuf", [128, 8], "bfloat16")
+SCRATCH["cst"] = ("sbuf", [128, 16], "int32")
+SCRATCH["rowm"] = ("sbuf", [128, 512], "bfloat16")
+SCRATCH["rowg"] = ("sbuf", [128, 128], "bfloat16")
+SCRATCH["rowj"] = ("sbuf", [128, 8], "bfloat16")
+SCRATCH["If"] = ("sbuf", [128, 128], "float32")
+for _q in range(2):
+    for _n in range(4):
+        SCRATCH["d%d%d" % (_n, _q)] = ("sbuf", [128, 2048], "bfloat16")
+        SCRATCH["r%d%d" % (_n, _q)] = ("sbuf", [128, 2048], "bfloat16")
+    for _n, _w, _d in (("Di", 128, "int32"), ("Hh", 128, "bfloat16"), ("fl", 128, "bfloat16"),
+                       ("sg", 128, "bfloat16"), ("Gs", 128, "float32"), ("ths", 128, "float32"), ("ov", 128, "float16"),
+                       ("fi", 128, "float16"), ("PG", 128, "float16"), ("Pe", 128, "float16"), ("ru", 128, "float16"),
+                       ("mo", 128, "float16"), ("mz", 512, "float16"), ("pr", 128, "float32"), ("ls", 384, "float32"),
+                       ("lz", 512, "uint16"), ("lx", 128, "uint16"), ("PD", 128, "float32"), ("ai", 128, "int32"),
+                       ("ah", 128, "float16"), ("rn", 128, "bfloat16"), ("ax", 128, "bfloat16"), ("tx", 128, "float16"),
+                       ("xi", 128, "int32"), ("cf", 72, "float32"), ("ci", 128, "int32"), ("ya", 4, "float32")):
+        SCRATCH["%s%d" % (_n, _q)] = ("sbuf", [128, _w], _d)
+    for _n in ("pA", "pZ", "pN", "pS"):
+        SCRATCH["%s%d" % (_n, _q)] = ("psum", [128, 512], "float32")
+
+SEMAPHORES = ["sv", "ss", "sp", "sg", "out", "ldD", "ldH", "ldt", "ldA"]
+SEMAPHORES += ["lx%d" % k for k in [0] + list(range(VCOPIES + 1, COPIES))] + ["loc%d" % t for t in range(RO)]
+SEMAPHORES += ["ar%d%d%d" % (t, q, h) for t in range(RO) for q in range(2) for h in range(XP)]
+
+CY = 0.83 * 1.2
+GC = 1.56
+HOP = 120.0
+SEED = 1
+NOISE = 0.0
+BIAS = 7000.0
+SLACK = 200.0
+
+
+def schedule(ops):
+    n = len(ops)
+    succ = [[] for _ in range(n)]
+    for i, o in enumerate(ops):
+        for j in o["hard"] | o["order"]:
+            succ[j].append(i)
+    prio = [0.0] * n
+    for i in range(n - 1, -1, -1):
+        prio[i] = ops[i]["cost"] + ops[i]["lat"] + max([prio[j] + HOP for j in succ[i]], default=0.0)
+    rnd = SEED
+    for i in range(n):
+        rnd = (rnd * 1103515245 + 12345) % 2147483648
+        prio[i] += (BIAS if ops[i]["ch"] == 0 else 0.0) + NOISE * (rnd / 2147483648.0 - 0.5)
+    left = [len(o["hard"] | o["order"]) for o in ops]
+    ready = [0.0] * n
+    avail = {}
+    pend = {}
+    for i in range(n):
+        if left[i] == 0:
+            pend.setdefault(ops[i]["q"], []).append(i)
+    done = []
+    while len(done) < n:
+        best = None
+        for q, lst in pend.items():
+            if not lst:
+                continue
+            av = avail.get(q, 0.0)
+            m = min(max(av, ready[i]) for i in lst)
+            c = max((i for i in lst if max(av, ready[i]) <= m + SLACK), key=lambda i: prio[i])
+            st = max(av, ready[c])
+            if best is None or st < best[0]:
+                best = (st, c)
+        st, c = best
+        o = ops[c]
+        pend[o["q"]].remove(c)
+        avail[o["q"]] = st + o["cost"]
+        o["st"] = st
+        end = st + o["cost"] + o["lat"]
+        done.append(c)
+        for j in succ[c]:
+            hop = 0.0 if c not in ops[j]["hard"] else (60.0 if ops[j]["q"] == o["q"] else HOP)
+            ready[j] = max(ready[j], (end if c in ops[j]["hard"] else st) + hop)
+            left[j] -= 1
+            if left[j] == 0:
+                pend.setdefault(ops[j]["q"], []).append(j)
+    return done
+
+
+def rank_program(g, core, T, topo):
+    rank = T.rank_of(core)
+    if rank is None:
+        return
+    n_ranks = len(T.cores)
+    ops = []
+    lastw, readers, bankacc = {}, {}, {}
+    chunk = [0]
+
+    def op(q, cost, fn, R=(), W=(), banks=(), lat=0.0, sem=None, inc=1):
+        i = len(ops)
+        hard, order = set(), set()
+        for k in R:
+            if k in lastw:
+                hard.add(lastw[k])
+        for k in W:
+            if k in lastw:
+                hard.add(lastw[k])
+            hard.update(readers.get(k, ()))
+        for b in banks:
+            d = bankacc.setdefault(b, {})
+            for e, j in d.items():
+                if e == q:
+                    order.add(j)
+                else:
+                    hard.add(j)
+            d[q] = i
+        for k in R:
+            readers.setdefault(k, []).append(i)
+        for k in W:
+            lastw[k] = i
+            readers[k] = []
+        hard.discard(i)
+        ops.append({"q": q, "cost": cost, "fn": fn, "hard": hard, "order": order - hard, "lat": lat, "sem": sem, "inc": inc, "ch": chunk[0]})
+        return i
+
+    V, S, P = g.vector, g.scalar, g.tensor
+
+    def cyc(n):
+        return max(n, 64) * CY
+
+    def tt(out, a, b, o, R, W, n, banks=()):
+        op("V", cyc(n if banks else 2 * n), lambda: [V.tensor_tensor(out, a, b, o)], R, W, banks)
+
+    def ts(out, a, s1, s2, o0, o1, R, W, n, banks=(), half=False):
+        def f():
+            if o1 is None:
+                return [V.tensor_scalar(out, a, s1, None, o0)]
+            return [V.tensor_scalar(out, a, s1, s2, o0, o1)]
+        op("V", cyc(n / 2 if half else n), f, R, W, banks)
+
+    def cp(out, a, R, W, n, banks=(), half=False):
+        op("V", cyc(n / 2 if half else n), lambda: [V.tensor_copy(out, a)], R, W, banks)
+
+    def act(out, a, fn, R, W, n, banks=(), scale=None):
+        def f():
+            if scale is None:
+                return [S.activation(out, a, fn)]
+            return [S.activation(out, a, fn, 0.0, scale)]
+        op("S", cyc(n), f, R, W, banks)
+
+    def mms(lst, R, W, banks):
+        def f():
+            return [P.matmul(o, l, r, a, b) for (o, l, r, a, b, c) in lst]
+        op("P", sum(x[5] for x in lst) * 0.417 * 1.2 + 5.0 * len(lst), f, R, W, banks)
+
+    def load(out, in_, sem, W, lat):
+        op("Y", 60.0, lambda: g.sync.dma_start(out, in_), (), W, (), lat, sem, 16)
+
+    load(T.Dl[:], T.D[:], "ldD", ["Dl"], 2000.0)
+    load(T.Hl[:], T.H[:], "ldH", ["Hl"], 2000.0)
+    load(T.tl[:], T.th[:], "ldt", ["tl"], 2200.0)
+    load(T.Al[:], T.A[:], "ldA", ["Al"], 2200.0)
+    load(T.Xw[:, 0:4096], T.X[:], "lx0", ["X0"], 6500.0)
+
+    def fill(ap, val, W, n):
+        op("V", cyc(n), lambda: [V.memset(ap, val)], (), W)
+
+    fill(T.ones[:], 1.0, ["ones"], 64)
+    fill(T.rowm[0:1, :], -2040.0, ["rowm"], 256)
+    fill(T.rowg[0:1, :], 16.5, ["rowg"], 64)
+    fill(T.rowj[0:1, 0:4], -1.5, ["rowj0"], 64)
+    fill(T.rowj[0:1, 4:8], 0.5, ["rowj1"], 64)
+
+    def sel(out, in_, pat, cmp, base, cm, R, W, n):
+        op("G", 200.0 + 2 * n * CY, lambda: [g.affine_select(out, in_, pat, cmp, 0.0, base, cm)], R, W)
+
+    sel(T.Ib[:], T.ones[:], [[-1, 128]], A.is_equal, 0, 1, ["ones"], ["Ib"], 128)
+    sel(T.keep[:], T.ones[:], [[0, 4], [1, 32]], A.is_gt, 0, 0, ["ones"], ["keep"], 128)
+    sel(T.selt[:], T.ones[:, 0:8], [[-16, 8]], A.is_ge, 0, 1, ["ones"], ["selt"], 8)
+    sel(T.sel[:], T.selt[:], [[16, 8]], A.is_ge, 15, -1, ["selt"], ["sel"], 8)
+    sel(T.Bt[:], T.ones[:], [[-32, 4], [0, 32]], A.is_ge, 0, 1, ["ones"], ["Bt"], 128)
+    sel(T.Bb[:], T.Bt[:], [[32, 4], [0, 32]], A.is_ge, 31, -1, ["Bt"], ["Bb"], 128)
+    sel(T.Ss[:], T.Bb[:], [[1, 128]], A.is_ge, -1, -1, ["Bb"], ["Ss"], 128)
+    op("G", 200.0, lambda: [g.iota(T.cst[:], [[4, 4], [0, 4]], 19, 0)], (), ["cst"])
+
+    for q in range(2):
+        c0 = slice(128 * q, 128 * q + 128)
+        ts(T["Di%d" % q][:], T.Dl[:, c0], 613.0, None, A.add, None, ["Dl"], ["Di%d" % q], 128)
+        ts(T["Hh%d" % q][:], T.Hl[:, c0], 0.5, None, A.add, None, ["Hl"], ["Hh%d" % q], 128)
+
+    def konst():
+        ts(T.nIb[:], T.Ib[:], -1.0, None, A.mult, None, ["Ib"], ["nIb"], 128, half=True)
+        ts(T.I16[:], T.Ib[:], 16.0, None, A.mult, None, ["Ib"], ["I16"], 128, half=True)
+        cp(T.Ih[:], T.Ib[:], ["Ib"], ["Ih"], 128, half=True)
+        cp(T.If[:], T.Ib[:], ["Ib"], ["If"], 128)
+        for n in (1, 2, 3):
+            ts(T.I4[:, 128 * n - 128:128 * n], T.Ib[:], 4.0 * n, None, A.mult, None, ["Ib"], ["I4%d" % n], 128, half=True)
+        ts(T.sel2[:], T.sel[:], 2.0, None, A.mult, None, ["sel"], ["sel2"], 8)
+        ts(T.seln[:], T.sel[:], -1.0, None, A.mult, None, ["sel"], ["seln"], 8)
+        tt(T.V1[:], T.Ib[:], T.Ss[:], A.subtract, ["Ib", "Ss"], ["V1"], 128)
+        tt(T.Tri[:], T.Ib[:], T.Ss[:], A.add, ["Ib", "Ss"], ["Tri"], 128)
+        cp(T.Bh[:], T.Bb[:], ["Bb"], ["Bh"], 128, half=True)
+        for n in range(4):
+            cp(T.B4[:, 4 * n:4 * n + 4], T.Bb[:, 0:128:32], ["Bb"], ["B4%d" % n], 4)
+        ts(T.B16[:], T.Bb[:, 0:128:32], 16.0, None, A.mult, None, ["Bb"], ["B16"], 4)
+        ts(T.thm[:], T.tl[:], -2040.0, None, A.add, None, ["tl"], ["thm"], 8)
+        for q in range(2):
+            cp(T["ci%d" % q][:, 120:124], T.Al[:, 4 * q:4 * q + 4], ["Al"], ["A%d" % q], 4)
+            fill(T["fl%d" % q][:, 0:1], 0.0, ["fl0%d" % q], 64)
+            for b in range(4):
+                ts(T["tx%d" % q][:, 32 * b:32 * b + 32], T.ones[:, 0:32], T.thm[:, 4 * q + b:4 * q + b + 1], None, A.mult, None,
+                   ["ones", "thm"], ["tx%d%d" % (b, q)], 32)
+
+    B4 = ["B40", "B41", "B42", "B43"]
+
+    def xpart(t, q):
+        K = lambda s: "%s%d" % (s, q)
+        chunk[0] = q
+        xb = "x%d" % (t % 3)
+        tt(T[K("PD")][:], T[K("Di")][:], T[K("Hh")][:], A.mult, [K("Di"), K("Hh")], [K("PD")], 128)
+        ts(T[K("xi")][:], T[K("PD")][:], -306.75, None, A.add, None, [K("PD")], [K("xi")], 128)
+        ts(T[K("xi")][:], T[K("xi")][:], 4095, None, A.bitwise_and, None, [K("xi")], [K("xi")], 128)
+        cp(T[K("lx")][:], T[K("xi")][:], [K("xi")], [K("lx")], 128)
+        w = 2048 // XP
+        u = DIST[t % 3]
+        dst = T.cores[(rank - u) % n_ranks]
+        rid, pid = topo.addr(dst)[:2]
+        for h in range(XP):
+            cs = slice(2048 * q + w * h, 2048 * q + w * h + w)
+            src = T.Xw[:, 0:4096].indirect(T[K("lx")][:, (w // 16) * h:(w // 16) * (h + 1)])
+            R, W = ["X0", K("lx")] + (["loc%d" % (t - 3)] if t >= 3 else []), ["%s_%d%d" % (xb, q, h)]
+            if h in XV or (t == 0 and q == 0 and h % 2 == 1):
+                op("V", 60.0 + w * GC * CY, lambda src=src, cs=cs: [V.tensor_copy(T[xb][:, cs], src)], R, W)
+            else:
+                op("S", 80.0 + w * GC * CY, lambda src=src, cs=cs: [S.activation(T[xb][:, cs], src, F.Copy)], R, W)
+            ar = "ar%d%d%d" % (t, q, h)
+            i = op("G", 900.0, lambda cs=cs, ar=ar: g.remote_dma(T["y%d" % t][:, cs], T[xb][:, cs], T.sem[ar], T.sem["loc%d" % t],
+                                                                  pid, rid, topo.mask(core, dst)),
+                   ["%s_%d%d" % (xb, q, h)], [], (), 0.0, None, 0)
+            a = op("arr%s" % ar, 0.0, None, (), ["y%d_%d%d" % (t, q, h)], (), 2200.0, ar, 16)
+            ops[a]["order"].add(i)
+
+    def gpart(t, q):
+        K = lambda s: "%s%d" % (s, q)
+        pA, pZ, A_, Z_ = T[K("pA")], T[K("pZ")], K("pA"), K("pZ")
+        mms([(pA[:, 129:256], T.Ib[:], T[K("Hh")][:, 1:128], True, False, 127),
+             (pA[:, 129:256], T.nIb[:], T[K("Hh")][:, 0:127], False, True, 127)], ["Ib", "nIb", K("Hh")], [K("v")], [A_])
+        ts(T[K("fl")][:, 1:128], pA[:, 129:256], 0.0, None, A.not_equal, None, [K("v")], [K("fl")], 127, [A_])
+        op("V", cyc(64), lambda: [V.tensor_tensor_scan(T[K("sg")][:], T.keep[:], T[K("fl")][:], 0.0, A.mult, A.add)],
+           [K("fl"), K("fl0"), "keep"], [K("sg")])
+        mms([(pA[:, 384:512], T.ones[0:1, :], T.rowg[0:1, :], True, False, 128),
+             (pA[:, 384:512], T[K("Hh")][:], T.Ib[:], False, False, 128),
+             (pA[:, 384:512], T[K("sg")][:], T.I16[:], False, True, 128)],
+            ["ones", "rowg", K("Hh"), K("sg"), "Ib", "I16"], [K("GT")], [A_])
+        act(T[K("Gs")][:], pA[:, 384:512], F.Copy, [K("GT")], [K("Gs")], 128, [A_])
+        ci, cf = T[K("ci")], T[K("cf")]
+        ts(ci[:, 124:128], ci[:, 120:124], 31, None, A.bitwise_and, None, [K("A")], [K("a31")], 4)
+        cp(cf[:, 60:64], ci[:, 124:128], [K("a31")], [K("a31f")], 4)
+        for b in range(4):
+            act(T[K("ax")][:, 32 * b:32 * b + 32], T.ones[:, 0:32], F.Identity, ["ones", K("a31f")], [K("ax%d" % b)], 64, (),
+                cf[:, 60 + b:61 + b])
+        mms([(pA[:, 256:384], T[K("tx")][:], T.Ih[:], True, False, 128),
+             (pA[:, 256:384], T[K("ax")][:], T.Ib[:], False, True, 128)],
+            ["Ih", "Ib"] + [K("tx%d" % b) for b in range(4)] + [K("ax%d" % b) for b in range(4)], [K("GP")], [A_])
+        act(T[K("ths")][:], pA[:, 256:384], F.Copy, [K("GP")], [K("ths")], 128, [A_])
+        ts(T[K("ai")][:], T[K("Di")][:], 1023, None, A.bitwise_and, None, [K("Di")], [K("ai")], 128)
+        cp(T[K("ah")][:], T[K("ai")][:], [K("ai")], [K("ah")], 128)
+        if not PEADD:
+            mms([(pZ[:, 128 * n:128 * n + 128], T.I4[:, 128 * n - 128:128 * n], T[K("ah")][:], True, True, 128) for n in (1, 2, 3)],
+                [K("ah"), "I41", "I42", "I43"], [K("C"), K("Z")], [Z_])
+
+    def epart(t, q):
+        K = lambda s: "%s%d" % (s, q)
+        pA, pN, A_, N_ = T[K("pA")], T[K("pN")], K("pA"), K("pN")
+        xb = T["x%d" % (t % 3)]
+        yb = T["y%d" % t]
+        ab = T["r2%d" % q]
+        for s in range(4):
+            cs = slice(2048 * q + 512 * s, 2048 * q + 512 * s + 512)
+            h = s * XP // 4
+            bk = K("pS") if s % 2 == 0 else N_
+            ks = [K("NN")] if s % 2 else []
+            mms([(T[bk][:], T.Ib[:], xb[:, cs], True, False, 512), (T[bk][:], T.nIb[:], yb[:, cs], False, True, 512)],
+                ["Ib", "nIb", "x%d_%d%d" % (t % 3, q, h), "y%d_%d%d" % (t, q, h)], [K("sub" + bk)] + ks, [bk])
+            act(ab[:, 512 * s:512 * s + 512], T[bk][:], F.Abs, [K("sub" + bk)], [K("r2_%d" % s)], 512, [bk])
+        lst = [(pA[:, 0:128], T.ones[0:1, :], T.rowm[0:1, 0:128], True, False, 128)]
+        for i in range(16):
+            lst.append((pA[:, i:128:16], ab[:, i:2048:16], T.sel[:], False, i == 15, 64))
+        mms(lst, ["ones", "rowm", "sel"] + [K("r2_%d" % s) for s in range(4)], [K("eT")], [A_])
+        tt(T[K("ov")][:], pA[:, 0:128], T[K("ths")][:], A.is_gt, [K("eT"), K("ths")], [K("ov")], 128, [A_])
+        mms([(pA[:, 128:256], T.V1[:], T[K("ov")][:], True, True, 128)], ["V1", K("ov")], [K("v")], [A_])
+        ts(T[K("fi")][:], pA[:, 128:256], 0.0, None, A.max, None, [K("v")], [K("fi")], 128, [A_])
+        tt(T[K("Pe")][:], pA[:, 0:128], T[K("fi")][:], A.mult, [K("eT"), K("fi")], [K("Pe")], 128, [A_])
+        tt(T[K("PG")][:], pA[:, 384:512], T[K("fi")][:], A.mult, [K("GT"), K("fi")], [K("PG")], 128, [A_])
+        mms([(pN[:, 436:444], T.ones[0:1, :], T.rowj[0:1, :], True, False, 64),
+             (pN[:, 436:444], T[K("Pe")][:], T.B4[:, 0:8], False, False, 64),
+             (pN[:, 436:444], T[K("PG")][:], T.B4[:, 0:8], False, True, 64),
+             (pN[:, 400:416], T[K("Pe")][:], T.B4[:], True, True, 64),
+             (pN[:, 384:400], T[K("PG")][:], T.B4[:], True, True, 64)],
+            [K("Pe"), K("PG"), "ones", "rowj0", "rowj1"] + B4, [K("CE"), K("NN")], [N_])
+        ci, cf = T[K("ci")], T[K("cf")]
+        ts(cf[:, 68:72], pN[:, 436:440], MAGIC, -MAGIC, A.add, A.add, [K("CE")], [K("rr")], 4, [N_])
+        tt(cf[:, 48:52], pN[:, 440:444], cf[:, 68:72], A.subtract, [K("CE"), K("rr")], [K("jf")], 4, [N_])
+        pZ, Z_ = T[K("pZ")], K("pZ")
+        prk = [K("pr%d" % b) for b in range(4)]
+        for b in range(4):
+            bs = slice(32 * b, 32 * b + 32)
+            ts(T[K("pr")][:, bs], T[K("Di")][:, bs], cf[:, 48 + b:49 + b], -306.75, A.mult, A.add, [K("Di"), K("jf")], [prk[b]], 32)
+        for n in ORDER:
+            ns = slice(128 * n, 128 * n + 128)
+            if n == 0:
+                cp(T[K("lz")][:, ns], T[K("pr")][:], prk, [K("lz0")], 128)
+            elif PEADD:
+                mms([(pZ[:, ns], T.I4[:, 128 * n - 128:128 * n], T[K("ah")][:], True, False, 128),
+                     (pZ[:, ns], T.If[:], T[K("pr")][:], False, True, 512)], [K("ah"), "If", "I41", "I42", "I43"] + prk, [K("C%d" % n), K("Z")], [Z_])
+                cp(T[K("lz")][:, ns], pZ[:, ns], [K("C%d" % n)], [K("lz%d" % n)], 128, [Z_])
+            else:
+                l = T[K("ls")][:, 128 * n - 128:128 * n]
+                tt(l, pZ[:, ns], T[K("pr")][:], A.add, [K("C")] + prk, [K("ls%d" % n)], 128, [Z_])
+                cp(T[K("lz")][:, ns], l, [K("ls%d" % n)], [K("lz%d" % n)], 128)
+        cp(ci[:, 0:16], pN[:, 400:416], [K("CE")], [K("i1")], 16, [N_])
+        ts(ci[:, 16:32], ci[:, 0:16], 3, None, A.bitwise_and, None, [K("i1")], [K("i2")], 16)
+        tt(ci[:, 32:48], pN[:, 384:400], ci[:, 16:32], A.add, [K("CE"), K("i2")], [K("t3")], 16, [N_])
+        mms([(pA[:, 256:384], T.Bh[:], T[K("PG")][:], True, True, 128)], ["Bh", K("PG")], [K("GP")], [A_])
+        tt(T[K("ru")][:], pA[:, 256:384], T[K("Gs")][:], A.is_equal, [K("GP"), K("Gs")], [K("ru")], 128, [A_])
+        tt(T[K("mo")][:], pA[:, 0:128], T[K("ru")][:], A.mult, [K("eT"), K("ru")], [K("mo")], 128, [A_])
+        mms([(pN[:, 256:384], T[K("fi")][:], T.Ih[:], True, True, 128),
+             (pN[:, 128:256], T[K("fi")][:], T.Tri[:], True, True, 128),
+             (pN[:, 0:128], T[K("ru")][:], T.Ih[:], True, True, 128),
+             (pN[:, 432:436], T[K("mo")][:], T.B16[:], True, True, 64)],
+            ["Ih", "Tri", "B16", K("fi"), K("ru"), K("mo"), K("NN")], [K("FI"), K("FN"), K("RN"), K("OC")], [N_])
+        act(T[K("rn")][:], pN[:, 0:128], F.Copy, [K("RN")], [K("rn")], 128, [N_])
+        tt(ci[:, 48:64], T.cst[:], ci[:, 32:48], A.subtract, ["cst", K("t3")], [K("t2")], 16)
+        ts(ci[:, 64:80], ci[:, 48:64], 12, None, A.bitwise_and, None, [K("t2")], [K("tb")], 16)
+        ts(ci[:, 84:88], pN[:, 384:388], -1.0, None, A.add, None, [K("CE")], [K("gi")], 4, [N_])
+        ts(ci[:, 88:92], ci[:, 84:88], 15, None, A.bitwise_and, None, [K("gi")], [K("hp")], 4)
+        ts(cf[:, 12:16], pN[:, 384:388], 0.5, None, A.is_gt, None, [K("CE")], [K("sm")], 4, [N_])
+        tt(T[K("PD")][:], pN[:, 256:384], T[K("Di")][:], A.mult, [K("FI"), K("Di")], [K("PD")], 128, [N_])
+        op("V", cyc(128), lambda: [V.tensor_tensor_scan(T[K("pr")][:], T.keep[:], T[K("PD")][:], 0.0, A.mult, A.add)],
+           [K("PD"), "keep"], prk)
+        ts(cf[:, 0:4], T[K("pr")][:, 31:128:32], -613.0, None, A.add, None, prk, [K("dp")], 4)
+        ts(cf[:, 4:8], cf[:, 0:4], 13.0, 2040.0, A.mult, A.add, [K("dp")], [K("nd")], 4)
+        tt(ci[:, 92:96], pN[:, 400:404], cf[:, 4:8], A.add, [K("CE"), K("nd")], [K("nd2")], 4, [N_])
+        ts(ci[:, 96:100], ci[:, 92:96], 4095, None, A.bitwise_and, None, [K("nd2")], [K("nd3")], 4)
+        tt(cf[:, 8:12], ci[:, 96:100], cf[:, 0:4], A.subtract, [K("nd3"), K("dp")], [K("dd")], 4)
+
+    def zpart(t, q):
+        K = lambda s: "%s%d" % (s, q)
+        pZ, Z_ = T[K("pZ")], K("pZ")
+        yb = T["y%d" % t]
+        yk = ["y%d_%d%d" % (t, q, h) for h in range(XP)]
+        mms([(pZ[:], T.ones[0:1, :], T.rowm[0:1, :], True, False, 512)], ["ones", "rowm"], [K("Z"), K("C"), K("C1"), K("C2"), K("C3")], [Z_])
+        for n in ORDER:
+            win = T.Xw[:, 0:WIN[n]]
+            wk = ["X%d" % k for k in range(WIN[n] // 4096)]
+            d, r = T["d%d%d" % (n, q)], T["r%d%d" % (n, q)]
+            pn = VPN if n in VT else SPN
+            w = 2048 // pn
+            for h in range(pn):
+                cs = slice(w * h, w * h + w)
+                ys = slice(2048 * q + w * h, 2048 * q + w * h + w)
+                src = win.indirect(T[K("lz")][:, 128 * n + (w // 16) * h:128 * n + (w // 16) * (h + 1)])
+                if n in VT:
+                    op("V", 60.0 + w * GC * CY, lambda cs=cs, ys=ys, src=src, d=d: [V.tensor_tensor(d[:, cs], src, yb[:, ys], A.subtract)],
+                       wk + yk + [K("lz%d" % n)], [K("d%d_%d" % (n, h))])
+                    ts(r[:, cs], d[:, cs], 0.0, None, A.max, None, [K("d%d_%d" % (n, h))], [K("r%d_%d" % (n, h))], w, half=True)
+                else:
+                    op("S", 80.0 + w * GC * CY, lambda cs=cs, src=src, d=d: [S.activation(d[:, cs], src, F.Copy)],
+                       wk + [K("lz%d" % n)], [K("d%d_%d" % (n, h))])
+                    for s in range(4 * h // SPN, 4 * (h + 1) // SPN):
+                        c5 = slice(512 * s, 512 * s + 512)
+                        y5 = slice(2048 * q + 512 * s, 2048 * q + 512 * s + 512)
+                        mms([(T[K("pS")][:], T.Ib[:], d[:, c5], True, False, 512), (T[K("pS")][:], T.nIb[:], yb[:, y5], False, True, 512)],
+                            ["Ib", "nIb", K("d%d_%d" % (n, h))] + yk, [K("subpS%d" % q)], [K("pS")])
+                        act(r[:, c5], T[K("pS")][:], F.Abs, [K("subpS%d" % q)], [K("r%d_%d" % (n, s))], 512, [K("pS")])
+            lst = []
+            last = n == ORDER[3]
+            for i in range(16):
+                o = pZ[:, 128 * n + i:128 * n + 128:16]
+                if n in VT:
+                    lst.append((o, r[:, i:2048:16], T.sel2[:], False, False, 64))
+                    lst.append((o, d[:, i:2048:16], T.seln[:], False, last and i == 15, 64))
+                else:
+                    lst.append((o, r[:, i:2048:16], T.sel[:], False, last and i == 15, 64))
+            mms(lst, ["sel", "sel2", "seln", K("Z")] + [K("r%d_%d" % (n, s)) for s in range(VPN if n in VT else 4)]
+                + [K("d%d_%d" % (n, s)) for s in range(pn)], [K("Zt%d" % n)], [Z_])
+
+    def fin(t, q):
+        K = lambda s: "%s%d" % (s, q)
+        pZ, Z_, pN, N_ = T[K("pZ")], K("pZ"), T[K("pN")], K("pN")
+        ci, cf = T[K("ci")], T[K("cf")]
+        for n in range(4):
+            ns = slice(128 * n, 128 * n + 128)
+            tt(T[K("mz")][:, ns], pZ[:, ns], T[K("ru")][:], A.mult, [K("Z"), K("Zt0"), K("Zt1"), K("Zt2"), K("Zt3"), K("ru")],
+               [K("mz%d" % n)], 128, [Z_])
+        mms([(pN[:, 416 + 4 * n:420 + 4 * n], T[K("mz")][:, 128 * n:128 * n + 128], T.B16[:], True, True, 64) for n in range(4)],
+            ["B16", K("NN")] + [K("mz%d" % n) for n in range(4)], [K("EC")], [N_])
+        tt(cf[:, 16:32], pN[:, 416:432], ci[:, 64:80], A.add, [K("EC"), K("tb")], [K("key")], 16, [N_])
+        tt(cf[:, 32:40], cf[:, 16:24], cf[:, 24:32], A.min, [K("key")], [K("k1")], 8)
+        tt(ci[:, 100:104], cf[:, 32:36], cf[:, 36:40], A.min, [K("k1")], [K("k2")], 4)
+        tt(cf[:, 40:44], pN[:, 432:436], ci[:, 100:104], A.is_gt, [K("k2"), K("OC")], [K("bt")], 4, [N_])
+        ts(ci[:, 104:108], ci[:, 100:104], 12, None, A.bitwise_and, None, [K("k2")], [K("m4")], 4)
+        tt(ci[:, 108:112], ci[:, 104:108], cf[:, 40:44], A.mult, [K("m4"), K("bt")], [K("me")], 4)
+        tt(ci[:, 112:116], ci[:, 108:112], ci[:, 32:36], A.add, [K("me"), K("t3")], [K("hr")], 4)
+        ts(ci[:, 116:120], ci[:, 112:116], 15, None, A.bitwise_and, None, [K("hr")], [K("hn")], 4)
+        tt(cf[:, 52:56], ci[:, 116:120], ci[:, 88:92], A.subtract, [K("hn"), K("hp")], [K("df")], 4)
+        fnk = [K("fn%d" % b) for b in range(4)]
+        for b in range(4):
+            ps = pN[:, 128 + 32 * b:160 + 32 * b]
+            ts(ps, ps, cf[:, 40 + b:41 + b], cf[:, 52 + b:53 + b], A.max, A.mult, [K("FN"), K("bt"), K("df")], [fnk[b]], 32, [N_])
+        tt(pN[:, 128:256], pN[:, 128:256], T[K("rn")][:], A.mult, fnk + [K("rn")], [K("FN")] + fnk, 128, [N_])
+        tt(T[K("Hh")][:], pN[:, 128:256], T[K("Hh")][:], A.add, [K("FN"), K("Hh")], [K("Hh")], 128, [N_])
+        ts(cf[:, 44:48], cf[:, 40:44], -1.0, 1.0, A.mult, A.add, [K("bt")], [K("nb")], 4)
+        tt(cf[:, 56:60], cf[:, 8:12], cf[:, 44:48], A.mult, [K("dd"), K("nb")], [K("md")], 4)
+        fik = [K("fi%d" % b) for b in range(4)]
+        for b in range(4):
+            ps = pN[:, 256 + 32 * b:288 + 32 * b]
+            ts(ps, ps, cf[:, 56 + b:57 + b], None, A.mult, None, [K("FI"), K("md")], [fik[b]], 32, [N_])
+        tt(T[K("Di")][:], pN[:, 256:384], T[K("Di")][:], A.add, fik + [K("Di")], [K("Di"), K("FI")], 128, [N_])
+        tt(cf[:, 64:68], cf[:, 12:16], cf[:, 44:48], A.mult, [K("sm"), K("nb")], [K("as")], 4)
+        tt(ci[:, 120:124], ci[:, 120:124], cf[:, 64:68], A.add, [K("A"), K("as")], [K("A")], 4)
+
+    for q in range(2):
+        xpart(0, q)
+    konst()
+    chunk[0] = 0
+    for k in range(VCOPIES + 1, COPIES):
+        op("Y", 60.0, lambda k=k: g.sync.dma_start(T.Xw[:, 4096 * k:4096 * k + 4096], T.Xw[:, 0:4096]),
+           ["X0"] + ["x0_0%d" % h for h in range(XP)], ["X%d" % k], (), 2000.0 + 4000.0 * (k - VCOPIES), "lx%d" % k, 16)
+    for k in range(1, VCOPIES + 1):
+        cp(T.Xw[:, 4096 * k:4096 * k + 4096], T.Xw[:, 0:4096], ["X0"], ["X%d" % k], 4096, half=True)
+    for t in range(RO):
+        for q in range(2):
+            chunk[0] = q
+            if t:
+                xpart(t, q)
+            gpart(t, q)
+            epart(t, q)
+            zpart(t, q)
+            fin(t, q)
+            if t < RO - 1:
+                if q == 1:
+                    op("loc%d" % t, 0.0, None, (), ["loc%d" % t], (), 1000.0, "loc%d" % t, 16 * 2 * XP)
+    for q in range(2):
+        K = lambda s: "%s%d" % (s, q)
+        for nm, src, add, y, n in (("PD", T["Di%d" % q][:], -613.0, T.yD, 128), ("Gs", T["Hh%d" % q][:], -0.5, T.yH, 128),
+                                   ("ya", T["ci%d" % q][:, 120:124], 0.0, T.yA, 4)):
+            k = {"PD": "Di", "Gs": "Hh", "ya": "A"}[nm]
+            ts(T[K(nm)][:], src, add, None, A.add, None, [K(k)], [K(nm)], n)
+            op("Y", 60.0, lambda nm=nm, y=y, n=n, q=q: g.sync.dma_start(y[:, n * q:n * q + n], T[K2(nm, q)][:]), [K(nm)], [], (), 2000.0, "out", 16)
+
+    seq = schedule(ops)
+    SEM = {"V": "sv", "S": "ss", "P": "sp", "G": "sg"}
+    ENG = {"V": g.vector, "S": g.scalar, "P": g.tensor, "G": g, "Y": g.sync}
+    count = {"sv": 0, "ss": 0, "sp": 0, "sg": 0, "out": 0}
+    val = {}
+    clock = {q: {} for q in ENG}
+    tail = {q: {} for q in ENG}
+    fin_clock = {}
+    for i in seq:
+        o = ops[i]
+        q = o["q"]
+        if q not in ENG:
+            val[i] = (o["sem"], o["inc"])
+            fin_clock[i] = {o["sem"]: o["inc"]}
+            continue
+        cur = clock[q]
+        need = {}
+        for j in o["hard"]:
+            if j in val:
+                s, v = val[j]
+                if cur.get(s, 0) < v and need.get(s, (0, 0))[0] < v:
+                    need[s] = (v, j)
+        for s in sorted(need, key=lambda s: -need[s][1]):
+            v, j = need[s]
+            if cur.get(s, 0) < v:
+                ENG[q].wait_ge(T.sem[s], v)
+                for a, b in fin_clock[j].items():
+                    if cur.get(a, 0) < b:
+                        cur[a] = b
+        r = o["fn"]()
+        if o["sem"]:
+            r.then_inc(T.sem[o["sem"]], 16)
+            count[o["sem"]] = count.get(o["sem"], 0) + 16
+            val[i] = (o["sem"], count[o["sem"]])
+            fin_clock[i] = dict(cur)
+            fin_clock[i][o["sem"]] = count[o["sem"]]
+        elif o["inc"]:
+            s = SEM[q]
+            for x in r:
+                x.then_inc(T.sem[s], 1)
+            count[s] += len(r)
+            val[i] = (s, count[s])
+            d = tail[q]
+            for a, b in cur.items():
+                if d.get(a, 0) < b:
+                    d[a] = b
+            d[s] = count[s]
+            fin_clock[i] = dict(d)
+    g.sync.wait_ge(T.sem.out, count["out"])
+    for s in ("sv", "ss", "sp", "sg"):
+        g.wait_ge(T.sem[s], count[s])
+    for t in range(RO):
+        g.wait_ge(T.sem["loc%d" % t], 16 * 2 * XP)
+
+
+def K2(s, q):
+    return "%s%d" % (s, q)

@@ -5,63 +5,74 @@ A = AluOpType
 F = ActivationFunctionType
 RO = 5
 DIST = (1, 3, 6)
-COPIES = 7
-VCOPIES = 6
-MAGIC = 50331648.0
-WIN = [16384, 20480, 24576, 28672]
-VT = (0, 1)
-ORDER = (0, 2, 1, 3)
+XW = 16384
+WIN = [(6144 - 2048 * n, 10240 + 2048 * n) for n in range(4)]
+FR = 613.0 + 1.0 / 32
+M4 = 1.5 * 2 ** 25
+M32 = 1.5 * 2 ** 28
+M1K = 1.5 * 2 ** 33
+M4K = 1.5 * 2 ** 35
+GV = 1
+GS = 1
 XP = 4
-XV = (3,)
-VPN = 4
-SPN = 4
-PEADD = True
+XT = ("SSSV", "SSSV")
+XT0 = ("SVSV", "SVSV")
+ZT = (("RRRR", "SSSS", "RRRR", "ASSS"), ("RRRR", "SSSS", "RRRR", "ASSS"))
+ORDER = (0, 1, 2, 3)
+COPY = "VVVVVV"
+FI_ON = "V"
+HCOPY = True
 
-SCRATCH = {"Xw": ("sbuf", [128, 4096 * COPIES], "bfloat16"),
+SCRATCH = {"Xw": ("sbuf", [128, XW], "bfloat16"),
            "Dl": ("sbuf", [128, 256], "int32"), "Hl": ("sbuf", [128, 256], "int32"),
-           "tl": ("sbuf", [128, 8], "int32"), "Al": ("sbuf", [128, 8], "int32"), "thm": ("sbuf", [128, 8], "float32")}
+           "tl": ("sbuf", [128, 8], "int32"), "Al": ("sbuf", [128, 8], "int32"), "Am": ("sbuf", [128, 8], "int32"),
+           "Ab": ("sbuf", [128, 8], "float32"), "thm": ("sbuf", [128, 8], "float16")}
 for _t in range(3):
     SCRATCH["x%d" % _t] = ("sbuf", [128, 4096], "bfloat16")
 for _t in range(RO):
     SCRATCH["y%d" % _t] = ("sbuf", [128, 4096], "bfloat16")
-for _n in ("ones", "Ib", "Bt", "Bb", "Ss", "nIb", "I16", "keep"):
+for _n in ("ones", "Bt", "Bb", "Ss", "V1", "Tri", "nSl", "Bi", "Bp", "Ce", "Cg"):
     SCRATCH[_n] = ("sbuf", [128, 128], "bfloat16")
-for _n in ("Ih", "Bh", "V1", "Tri"):
+IS = {1: 0, -1: 1, 2: 2, 1024: 3, 4: 4, -4: 5, 128: 6, 112: 7}
+SCRATCH["Is"] = ("sbuf", [128, 128 * len(IS)], "bfloat16")
+SCRATCH["nTri"] = ("sbuf", [128, 128], "bfloat16")
+for _n in ("nIh", "Bh", "Bih", "Be", "Bg", "oneh", "rowp"):
     SCRATCH[_n] = ("sbuf", [128, 128], "float16")
 SCRATCH["I4"] = ("sbuf", [128, 384], "float16")
-SCRATCH["B4"] = ("sbuf", [128, 16], "float16")
-SCRATCH["B16"] = ("sbuf", [128, 4], "float16")
-for _n in ("selt", "sel", "sel2", "seln"):
+SCRATCH["B256"] = ("sbuf", [128, 4], "float16")
+SCRATCH["Bd"] = ("sbuf", [128, 8], "float32")
+SCRATCH["sel"] = ("sbuf", [128, 16], "bfloat16")
+for _n in ("selt", "sel2", "seln"):
     SCRATCH[_n] = ("sbuf", [128, 8], "bfloat16")
-SCRATCH["cst"] = ("sbuf", [128, 16], "int32")
-SCRATCH["rowm"] = ("sbuf", [128, 512], "bfloat16")
-SCRATCH["rowg"] = ("sbuf", [128, 128], "bfloat16")
-SCRATCH["rowj"] = ("sbuf", [128, 8], "bfloat16")
+SCRATCH["rowm"] = ("sbuf", [128, 128], "bfloat16")
+SCRATCH["rowk"] = ("sbuf", [128, 40], "bfloat16")
+SCRATCH["rs"] = ("sbuf", [128, 20], "float32")
 SCRATCH["If"] = ("sbuf", [128, 128], "float32")
 for _q in range(2):
     for _n in range(4):
         SCRATCH["d%d%d" % (_n, _q)] = ("sbuf", [128, 2048], "bfloat16")
         SCRATCH["r%d%d" % (_n, _q)] = ("sbuf", [128, 2048], "bfloat16")
-    for _n, _w, _d in (("Di", 128, "int32"), ("Hh", 128, "bfloat16"), ("fl", 128, "bfloat16"),
-                       ("sg", 128, "bfloat16"), ("Gs", 128, "float32"), ("ths", 128, "float32"), ("ov", 128, "float16"),
-                       ("fi", 128, "float16"), ("PG", 128, "float16"), ("Pe", 128, "float16"), ("ru", 128, "float16"),
-                       ("mo", 128, "float16"), ("mz", 512, "float16"), ("pr", 128, "float32"), ("ls", 384, "float32"),
-                       ("lz", 512, "uint16"), ("lx", 128, "uint16"), ("PD", 128, "float32"), ("ai", 128, "int32"),
-                       ("ah", 128, "float16"), ("rn", 128, "bfloat16"), ("ax", 128, "bfloat16"), ("tx", 128, "float16"),
-                       ("xi", 128, "int32"), ("cf", 72, "float32"), ("ci", 128, "int32"), ("ya", 4, "float32")):
+        if "R" in ZT[_q][_n] and ZT[_q][_n] != "RRRR":
+            SCRATCH["z%d%d" % (_n, _q)] = ("sbuf", [128, 2048], "bfloat16")
+    for _n, _w, _d in (("ab", 2048, "bfloat16"), ("Dp", 128, "float32"), ("Hh", 144, "bfloat16"), ("fl", 128, "bfloat16"),
+                       ("TR", 256, "float16"), ("ov", 128, "bfloat16"), ("fi", 128, "bfloat16"), ("PG", 128, "float16"),
+                       ("Pe", 128, "float16"), ("Pd", 128, "float32"), ("ru", 128, "bfloat16"), ("mo", 128, "float16"),
+                       ("mz", 512, "float16"), ("pr", 128, "float32"), ("lz", 512, "uint16"), ("lx", 128, "uint16"),
+                       ("ah", 128, "float16"), ("rp", 128, "float16"), ("xi", 128, "int32"), ("cf", 112, "float32"), ("cb", 80, "bfloat16"),
+                       ("ch", 8, "float16"), ("oD", 128, "float32"), ("oH", 128, "float32"), ("oA", 4, "float32")):
         SCRATCH["%s%d" % (_n, _q)] = ("sbuf", [128, _w], _d)
     for _n in ("pA", "pZ", "pN", "pS"):
         SCRATCH["%s%d" % (_n, _q)] = ("psum", [128, 512], "float32")
 
-SEMAPHORES = ["sv", "ss", "sp", "sg", "out", "ldD", "ldH", "ldt", "ldA"]
-SEMAPHORES += ["lx%d" % k for k in [0] + list(range(VCOPIES + 1, COPIES))] + ["loc%d" % t for t in range(RO)]
+SEMAPHORES = ["sv", "ss", "sp", "sg", "out", "ldD", "ldH", "ldt", "ldA", "lxa", "lxb"]
+SEMAPHORES += ["lc%d" % k for k in range(6)] + ["loc%d" % t for t in range(RO)]
 SEMAPHORES += ["ar%d%d%d" % (t, q, h) for t in range(RO) for q in range(2) for h in range(XP)]
 
 CY = 0.83 * 1.2
 GC = 1.56
 HOP = 120.0
-SEED = 1
-NOISE = 0.0
+OWN = 60.0
+ARR = 2600.0
 BIAS = 7000.0
 SLACK = 200.0
 
@@ -75,10 +86,8 @@ def schedule(ops):
     prio = [0.0] * n
     for i in range(n - 1, -1, -1):
         prio[i] = ops[i]["cost"] + ops[i]["lat"] + max([prio[j] + HOP for j in succ[i]], default=0.0)
-    rnd = SEED
     for i in range(n):
-        rnd = (rnd * 1103515245 + 12345) % 2147483648
-        prio[i] += (BIAS if ops[i]["ch"] == 0 else 0.0) + NOISE * (rnd / 2147483648.0 - 0.5)
+        prio[i] += BIAS if ops[i]["ch"] == 0 else 0.0
     left = [len(o["hard"] | o["order"]) for o in ops]
     ready = [0.0] * n
     avail = {}
@@ -102,11 +111,10 @@ def schedule(ops):
         o = ops[c]
         pend[o["q"]].remove(c)
         avail[o["q"]] = st + o["cost"]
-        o["st"] = st
         end = st + o["cost"] + o["lat"]
         done.append(c)
         for j in succ[c]:
-            hop = 0.0 if c not in ops[j]["hard"] else (60.0 if ops[j]["q"] == o["q"] else HOP)
+            hop = 0.0 if c not in ops[j]["hard"] else (OWN if ops[j]["q"] == o["q"] else HOP)
             ready[j] = max(ready[j], (end if c in ops[j]["hard"] else st) + hop)
             left[j] -= 1
             if left[j] == 0:
@@ -175,88 +183,130 @@ def rank_program(g, core, T, topo):
             return [S.activation(out, a, fn, 0.0, scale)]
         op("S", cyc(n), f, R, W, banks)
 
-    def mms(lst, R, W, banks):
+    def mms(lst, R, W, banks, start=True, stop=True):
         def f():
-            return [P.matmul(o, l, r, a, b) for (o, l, r, a, b, c) in lst]
-        op("P", sum(x[5] for x in lst) * 0.417 * 1.2 + 5.0 * len(lst), f, R, W, banks)
+            return [P.matmul(o, l, r, start and i == 0, stop and i == len(lst) - 1) for i, (o, l, r, c) in enumerate(lst)]
+        op("P", sum(x[3] for x in lst) * 0.417 * 1.2 + 5.0 * len(lst), f, R, W, banks)
 
-    def load(out, in_, sem, W, lat):
-        op("Y", 60.0, lambda: g.sync.dma_start(out, in_), (), W, (), lat, sem, 16)
+    def load(out, in_, sem, W, lat, R=()):
+        op("Y", 60.0, lambda: g.sync.dma_start(out, in_), R, W, (), lat, sem, 16)
 
-    load(T.Dl[:], T.D[:], "ldD", ["Dl"], 2000.0)
-    load(T.Hl[:], T.H[:], "ldH", ["Hl"], 2000.0)
-    load(T.tl[:], T.th[:], "ldt", ["tl"], 2200.0)
-    load(T.Al[:], T.A[:], "ldA", ["Al"], 2200.0)
-    load(T.Xw[:, 0:4096], T.X[:], "lx0", ["X0"], 6500.0)
-
-    def fill(ap, val, W, n):
+    def fill(ap, val, W, n=64):
         op("V", cyc(n), lambda: [V.memset(ap, val)], (), W)
-
-    fill(T.ones[:], 1.0, ["ones"], 64)
-    fill(T.rowm[0:1, :], -2040.0, ["rowm"], 256)
-    fill(T.rowg[0:1, :], 16.5, ["rowg"], 64)
-    fill(T.rowj[0:1, 0:4], -1.5, ["rowj0"], 64)
-    fill(T.rowj[0:1, 4:8], 0.5, ["rowj1"], 64)
 
     def sel(out, in_, pat, cmp, base, cm, R, W, n):
         op("G", 200.0 + 2 * n * CY, lambda: [g.affine_select(out, in_, pat, cmp, 0.0, base, cm)], R, W)
 
-    sel(T.Ib[:], T.ones[:], [[-1, 128]], A.is_equal, 0, 1, ["ones"], ["Ib"], 128)
-    sel(T.keep[:], T.ones[:], [[0, 4], [1, 32]], A.is_gt, 0, 0, ["ones"], ["keep"], 128)
+    def I(k):
+        return T.Is[:, 128 * IS[k]:128 * IS[k] + 128]
+
+    load(T.Dl[:], T.D[:], "ldD", ["Dl"], 7000.0)
+    load(T.Hl[:], T.H[:], "ldH", ["Hl"], 7000.0)
+    load(T.Xw[:, 6451:10240], T.X[:, 0:3789], "lxa", ["Xa"], 6500.0)
+    load(T.Xw[:, 6144:6451], T.X[:, 3789:4096], "lxb", ["Xb"], 6500.0)
+    load(T.tl[:], T.th[:], "ldt", ["tl"], 6500.0)
+    load(T.Al[:], T.A[:], "ldA", ["Al"], 6500.0)
+    X0 = ["Xa", "Xb"]
+
+    fill(T.ones[:], 1.0, ["ones"])
+    sel(I(1), T.ones[:], [[-1, 128]], A.is_equal, 0, 1, ["ones"], ["I1"], 128)
     sel(T.selt[:], T.ones[:, 0:8], [[-16, 8]], A.is_ge, 0, 1, ["ones"], ["selt"], 8)
-    sel(T.sel[:], T.selt[:], [[16, 8]], A.is_ge, 15, -1, ["selt"], ["sel"], 8)
+    sel(T.sel[:, 0:8], T.selt[:], [[16, 8]], A.is_ge, 15, -1, ["selt"], ["sel"], 8)
     sel(T.Bt[:], T.ones[:], [[-32, 4], [0, 32]], A.is_ge, 0, 1, ["ones"], ["Bt"], 128)
     sel(T.Bb[:], T.Bt[:], [[32, 4], [0, 32]], A.is_ge, 31, -1, ["Bt"], ["Bb"], 128)
     sel(T.Ss[:], T.Bb[:], [[1, 128]], A.is_ge, -1, -1, ["Bb"], ["Ss"], 128)
-    op("G", 200.0, lambda: [g.iota(T.cst[:], [[4, 4], [0, 4]], 19, 0)], (), ["cst"])
+    sel(T.Bt[:], T.ones[:], [[1, 128]], A.is_ge, 0, -32, ["ones"], ["Bt"], 128)
+    sel(T.Bi[:], T.Bt[:], [[-1, 128]], A.is_ge, 31, 32, ["Bt"], ["Bi"], 128)
+    for c0, rep, w in ((0, 3, 5), (60, 2, 1), (68, 3, 5)):
+        cs = slice(c0, c0 + 4 * rep * w)
+        sel(T.Bt[:, cs], T.ones[:, cs], [[0, rep], [-32, 4], [0, w]], A.is_ge, 0, 1, ["ones"], ["Bt"], 64)
+        sel(T.Bp[:, cs], T.Bt[:, cs], [[0, rep], [32, 4], [0, w]], A.is_ge, 31, -1, ["Bt"], ["Bp%d" % c0], 64)
 
     for q in range(2):
         c0 = slice(128 * q, 128 * q + 128)
-        ts(T["Di%d" % q][:], T.Dl[:, c0], 613.0, None, A.add, None, ["Dl"], ["Di%d" % q], 128)
-        ts(T["Hh%d" % q][:], T.Hl[:, c0], 0.5, None, A.add, None, ["Hl"], ["Hh%d" % q], 128)
+        ts(T["Dp%d" % q][:], T.Dl[:, c0], FR, None, A.add, None, ["Dl"], ["Dp%d" % q], 128)
+        ts(T["Hh%d" % q][:, 16:144], T.Hl[:, c0], 0.5, None, A.add, None, ["Hl"], ["Hh%d" % q], 128)
 
     def konst():
-        ts(T.nIb[:], T.Ib[:], -1.0, None, A.mult, None, ["Ib"], ["nIb"], 128, half=True)
-        ts(T.I16[:], T.Ib[:], 16.0, None, A.mult, None, ["Ib"], ["I16"], 128, half=True)
-        cp(T.Ih[:], T.Ib[:], ["Ib"], ["Ih"], 128, half=True)
-        cp(T.If[:], T.Ib[:], ["Ib"], ["If"], 128)
+        for k in IS:
+            if k != 1:
+                ts(I(k), I(1), float(k), None, A.mult, None, ["I1"], ["I%d" % k], 128, half=True)
+        ts(T.nIh[:], I(1), -1.0, None, A.mult, None, ["I1"], ["nIh"], 128, half=True)
+        cp(T.If[:], I(1), ["I1"], ["If"], 128)
         for n in (1, 2, 3):
-            ts(T.I4[:, 128 * n - 128:128 * n], T.Ib[:], 4.0 * n, None, A.mult, None, ["Ib"], ["I4%d" % n], 128, half=True)
-        ts(T.sel2[:], T.sel[:], 2.0, None, A.mult, None, ["sel"], ["sel2"], 8)
-        ts(T.seln[:], T.sel[:], -1.0, None, A.mult, None, ["sel"], ["seln"], 8)
-        tt(T.V1[:], T.Ib[:], T.Ss[:], A.subtract, ["Ib", "Ss"], ["V1"], 128)
-        tt(T.Tri[:], T.Ib[:], T.Ss[:], A.add, ["Ib", "Ss"], ["Tri"], 128)
+            ts(T.I4[:, 128 * n - 128:128 * n], I(1), 4.0 * n, None, A.mult, None, ["I1"], ["J%d" % n], 128, half=True)
+        cp(T.sel[:, 8:16], T.sel[:, 0:8], ["sel"], ["selb"], 8)
+        ts(T.sel2[:], T.sel[:, 0:8], 2.0, None, A.mult, None, ["sel"], ["sel2"], 8)
+        ts(T.seln[:], T.sel[:, 0:8], -1.0, None, A.mult, None, ["sel"], ["seln"], 8)
+        tt(T.V1[:], I(1), T.Ss[:], A.subtract, ["I1", "Ss"], ["V1"], 128)
+        tt(T.Tri[:], I(1), T.Ss[:], A.add, ["I1", "Ss"], ["Tri"], 128)
+        tt(T.nSl[:], T.Tri[:], T.Bb[:], A.subtract, ["Tri", "Bb"], ["nSl"], 128)
+        ts(T.nTri[:], T.Tri[:], -16.0, None, A.mult, None, ["Tri"], ["nTri"], 128, half=True)
+        ts(T.Tri[:], T.Tri[:], 16.0, None, A.mult, None, ["Tri"], ["Tri"], 128, half=True)
         cp(T.Bh[:], T.Bb[:], ["Bb"], ["Bh"], 128, half=True)
-        for n in range(4):
-            cp(T.B4[:, 4 * n:4 * n + 4], T.Bb[:, 0:128:32], ["Bb"], ["B4%d" % n], 4)
-        ts(T.B16[:], T.Bb[:, 0:128:32], 16.0, None, A.mult, None, ["Bb"], ["B16"], 4)
+        cp(T.Bih[:], T.Bi[:], ["Bi"], ["Bih"], 128, half=True)
+        ts(T.B256[:], T.Bb[:, 0:128:32], 256.0, None, A.mult, None, ["Bb"], ["B256"], 4)
+        ts(T.Bd[:, 0:4], T.Bb[:, 0:128:32], 13.0 / 1024, None, A.mult, None, ["Bb"], ["Bd0"], 4)
+        ts(T.Bd[:, 4:8], T.Bb[:, 0:128:32], 12.0 / 1024, None, A.mult, None, ["Bb"], ["Bd1"], 4)
+        fill(T.Ce[:], 1.0, ["Ce"])
+        fill(T.Ce[:, 60:68], 1.0 / 1024, ["Ce"])
+        fill(T.Cg[:], 0.0, ["Cg"])
+        fill(T.rowp[0:2, :], 0.0, ["rowp"])
+        for c in (0, 68):
+            fill(T.Ce[:, c + 24:c + 40:5], 0.0, ["Ce"])
+            fill(T.Ce[:, c + 40:c + 60], 0.0, ["Ce"])
+            fill(T.Cg[:, c:c + 20], 1.0, ["Cg"])
+            fill(T.Cg[:, c + 40:c + 60], 0.25, ["Cg"])
+            fill(T.Cg[:, c + 4:c + 60:5], 0.0, ["Cg"])
+            fill(T.Cg[:, c + 24:c + 40:5], -0.25, ["Cg"])
+        Bp = ["Bp0", "Bp60", "Bp68"]
+        tt(T.Be[:], T.Bp[:], T.Ce[:], A.mult, Bp + ["Ce"], ["Be"], 128)
+        tt(T.Bg[:], T.Bp[:], T.Cg[:], A.mult, Bp + ["Cg"], ["Bg"], 128)
+        fill(T.rowp[0:2, 64:68], 3.625 / 1024, ["rowp"])
+        for cs, v in ((slice(0, 20), -1.0), (slice(20, 40), -1.5), (slice(40, 60), -1.9375), (slice(4, 20, 5), -1.5),
+                      (slice(24, 40, 5), 1.9375), (slice(44, 60, 5), 0.0), (slice(60, 64), 215.0 / 1024),
+                      (slice(64, 68), 2872.0 / 1024), (slice(68, 88), 1.0), (slice(72, 88, 5), 0.0)):
+            fill(T.rowp[0:1, cs], v, ["rowp"])
+        fill(T.oneh[0:2, :], 1.0, ["oneh"])
+        fill(T.rowm[0:1, :], -2040.0, ["rowm"])
+        for n in range(5):
+            fill(T.rowk[0:1, n:20:5], 0.5 - 4 * (n + 1) if n < 4 else 0.0, ["rowk"])
+            fill(T.rowk[0:1, 20 + n:40:5], 32.0 + 36 * n if n < 4 else 1.0, ["rowk"])
+        fill(T.rs[:], 0.0, ["rs"])
+        fill(T.rs[:, 0:20:5], 1e9, ["rs"])
         ts(T.thm[:], T.tl[:], -2040.0, None, A.add, None, ["tl"], ["thm"], 8)
+        ts(T.Am[:], T.Al[:], 31, None, A.bitwise_and, None, ["Al"], ["Am"], 8)
+        tt(T.Ab[:], T.Al[:], T.Am[:], A.subtract, ["Al", "Am"], ["Ab"], 8)
         for q in range(2):
-            cp(T["ci%d" % q][:, 120:124], T.Al[:, 4 * q:4 * q + 4], ["Al"], ["A%d" % q], 4)
-            fill(T["fl%d" % q][:, 0:1], 0.0, ["fl0%d" % q], 64)
-            for b in range(4):
-                ts(T["tx%d" % q][:, 32 * b:32 * b + 32], T.ones[:, 0:32], T.thm[:, 4 * q + b:4 * q + b + 1], None, A.mult, None,
-                   ["ones", "thm"], ["tx%d%d" % (b, q)], 32)
-
-    B4 = ["B40", "B41", "B42", "B43"]
+            cp(T["ch%d" % q][:, 0:4], T.Am[:, 4 * q:4 * q + 4], ["Am"], ["a%d" % q], 4)
+            fill(T["Hh%d" % q][:, 0:16], 0.0, ["H0%d" % q])
+            fill(T["TR%d" % q][0:4, 128:256], -2040.0, ["TRc%d" % q])
+            for n in range(4):
+                if "z%d%d" % (n, q) in SCRATCH:
+                    for h in range(4):
+                        if ZT[q][n][h] != "R":
+                            fill(T["d%d%d" % (n, q)][:, 512 * h:512 * h + 512], 0.0, ["d%d_%d%d" % (n, h, q)], 256)
 
     def xpart(t, q):
         K = lambda s: "%s%d" % (s, q)
         chunk[0] = q
         xb = "x%d" % (t % 3)
-        tt(T[K("PD")][:], T[K("Di")][:], T[K("Hh")][:], A.mult, [K("Di"), K("Hh")], [K("PD")], 128)
-        ts(T[K("xi")][:], T[K("PD")][:], -306.75, None, A.add, None, [K("PD")], [K("xi")], 128)
+        if t == 0 or not HCOPY:
+            tt(T[K("xi")][:], T[K("Dp")][:], T[K("Hh")][:, 16:144], A.mult, [K("Dp"), K("Hh")], [K("xi")], 128)
+        else:
+            pN = T[K("pN")]
+            tt(T[K("xi")][:], pN[:, 128:256], T[K("Dp")][:], A.mult, [K("Dp"), K("m")], [K("xi")], 128, [K("pN")])
+            act(T[K("Hh")][:, 16:144], pN[:, 128:256], F.Copy, [K("m")], [K("Hh")], 128, [K("pN")])
         ts(T[K("xi")][:], T[K("xi")][:], 4095, None, A.bitwise_and, None, [K("xi")], [K("xi")], 128)
         cp(T[K("lx")][:], T[K("xi")][:], [K("xi")], [K("lx")], 128)
         w = 2048 // XP
-        u = DIST[t % 3]
-        dst = T.cores[(rank - u) % n_ranks]
+        dst = T.cores[(rank - DIST[t % 3]) % n_ranks]
         rid, pid = topo.addr(dst)[:2]
         for h in range(XP):
             cs = slice(2048 * q + w * h, 2048 * q + w * h + w)
-            src = T.Xw[:, 0:4096].indirect(T[K("lx")][:, (w // 16) * h:(w // 16) * (h + 1)])
-            R, W = ["X0", K("lx")] + (["loc%d" % (t - 3)] if t >= 3 else []), ["%s_%d%d" % (xb, q, h)]
-            if h in XV or (t == 0 and q == 0 and h % 2 == 1):
+            src = T.Xw[:, 6144:10240].indirect(T[K("lx")][:, (w // 16) * h:(w // 16) * (h + 1)])
+            R, W = X0 + [K("lx")] + (["loc%d" % (t - 3)] if t >= 3 else []), ["%s_%d%d" % (xb, q, h)]
+            if (XT if t else XT0)[q][h] == "V":
                 op("V", 60.0 + w * GC * CY, lambda src=src, cs=cs: [V.tensor_copy(T[xb][:, cs], src)], R, W)
             else:
                 op("S", 80.0 + w * GC * CY, lambda src=src, cs=cs: [S.activation(T[xb][:, cs], src, F.Copy)], R, W)
@@ -264,198 +314,183 @@ def rank_program(g, core, T, topo):
             i = op("G", 900.0, lambda cs=cs, ar=ar: g.remote_dma(T["y%d" % t][:, cs], T[xb][:, cs], T.sem[ar], T.sem["loc%d" % t],
                                                                   pid, rid, topo.mask(core, dst)),
                    ["%s_%d%d" % (xb, q, h)], [], (), 0.0, None, 0)
-            a = op("arr%s" % ar, 0.0, None, (), ["y%d_%d%d" % (t, q, h)], (), 2200.0, ar, 16)
+            a = op("arr%s" % ar, 0.0, None, (), ["y%d_%d%d" % (t, q, h)], (), ARR, ar, len(topo.engines(core, dst)))
             ops[a]["order"].add(i)
 
     def gpart(t, q):
         K = lambda s: "%s%d" % (s, q)
         pA, pZ, A_, Z_ = T[K("pA")], T[K("pZ")], K("pA"), K("pZ")
-        mms([(pA[:, 129:256], T.Ib[:], T[K("Hh")][:, 1:128], True, False, 127),
-             (pA[:, 129:256], T.nIb[:], T[K("Hh")][:, 0:127], False, True, 127)], ["Ib", "nIb", K("Hh")], [K("v")], [A_])
-        ts(T[K("fl")][:, 1:128], pA[:, 129:256], 0.0, None, A.not_equal, None, [K("v")], [K("fl")], 127, [A_])
-        op("V", cyc(64), lambda: [V.tensor_tensor_scan(T[K("sg")][:], T.keep[:], T[K("fl")][:], 0.0, A.mult, A.add)],
-           [K("fl"), K("fl0"), "keep"], [K("sg")])
-        mms([(pA[:, 384:512], T.ones[0:1, :], T.rowg[0:1, :], True, False, 128),
-             (pA[:, 384:512], T[K("Hh")][:], T.Ib[:], False, False, 128),
-             (pA[:, 384:512], T[K("sg")][:], T.I16[:], False, True, 128)],
-            ["ones", "rowg", K("Hh"), K("sg"), "Ib", "I16"], [K("GT")], [A_])
-        act(T[K("Gs")][:], pA[:, 384:512], F.Copy, [K("GT")], [K("Gs")], 128, [A_])
-        ci, cf = T[K("ci")], T[K("cf")]
-        ts(ci[:, 124:128], ci[:, 120:124], 31, None, A.bitwise_and, None, [K("A")], [K("a31")], 4)
-        cp(cf[:, 60:64], ci[:, 124:128], [K("a31")], [K("a31f")], 4)
-        for b in range(4):
-            act(T[K("ax")][:, 32 * b:32 * b + 32], T.ones[:, 0:32], F.Identity, ["ones", K("a31f")], [K("ax%d" % b)], 64, (),
-                cf[:, 60 + b:61 + b])
-        mms([(pA[:, 256:384], T[K("tx")][:], T.Ih[:], True, False, 128),
-             (pA[:, 256:384], T[K("ax")][:], T.Ib[:], False, True, 128)],
-            ["Ih", "Ib"] + [K("tx%d" % b) for b in range(4)] + [K("ax%d" % b) for b in range(4)], [K("GP")], [A_])
-        act(T[K("ths")][:], pA[:, 256:384], F.Copy, [K("GP")], [K("ths")], 128, [A_])
-        ts(T[K("ai")][:], T[K("Di")][:], 1023, None, A.bitwise_and, None, [K("Di")], [K("ai")], 128)
-        cp(T[K("ah")][:], T[K("ai")][:], [K("ai")], [K("ah")], 128)
-        if not PEADD:
-            mms([(pZ[:, 128 * n:128 * n + 128], T.I4[:, 128 * n - 128:128 * n], T[K("ah")][:], True, True, 128) for n in (1, 2, 3)],
-                [K("ah"), "I41", "I42", "I43"], [K("C"), K("Z")], [Z_])
+        Hh, ch = T[K("Hh")], T[K("ch")]
+        ts(ch[:, 4:8], ch[:, 0:4], 31.5, -32.0, A.is_gt, A.mult, [K("a")], [K("w")], 4)
+        mms([(pZ[0:4, 128:256], T.thm[:, 4 * q:4 * q + 4], T.nIh[:], 128), (pZ[0:4, 128:256], ch[:, 0:4], T.nIh[:], 128),
+             (pZ[0:4, 128:256], ch[:, 4:8], T.nIh[:], 128)], ["thm", "nIh", K("a"), K("w")], [K("Z1")], [Z_])
+        mms([(pZ[:, 0:128], Hh[:, 16:144], I(1), 128), (pZ[:, 0:128], Hh[:, 15:143], I(-1), 128)],
+            ["I1", "I-1", K("Hh"), K("H0")], [K("Z0")], [Z_])
+        cp(T[K("TR")][0:4, 0:128], pZ[0:4, 128:256], [K("Z1")], [K("TR")], 128, [Z_])
+        ts(T[K("fl")][:], pZ[:, 0:128], 0.0, None, A.not_equal, None, [K("Z0")], [K("fl")], 128, [Z_])
+        ts(pZ[:, 256:384], T[K("Dp")][:], M1K, -M1K, A.add, A.add, [K("Dp")], [K("Z2")], 128, [Z_])
+        tt(T[K("ah")][:], T[K("Dp")][:], pZ[:, 256:384], A.subtract, [K("Dp"), K("Z2")], [K("ah")], 128, [Z_])
+        mms([(pA[:, 384:512], T[K("Dp")][:], T.If[:], 512)], [K("Dp"), "If"], [K("DT")], [A_])
+        mms([(pA[:, 256:384], Hh[:, 16:144], I(1), 128), (pA[:, 256:384], T.Tri[:], T[K("fl")][:], 128)],
+            [K("Hh"), K("fl"), "I1", "Tri"], [K("G1")], [A_])
 
     def epart(t, q):
         K = lambda s: "%s%d" % (s, q)
-        pA, pN, A_, N_ = T[K("pA")], T[K("pN")], K("pA"), K("pN")
-        xb = T["x%d" % (t % 3)]
-        yb = T["y%d" % t]
-        ab = T["r2%d" % q]
+        pA, pN, pZ, A_, N_, Z_ = T[K("pA")], T[K("pN")], T[K("pZ")], K("pA"), K("pN"), K("pZ")
+        xb, yb, ab = T["x%d" % (t % 3)], T["y%d" % t], T[K("ab")]
+        cf, cb, Hh = T[K("cf")], T[K("cb")], T[K("Hh")]
+        NK = [K("G2"), K("m"), K("FI"), K("pk")]
         for s in range(4):
             cs = slice(2048 * q + 512 * s, 2048 * q + 512 * s + 512)
             h = s * XP // 4
             bk = K("pS") if s % 2 == 0 else N_
-            ks = [K("NN")] if s % 2 else []
-            mms([(T[bk][:], T.Ib[:], xb[:, cs], True, False, 512), (T[bk][:], T.nIb[:], yb[:, cs], False, True, 512)],
-                ["Ib", "nIb", "x%d_%d%d" % (t % 3, q, h), "y%d_%d%d" % (t, q, h)], [K("sub" + bk)] + ks, [bk])
-            act(ab[:, 512 * s:512 * s + 512], T[bk][:], F.Abs, [K("sub" + bk)], [K("r2_%d" % s)], 512, [bk])
-        lst = [(pA[:, 0:128], T.ones[0:1, :], T.rowm[0:1, 0:128], True, False, 128)]
-        for i in range(16):
-            lst.append((pA[:, i:128:16], ab[:, i:2048:16], T.sel[:], False, i == 15, 64))
-        mms(lst, ["ones", "rowm", "sel"] + [K("r2_%d" % s) for s in range(4)], [K("eT")], [A_])
-        tt(T[K("ov")][:], pA[:, 0:128], T[K("ths")][:], A.is_gt, [K("eT"), K("ths")], [K("ov")], 128, [A_])
-        mms([(pA[:, 128:256], T.V1[:], T[K("ov")][:], True, True, 128)], ["V1", K("ov")], [K("v")], [A_])
-        ts(T[K("fi")][:], pA[:, 128:256], 0.0, None, A.max, None, [K("v")], [K("fi")], 128, [A_])
-        tt(T[K("Pe")][:], pA[:, 0:128], T[K("fi")][:], A.mult, [K("eT"), K("fi")], [K("Pe")], 128, [A_])
-        tt(T[K("PG")][:], pA[:, 384:512], T[K("fi")][:], A.mult, [K("GT"), K("fi")], [K("PG")], 128, [A_])
-        mms([(pN[:, 436:444], T.ones[0:1, :], T.rowj[0:1, :], True, False, 64),
-             (pN[:, 436:444], T[K("Pe")][:], T.B4[:, 0:8], False, False, 64),
-             (pN[:, 436:444], T[K("PG")][:], T.B4[:, 0:8], False, True, 64),
-             (pN[:, 400:416], T[K("Pe")][:], T.B4[:], True, True, 64),
-             (pN[:, 384:400], T[K("PG")][:], T.B4[:], True, True, 64)],
-            [K("Pe"), K("PG"), "ones", "rowj0", "rowj1"] + B4, [K("CE"), K("NN")], [N_])
-        ci, cf = T[K("ci")], T[K("cf")]
-        ts(cf[:, 68:72], pN[:, 436:440], MAGIC, -MAGIC, A.add, A.add, [K("CE")], [K("rr")], 4, [N_])
-        tt(cf[:, 48:52], pN[:, 440:444], cf[:, 68:72], A.subtract, [K("CE"), K("rr")], [K("jf")], 4, [N_])
-        pZ, Z_ = T[K("pZ")], K("pZ")
+            ks = NK if s % 2 else [K("sub")]
+            mms([(T[bk][:], I(1), xb[:, cs], 512), (T[bk][:], I(-1), yb[:, cs], 512)],
+                ["I1", "I-1", "x%d_%d%d" % (t % 3, q, h), "y%d_%d%d" % (t, q, h)], ks, [bk])
+            act(ab[:, 512 * s:512 * s + 512], T[bk][:], F.Abs, ks, [K("ab%d" % s)], 512, [bk])
+        mms([(pA[:, 0:256], T.Bih[0:4, :], T[K("TR")][0:4, :], 256)], ["Bih", K("TR"), K("TRc")], [K("e1"), K("e0")], [A_], True, False)
+        mms([(pA[:, i:256:16], ab[:, i:2048:16], T.sel[:], 64) for i in range(16)],
+            ["sel", "selb"] + [K("ab%d" % s) for s in range(4)], [K("e1"), K("e0")], [A_], False, True)
+        ts(T[K("ov")][:], pA[:, 0:128], 2040.0, None, A.is_gt, None, [K("e1")], [K("ov")], 128, [A_])
+        mms([(pA[:, 0:128], T.V1[:], T[K("ov")][:], 128)], ["V1", K("ov")], [K("e1")], [A_])
+        if FI_ON == "V":
+            ts(T[K("fi")][:], pA[:, 0:128], 0.0, None, A.max, None, [K("e1")], [K("fi")], 128, [A_])
+        else:
+            act(T[K("fi")][:], pA[:, 0:128], F.Relu, [K("e1")], [K("fi")], 128, [A_])
+        tt(T[K("Pe")][:], pA[:, 128:256], T[K("fi")][:], A.mult, [K("e0"), K("fi")], [K("Pe")], 128, [A_])
+        tt(T[K("PG")][:], pA[:, 256:384], T[K("fi")][:], A.mult, [K("G1"), K("fi")], [K("PG")], 128, [A_])
+        tt(T[K("Pd")][:], pA[:, 384:512], T[K("fi")][:], A.mult, [K("DT"), K("fi")], [K("Pd")], 128, [A_])
+        mms([(pN[:, 384:512], T.oneh[0:2, :], T.rowp[0:2, :], 128), (pN[:, 384:512], T[K("Pe")][:], T.Be[:], 128),
+             (pN[:, 384:512], T[K("PG")][:], T.Bg[:], 128)],
+            [K("Pe"), K("PG"), "oneh", "rowp", "Be", "Bg"], [K("pk")], [N_], True, False)
+        mms([(pN[:, 444:452], T[K("Pd")][:], T.Bd[:], 256)], [K("Pd"), "Bd0", "Bd1"], [K("pk")], [N_], False, True)
+        ts(cf[:, 0:64], pN[:, 384:448], M4, -M4, A.add, A.add, [K("pk")], [K("rnd")], 64, [N_])
+        tt(cb[:, 0:60], pN[:, 452:512], cf[:, 0:60], A.subtract, [K("pk"), K("rnd")], [K("rem")], 60, [N_])
         prk = [K("pr%d" % b) for b in range(4)]
         for b in range(4):
             bs = slice(32 * b, 32 * b + 32)
-            ts(T[K("pr")][:, bs], T[K("Di")][:, bs], cf[:, 48 + b:49 + b], -306.75, A.mult, A.add, [K("Di"), K("jf")], [prk[b]], 32)
+            ts(T[K("pr")][:, bs], T[K("Dp")][:, bs], cb[:, 5 * b:5 * b + 1], 2048.5, A.mult, A.add, [K("Dp"), K("rem")], [prk[b]], 32)
+        ts(T[K("rp")][:], T[K("pr")][:], M4K, -M4K - 8192.0, A.add, A.add, prk, [K("rp")], 128)
         for n in ORDER:
             ns = slice(128 * n, 128 * n + 128)
-            if n == 0:
-                cp(T[K("lz")][:, ns], T[K("pr")][:], prk, [K("lz0")], 128)
-            elif PEADD:
-                mms([(pZ[:, ns], T.I4[:, 128 * n - 128:128 * n], T[K("ah")][:], True, False, 128),
-                     (pZ[:, ns], T.If[:], T[K("pr")][:], False, True, 512)], [K("ah"), "If", "I41", "I42", "I43"] + prk, [K("C%d" % n), K("Z")], [Z_])
-                cp(T[K("lz")][:, ns], pZ[:, ns], [K("C%d" % n)], [K("lz%d" % n)], 128, [Z_])
-            else:
-                l = T[K("ls")][:, 128 * n - 128:128 * n]
-                tt(l, pZ[:, ns], T[K("pr")][:], A.add, [K("C")] + prk, [K("ls%d" % n)], 128, [Z_])
-                cp(T[K("lz")][:, ns], l, [K("ls%d" % n)], [K("lz%d" % n)], 128)
-        cp(ci[:, 0:16], pN[:, 400:416], [K("CE")], [K("i1")], 16, [N_])
-        ts(ci[:, 16:32], ci[:, 0:16], 3, None, A.bitwise_and, None, [K("i1")], [K("i2")], 16)
-        tt(ci[:, 32:48], pN[:, 384:400], ci[:, 16:32], A.add, [K("CE"), K("i2")], [K("t3")], 16, [N_])
-        mms([(pA[:, 256:384], T.Bh[:], T[K("PG")][:], True, True, 128)], ["Bh", K("PG")], [K("GP")], [A_])
-        tt(T[K("ru")][:], pA[:, 256:384], T[K("Gs")][:], A.is_equal, [K("GP"), K("Gs")], [K("ru")], 128, [A_])
-        tt(T[K("mo")][:], pA[:, 0:128], T[K("ru")][:], A.mult, [K("eT"), K("ru")], [K("mo")], 128, [A_])
-        mms([(pN[:, 256:384], T[K("fi")][:], T.Ih[:], True, True, 128),
-             (pN[:, 128:256], T[K("fi")][:], T.Tri[:], True, True, 128),
-             (pN[:, 0:128], T[K("ru")][:], T.Ih[:], True, True, 128),
-             (pN[:, 432:436], T[K("mo")][:], T.B16[:], True, True, 64)],
-            ["Ih", "Tri", "B16", K("fi"), K("ru"), K("mo"), K("NN")], [K("FI"), K("FN"), K("RN"), K("OC")], [N_])
-        act(T[K("rn")][:], pN[:, 0:128], F.Copy, [K("RN")], [K("rn")], 128, [N_])
-        tt(ci[:, 48:64], T.cst[:], ci[:, 32:48], A.subtract, ["cst", K("t3")], [K("t2")], 16)
-        ts(ci[:, 64:80], ci[:, 48:64], 12, None, A.bitwise_and, None, [K("t2")], [K("tb")], 16)
-        ts(ci[:, 84:88], pN[:, 384:388], -1.0, None, A.add, None, [K("CE")], [K("gi")], 4, [N_])
-        ts(ci[:, 88:92], ci[:, 84:88], 15, None, A.bitwise_and, None, [K("gi")], [K("hp")], 4)
-        ts(cf[:, 12:16], pN[:, 384:388], 0.5, None, A.is_gt, None, [K("CE")], [K("sm")], 4, [N_])
-        tt(T[K("PD")][:], pN[:, 256:384], T[K("Di")][:], A.mult, [K("FI"), K("Di")], [K("PD")], 128, [N_])
-        op("V", cyc(128), lambda: [V.tensor_tensor_scan(T[K("pr")][:], T.keep[:], T[K("PD")][:], 0.0, A.mult, A.add)],
-           [K("PD"), "keep"], prk)
-        ts(cf[:, 0:4], T[K("pr")][:, 31:128:32], -613.0, None, A.add, None, prk, [K("dp")], 4)
-        ts(cf[:, 4:8], cf[:, 0:4], 13.0, 2040.0, A.mult, A.add, [K("dp")], [K("nd")], 4)
-        tt(ci[:, 92:96], pN[:, 400:404], cf[:, 4:8], A.add, [K("CE"), K("nd")], [K("nd2")], 4, [N_])
-        ts(ci[:, 96:100], ci[:, 92:96], 4095, None, A.bitwise_and, None, [K("nd2")], [K("nd3")], 4)
-        tt(cf[:, 8:12], ci[:, 96:100], cf[:, 0:4], A.subtract, [K("nd3"), K("dp")], [K("dd")], 4)
+            mms([(pZ[:, ns], T.If[:], T[K("pr")][:], 512), (pZ[:, ns], T.nIh[:], T[K("rp")][:], 128)]
+                + ([(pZ[:, ns], T.I4[:, 128 * n - 128:128 * n], T[K("ah")][:], 128)] if n else []),
+                [K("ah"), K("rp"), "If", "nIh", "J1", "J2", "J3"] + prk, [K("Z%d" % n)], [Z_])
+            ts(T[K("lz")][:, ns], pZ[:, ns], -0.5 - WIN[n][0], None, A.add, None, [K("Z%d" % n)], [K("lz%d" % n)], 128, [Z_])
+        tt(cf[:, 64:68], pN[:, 448:452], cf[:, 60:64], A.subtract, [K("pk"), K("rnd")], [K("dd")], 4, [N_])
+        mms([(pN[:, 0:128], T.Bh[:], T[K("PG")][:], 128), (pN[:, 0:128], Hh[:, 16:144], I(-1), 128),
+             (pN[:, 0:128], T.nTri[:], T[K("fl")][:], 128)], ["Bh", K("PG"), K("Hh"), "I-1", "nTri", K("fl")], [K("G2")], [N_])
+        ts(T[K("ru")][:], pN[:, 0:128], 0.0, None, A.is_equal, None, [K("G2")], [K("ru")], 128, [N_])
+        tt(T[K("mo")][:], pA[:, 128:256], T[K("ru")][:], A.mult, [K("e0"), K("ru")], [K("mo")], 128, [A_])
+        mms([(pN[:, 0:20], T.ones[0:1, :], T.rowk[0:1, 0:20], 64), (pN[:, 0:20], I(1), cb[:, 20:40], 64),
+             (pN[:, 0:20], I(4), cb[:, 40:60], 64)], ["ones", "rowk", "I1", "I4", K("rem")], [K("G2")], [N_])
+        mms([(pN[:, 128:256], T[K("ru")][:], I(2), 128), (pN[:, 128:256], T[K("fi")][:], T.nSl[:], 128)],
+            [K("ru"), K("fi"), "I2", "nSl"], [K("m")], [N_])
+        mms([(pN[:, 256:384], T[K("fi")][:], I(1024), 128)], [K("fi"), "I1024"], [K("FI")], [N_])
+        ts(cb[:, 60:80], pN[:, 0:20], 0.0, None, A.is_ge, None, [K("G2")], [K("flg")], 20, [N_])
+        mms([(pN[:, 32:52], T.ones[0:1, :], T.rowk[0:1, 20:40], 64), (pN[:, 32:52], I(1), cb[:, 0:20], 64),
+             (pN[:, 32:52], I(-4), cb[:, 40:60], 64), (pN[:, 32:52], I(128), cb[:, 60:80], 64),
+             (pN[:, 36:52:5], I(112), cb[:, 63:80:5], 64), (pN[:, 36:52:5], T[K("mo")][:], T.B256[:], 64)],
+            ["ones", "rowk", "I1", "I-4", "I128", "I112", "B256", K("rem"), K("flg"), K("mo")], [K("key"), K("G2")], [N_], True, False)
 
     def zpart(t, q):
         K = lambda s: "%s%d" % (s, q)
-        pZ, Z_ = T[K("pZ")], K("pZ")
+        pZ, Z_, pN, N_ = T[K("pZ")], K("pZ"), T[K("pN")], K("pN")
         yb = T["y%d" % t]
-        yk = ["y%d_%d%d" % (t, q, h) for h in range(XP)]
-        mms([(pZ[:], T.ones[0:1, :], T.rowm[0:1, :], True, False, 512)], ["ones", "rowm"], [K("Z"), K("C"), K("C1"), K("C2"), K("C3")], [Z_])
         for n in ORDER:
-            win = T.Xw[:, 0:WIN[n]]
-            wk = ["X%d" % k for k in range(WIN[n] // 4096)]
+            win = T.Xw[:, WIN[n][0]:WIN[n][1]]
+            wk = X0 + ["X%d" % k for k in range(2 * n)]
             d, r = T["d%d%d" % (n, q)], T["r%d%d" % (n, q)]
-            pn = VPN if n in VT else SPN
-            w = 2048 // pn
-            for h in range(pn):
-                cs = slice(w * h, w * h + w)
-                ys = slice(2048 * q + w * h, 2048 * q + w * h + w)
-                src = win.indirect(T[K("lz")][:, 128 * n + (w // 16) * h:128 * n + (w // 16) * (h + 1)])
-                if n in VT:
-                    op("V", 60.0 + w * GC * CY, lambda cs=cs, ys=ys, src=src, d=d: [V.tensor_tensor(d[:, cs], src, yb[:, ys], A.subtract)],
-                       wk + yk + [K("lz%d" % n)], [K("d%d_%d" % (n, h))])
-                    ts(r[:, cs], d[:, cs], 0.0, None, A.max, None, [K("d%d_%d" % (n, h))], [K("r%d_%d" % (n, h))], w, half=True)
+            two = "R" in ZT[q][n]
+            h = 0
+            while h < 4:
+                ty = ZT[q][n][h]
+                m = 1
+                while m < (GS if ty == "S" else GV) and h + m < 4 and ZT[q][n][h + m] == ty:
+                    m += 1
+                hs = range(h, h + m)
+                cs = slice(512 * h, 512 * (h + m))
+                ys = slice(2048 * q + cs.start, 2048 * q + cs.stop)
+                yk = ["y%d_%d%d" % (t, q, k * XP // 4) for k in hs]
+                src = win.indirect(T[K("lz")][:, 128 * n + 32 * h:128 * n + 32 * (h + m)])
+                nm = "z" if two and ty != "R" else "d"
+                z, zk, rk = T["%s%d%d" % (nm, n, q)], [K("%s%d_%d" % (nm, n, k)) for k in hs], [K("r%d_%d" % (n, k)) for k in hs]
+                sc = 0.5 if two else None
+                if ty == "S":
+                    op("S", 80.0 + 512 * m * GC * CY, lambda cs=cs, src=src, z=z: [S.activation(z[:, cs], src, F.Copy)], wk + [K("lz%d" % n)], zk)
+                    for k in range(m):
+                        c5 = slice(cs.start + 512 * k, cs.start + 512 * k + 512)
+                        y5 = slice(ys.start + 512 * k, ys.start + 512 * k + 512)
+                        mms([(T[K("pS")][:], I(1), z[:, c5], 512), (T[K("pS")][:], I(-1), yb[:, y5], 512)], ["I1", "I-1", zk[k], yk[k]], [K("sub")], [K("pS")])
+                        act(r[:, c5], T[K("pS")][:], F.Abs, [K("sub")], [rk[k]], 512, [K("pS")], sc)
                 else:
-                    op("S", 80.0 + w * GC * CY, lambda cs=cs, src=src, d=d: [S.activation(d[:, cs], src, F.Copy)],
-                       wk + [K("lz%d" % n)], [K("d%d_%d" % (n, h))])
-                    for s in range(4 * h // SPN, 4 * (h + 1) // SPN):
-                        c5 = slice(512 * s, 512 * s + 512)
-                        y5 = slice(2048 * q + 512 * s, 2048 * q + 512 * s + 512)
-                        mms([(T[K("pS")][:], T.Ib[:], d[:, c5], True, False, 512), (T[K("pS")][:], T.nIb[:], yb[:, y5], False, True, 512)],
-                            ["Ib", "nIb", K("d%d_%d" % (n, h))] + yk, [K("subpS%d" % q)], [K("pS")])
-                        act(r[:, c5], T[K("pS")][:], F.Abs, [K("subpS%d" % q)], [K("r%d_%d" % (n, s))], 512, [K("pS")])
-            lst = []
-            last = n == ORDER[3]
-            for i in range(16):
-                o = pZ[:, 128 * n + i:128 * n + 128:16]
-                if n in VT:
-                    lst.append((o, r[:, i:2048:16], T.sel2[:], False, False, 64))
-                    lst.append((o, d[:, i:2048:16], T.seln[:], False, last and i == 15, 64))
-                else:
-                    lst.append((o, r[:, i:2048:16], T.sel[:], False, last and i == 15, 64))
-            mms(lst, ["sel", "sel2", "seln", K("Z")] + [K("r%d_%d" % (n, s)) for s in range(VPN if n in VT else 4)]
-                + [K("d%d_%d" % (n, s)) for s in range(pn)], [K("Zt%d" % n)], [Z_])
+                    op("V", 60.0 + 512 * m * GC * CY, lambda cs=cs, ys=ys, src=src, z=z: [V.tensor_tensor(z[:, cs], src, yb[:, ys], A.subtract)],
+                       wk + yk + [K("lz%d" % n)], zk)
+                    if ty == "R":
+                        ts(r[:, cs], z[:, cs], 0.0, None, A.max, None, zk, rk, 512 * m, half=True)
+                    else:
+                        act(r[:, cs], z[:, cs], F.Abs, zk, rk, 512 * m, (), sc)
+                h += m
+            ns = slice(128 * n, 128 * n + 128)
+            lst = [(pZ[:, ns], T.ones[0:1, :], T.rowm[0:1, :], 128)]
+            if two:
+                lst += [(pZ[:, 128 * n + i:128 * n + 128:16], d[:, i:2048:16], T.seln[:], 64) for i in range(16)]
+            lst += [(pZ[:, 128 * n + i:128 * n + 128:16], r[:, i:2048:16], T.sel2[:] if two else T.sel[:, 0:8], 64) for i in range(16)]
+            mms(lst, ["ones", "rowm", "sel", "sel2", "seln"] + [K("r%d_%d" % (n, s)) for s in range(4)]
+                + [K("d%d_%d" % (n, s)) for s in range(4) if two], [K("Z%d" % n)], [Z_])
+            tt(T[K("mz")][:, ns], pZ[:, ns], T[K("ru")][:], A.mult, [K("Z%d" % n), K("ru")], [K("mz%d" % n)], 128, [Z_])
+            mms([(pN[:, 32 + n:52:5], T[K("mz")][:, ns], T.B256[:], 64)], ["B256", K("mz%d" % n)], [K("key")], [N_], False, n == ORDER[3])
 
     def fin(t, q):
         K = lambda s: "%s%d" % (s, q)
-        pZ, Z_, pN, N_ = T[K("pZ")], K("pZ"), T[K("pN")], K("pN")
-        ci, cf = T[K("ci")], T[K("cf")]
-        for n in range(4):
-            ns = slice(128 * n, 128 * n + 128)
-            tt(T[K("mz")][:, ns], pZ[:, ns], T[K("ru")][:], A.mult, [K("Z"), K("Zt0"), K("Zt1"), K("Zt2"), K("Zt3"), K("ru")],
-               [K("mz%d" % n)], 128, [Z_])
-        mms([(pN[:, 416 + 4 * n:420 + 4 * n], T[K("mz")][:, 128 * n:128 * n + 128], T.B16[:], True, True, 64) for n in range(4)],
-            ["B16", K("NN")] + [K("mz%d" % n) for n in range(4)], [K("EC")], [N_])
-        tt(cf[:, 16:32], pN[:, 416:432], ci[:, 64:80], A.add, [K("EC"), K("tb")], [K("key")], 16, [N_])
-        tt(cf[:, 32:40], cf[:, 16:24], cf[:, 24:32], A.min, [K("key")], [K("k1")], 8)
-        tt(ci[:, 100:104], cf[:, 32:36], cf[:, 36:40], A.min, [K("k1")], [K("k2")], 4)
-        tt(cf[:, 40:44], pN[:, 432:436], ci[:, 100:104], A.is_gt, [K("k2"), K("OC")], [K("bt")], 4, [N_])
-        ts(ci[:, 104:108], ci[:, 100:104], 12, None, A.bitwise_and, None, [K("k2")], [K("m4")], 4)
-        tt(ci[:, 108:112], ci[:, 104:108], cf[:, 40:44], A.mult, [K("m4"), K("bt")], [K("me")], 4)
-        tt(ci[:, 112:116], ci[:, 108:112], ci[:, 32:36], A.add, [K("me"), K("t3")], [K("hr")], 4)
-        ts(ci[:, 116:120], ci[:, 112:116], 15, None, A.bitwise_and, None, [K("hr")], [K("hn")], 4)
-        tt(cf[:, 52:56], ci[:, 116:120], ci[:, 88:92], A.subtract, [K("hn"), K("hp")], [K("df")], 4)
-        fnk = [K("fn%d" % b) for b in range(4)]
-        for b in range(4):
-            ps = pN[:, 128 + 32 * b:160 + 32 * b]
-            ts(ps, ps, cf[:, 40 + b:41 + b], cf[:, 52 + b:53 + b], A.max, A.mult, [K("FN"), K("bt"), K("df")], [fnk[b]], 32, [N_])
-        tt(pN[:, 128:256], pN[:, 128:256], T[K("rn")][:], A.mult, fnk + [K("rn")], [K("FN")] + fnk, 128, [N_])
-        tt(T[K("Hh")][:], pN[:, 128:256], T[K("Hh")][:], A.add, [K("FN"), K("Hh")], [K("Hh")], 128, [N_])
-        ts(cf[:, 44:48], cf[:, 40:44], -1.0, 1.0, A.mult, A.add, [K("bt")], [K("nb")], 4)
-        tt(cf[:, 56:60], cf[:, 8:12], cf[:, 44:48], A.mult, [K("dd"), K("nb")], [K("md")], 4)
-        fik = [K("fi%d" % b) for b in range(4)]
+        pN, N_ = T[K("pN")], K("pN")
+        cf, ch, Hh, Dp = T[K("cf")], T[K("ch")], T[K("Hh")], T[K("Dp")]
+        last = t == RO - 1
+        if last:
+            ts(T[K("oD")][:], Dp[:], -FR, None, A.add, None, [K("Dp")], [K("oD")], 128)
+            ts(T[K("oH")][:], Hh[:, 16:144], -0.5, None, A.add, None, [K("Hh")], [K("oH")], 128)
+            tt(T[K("oA")][:], T.Ab[:, 4 * q:4 * q + 4], ch[:, 0:4], A.add, ["Ab", K("a")], [K("oA")], 4)
+        op("V", cyc(64), lambda: [V.tensor_tensor_scan(cf[:, 72:92], T.rs[:], pN[:, 32:52], 0.0, A.add, A.min)],
+           [K("key"), "rs"], [K("sc")], [N_])
+        ts(cf[:, 96:100], cf[:, 76:92:5], M32, -M32, A.add, A.add, [K("sc")], [K("r32")], 4)
+        tt(cf[:, 92:96], cf[:, 75:92:5], cf[:, 76:92:5], A.is_gt, [K("sc")], [K("mut")], 4)
+        tt(cf[:, 100:104], cf[:, 76:92:5], cf[:, 96:100], A.subtract, [K("sc"), K("r32")], [K("df")], 4)
+        fik = [K("f%d" % b) for b in range(4)]
         for b in range(4):
             ps = pN[:, 256 + 32 * b:288 + 32 * b]
-            ts(ps, ps, cf[:, 56 + b:57 + b], None, A.mult, None, [K("FI"), K("md")], [fik[b]], 32, [N_])
-        tt(T[K("Di")][:], pN[:, 256:384], T[K("Di")][:], A.add, fik + [K("Di")], [K("Di"), K("FI")], 128, [N_])
-        tt(cf[:, 64:68], cf[:, 12:16], cf[:, 44:48], A.mult, [K("sm"), K("nb")], [K("as")], 4)
-        tt(ci[:, 120:124], ci[:, 120:124], cf[:, 64:68], A.add, [K("A"), K("as")], [K("A")], 4)
+            ts(ps, ps, cf[:, 92 + b:93 + b], cf[:, 64 + b:65 + b], A.mult, A.mult, [K("FI"), K("mut"), K("dd")], [fik[b]], 32, [N_])
+        mk = [K("m%d" % b) for b in range(4)]
+        for b in range(4):
+            ps = pN[:, 128 + 32 * b:160 + 32 * b]
+            ts(ps, ps, cf[:, 92 + b:93 + b], cf[:, 100 + b:101 + b], A.is_gt, A.mult, [K("m"), K("mut"), K("df")], [mk[b]], 32, [N_])
+        if last:
+            tt(T[K("oD")][:], pN[:, 256:384], T[K("oD")][:], A.add, fik + [K("oD")], [K("oD")], 128, [N_])
+            tt(T[K("oH")][:], pN[:, 128:256], T[K("oH")][:], A.add, mk + [K("oH")], [K("oH")], 128, [N_])
+            tt(T[K("oA")][:], T[K("oA")][:], cf[:, 92:96], A.add, [K("oA"), K("mut")], [K("oA")], 4)
+            for nm, y, n in (("oD", T.yD, 128), ("oH", T.yH, 128), ("oA", T.yA, 4)):
+                load(y[:, n * q:n * q + n], T[K(nm)][:], "out", [], 2000.0, [K(nm)])
+            return
+        tt(Dp[:], pN[:, 256:384], Dp[:], A.add, fik + [K("Dp")], [K("Dp"), K("FI")], 128, [N_])
+        if HCOPY:
+            tt(pN[:, 128:256], pN[:, 128:256], Hh[:, 16:144], A.add, mk + [K("Hh")], [K("m")], 128, [N_])
+        else:
+            tt(Hh[:, 16:144], pN[:, 128:256], Hh[:, 16:144], A.add, mk + [K("Hh")], [K("Hh"), K("m")], 128, [N_])
+        tt(ch[:, 0:4], ch[:, 0:4], cf[:, 92:96], A.add, [K("a"), K("mut")], [K("a")], 4)
 
     for q in range(2):
         xpart(0, q)
-    konst()
     chunk[0] = 0
-    for k in range(VCOPIES + 1, COPIES):
-        op("Y", 60.0, lambda k=k: g.sync.dma_start(T.Xw[:, 4096 * k:4096 * k + 4096], T.Xw[:, 0:4096]),
-           ["X0"] + ["x0_0%d" % h for h in range(XP)], ["X%d" % k], (), 2000.0 + 4000.0 * (k - VCOPIES), "lx%d" % k, 16)
-    for k in range(1, VCOPIES + 1):
-        cp(T.Xw[:, 4096 * k:4096 * k + 4096], T.Xw[:, 0:4096], ["X0"], ["X%d" % k], 4096, half=True)
+    konst()
+    for k in range(6):
+        a = 4096 - 2048 * (k // 2) if k % 2 == 0 else 10240 + 2048 * (k // 2)
+        c = 6144 + (a - 6144) % 4096
+        out, src = T.Xw[:, a:a + 2048], T.Xw[:, c:c + 2048]
+        if COPY[k] == "V":
+            cp(out, src, X0, ["X%d" % k], 2048, half=True)
+        elif COPY[k] == "S":
+            act(out, src, F.Copy, X0, ["X%d" % k], 2048)
+        else:
+            load(out, src, "lc%d" % k, ["X%d" % k], 6000.0, X0)
     for t in range(RO):
         for q in range(2):
             chunk[0] = q
@@ -465,16 +500,8 @@ def rank_program(g, core, T, topo):
             epart(t, q)
             zpart(t, q)
             fin(t, q)
-            if t < RO - 1:
-                if q == 1:
-                    op("loc%d" % t, 0.0, None, (), ["loc%d" % t], (), 1000.0, "loc%d" % t, 16 * 2 * XP)
-    for q in range(2):
-        K = lambda s: "%s%d" % (s, q)
-        for nm, src, add, y, n in (("PD", T["Di%d" % q][:], -613.0, T.yD, 128), ("Gs", T["Hh%d" % q][:], -0.5, T.yH, 128),
-                                   ("ya", T["ci%d" % q][:, 120:124], 0.0, T.yA, 4)):
-            k = {"PD": "Di", "Gs": "Hh", "ya": "A"}[nm]
-            ts(T[K(nm)][:], src, add, None, A.add, None, [K(k)], [K(nm)], n)
-            op("Y", 60.0, lambda nm=nm, y=y, n=n, q=q: g.sync.dma_start(y[:, n * q:n * q + n], T[K2(nm, q)][:]), [K(nm)], [], (), 2000.0, "out", 16)
+        if t < RO - 1:
+            op("loc%d" % t, 0.0, None, (), ["loc%d" % t], (), 1000.0, "loc%d" % t, 16 * 2 * XP)
 
     seq = schedule(ops)
     SEM = {"V": "sv", "S": "ss", "P": "sp", "G": "sg"}
@@ -529,7 +556,3 @@ def rank_program(g, core, T, topo):
         g.wait_ge(T.sem[s], count[s])
     for t in range(RO):
         g.wait_ge(T.sem["loc%d" % t], 16 * 2 * XP)
-
-
-def K2(s, q):
-    return "%s%d" % (s, q)

@@ -5,7 +5,13 @@ A = AluOpType
 F = ActivationFunctionType
 RO = 5
 DIST = (1, 3, 6)
-XW = 16384
+PS = 8
+TWOB = 1
+DIRECT = 1
+PDSEP = False
+CW = 512
+L0 = 4
+XW = 18560
 WIN = [(6144 - 2048 * n, 10240 + 2048 * n) for n in range(4)]
 FR = 613.0 + 1.0 / 32
 M4 = 1.5 * 2 ** 25
@@ -14,8 +20,9 @@ M1K = 1.5 * 2 ** 33
 M4K = 1.5 * 2 ** 35
 GV = 1
 GS = 1
+GD = 2
 XP = 4
-XT = ("SSSV", "SSSV")
+XT = ("VSSS", "SSSS")
 XT0 = ("SVSV", "SVSV")
 ZT = (("RRRR", "SSSS", "RRRR", "ASSS"), ("RRRR", "SSSS", "RRRR", "ASSS"))
 ORDER = (0, 1, 2, 3)
@@ -39,26 +46,26 @@ SCRATCH["nTri"] = ("sbuf", [128, 128], "bfloat16")
 for _n in ("nIh", "Bh", "Bih", "Be", "Bg", "oneh", "rowp"):
     SCRATCH[_n] = ("sbuf", [128, 128], "float16")
 SCRATCH["I4"] = ("sbuf", [128, 384], "float16")
-SCRATCH["B256"] = ("sbuf", [128, 4], "float16")
+SCRATCH["B256"] = ("sbuf", [128, 8], "float16")
 SCRATCH["Bd"] = ("sbuf", [128, 8], "float32")
 SCRATCH["sel"] = ("sbuf", [128, 16], "bfloat16")
 for _n in ("selt", "sel2", "seln"):
     SCRATCH[_n] = ("sbuf", [128, 8], "bfloat16")
 SCRATCH["rowm"] = ("sbuf", [128, 128], "bfloat16")
-SCRATCH["rowk"] = ("sbuf", [128, 40], "bfloat16")
-SCRATCH["rs"] = ("sbuf", [128, 20], "float32")
+SCRATCH["rowk"] = ("sbuf", [128, 60], "bfloat16")
+SCRATCH["rs"] = ("sbuf", [128, 40], "float32")
 SCRATCH["If"] = ("sbuf", [128, 128], "float32")
 for _q in range(2):
     for _n in range(4):
         SCRATCH["d%d%d" % (_n, _q)] = ("sbuf", [128, 2048], "bfloat16")
         SCRATCH["r%d%d" % (_n, _q)] = ("sbuf", [128, 2048], "bfloat16")
-        if "R" in ZT[_q][_n] and ZT[_q][_n] != "RRRR":
+        if set(ZT[_q][_n]) & set("RD") and set(ZT[_q][_n]) - set("RD"):
             SCRATCH["z%d%d" % (_n, _q)] = ("sbuf", [128, 2048], "bfloat16")
     for _n, _w, _d in (("ab", 2048, "bfloat16"), ("Dp", 128, "float32"), ("Hh", 144, "bfloat16"), ("fl", 128, "bfloat16"),
                        ("TR", 256, "float16"), ("ov", 128, "bfloat16"), ("fi", 128, "bfloat16"), ("PG", 128, "float16"),
                        ("Pe", 128, "float16"), ("Pd", 128, "float32"), ("ru", 128, "bfloat16"), ("mo", 128, "float16"),
                        ("mz", 512, "float16"), ("pr", 128, "float32"), ("lz", 512, "uint16"), ("lx", 128, "uint16"),
-                       ("ah", 128, "float16"), ("rp", 128, "float16"), ("xi", 128, "int32"), ("cf", 112, "float32"), ("cb", 80, "bfloat16"),
+                       ("ah", 128, "float16"), ("rp", 128, "float16"), ("xi", 128, "int32"), ("cf", 144, "float32"), ("cb", 80, "bfloat16"),
                        ("ch", 8, "float16"), ("oD", 128, "float32"), ("oH", 128, "float32"), ("oA", 4, "float32")):
         SCRATCH["%s%d" % (_n, _q)] = ("sbuf", [128, _w], _d)
     for _n in ("pA", "pZ", "pN", "pS"):
@@ -67,14 +74,20 @@ for _q in range(2):
 SEMAPHORES = ["sv", "ss", "sp", "sg", "out", "ldD", "ldH", "ldt", "ldA", "lxa", "lxb"]
 SEMAPHORES += ["lc%d" % k for k in range(6)] + ["loc%d" % t for t in range(RO)]
 SEMAPHORES += ["ar%d%d%d" % (t, q, h) for t in range(RO) for q in range(2) for h in range(XP)]
+SEMAPHORES += ["ac%d%d%d" % (q, n, h) for q in range(2) for n in range(4) for h in range(4) if ZT[q][n][h] in "DE"]
 
-CY = 0.83 * 1.2
+GDMA = 1000.0
+ACC0 = 2000.0
+ACC1 = 1300.0
+CY = 0.9
 GC = 1.56
-HOP = 120.0
-OWN = 60.0
-ARR = 2600.0
-BIAS = 7000.0
-SLACK = 200.0
+HOP = 250.0
+OWN = 250.0
+ARR = 3200.0
+PASSES = 4
+LEAD = 1.5
+BIAS = 1000000.0
+SLACK = 150.0
 
 
 def schedule(ops):
@@ -87,7 +100,9 @@ def schedule(ops):
     for i in range(n - 1, -1, -1):
         prio[i] = ops[i]["cost"] + ops[i]["lat"] + max([prio[j] + HOP for j in succ[i]], default=0.0)
     for i in range(n):
-        prio[i] += BIAS if ops[i]["ch"] == 0 else 0.0
+        prio[i] -= BIAS * ops[i]["ch"]
+    for i in range(n - 1, -1, -1):
+        prio[i] = max([prio[i]] + [prio[j] + 1.0 for j in succ[i]])
     left = [len(o["hard"] | o["order"]) for o in ops]
     ready = [0.0] * n
     avail = {}
@@ -120,6 +135,76 @@ def schedule(ops):
             if left[j] == 0:
                 pend.setdefault(ops[j]["q"], []).append(j)
     return done
+
+
+def place(ops, seq, before):
+    st = [0.0] * len(ops)
+    taken = {}
+    for i in seq:
+        t = max([st[j] + d for j, d in before[i]], default=0.0)
+        c = ops[i]["cost"]
+        lst = taken.setdefault(ops[i]["q"], [])
+        k = len(lst)
+        while k > 0 and lst[k - 1][1] > t:
+            k -= 1
+        while k < len(lst) and lst[k][0] < t + c:
+            t = max(t, lst[k][1])
+            k += 1
+        lst.insert(k, (t, t + c))
+        st[i] = t
+    return st
+
+
+def tighten(ops, seq):
+    n = len(ops)
+    fwd = [[] for _ in range(n)]
+    bwd = [[] for _ in range(n)]
+    for j, o in enumerate(ops):
+        for i in o["hard"] | o["order"]:
+            same = ops[i]["q"] == o["q"]
+            if i in o["hard"]:
+                gap = ops[i]["lat"] + (OWN if same else HOP)
+            else:
+                gap = 0.0 if same else -ops[i]["cost"]
+            fwd[j].append((i, ops[i]["cost"] + gap))
+            bwd[i].append((j, o["cost"] + gap))
+    best = None
+    for _ in range(PASSES):
+        st = place(ops, seq, fwd)
+        span = max(st[i] + ops[i]["cost"] + ops[i]["lat"] for i in range(n))
+        pos = {i: k for k, i in enumerate(seq)}
+        seq = sorted(range(n), key=lambda i: (st[i], pos[i]))
+        if best is None or span < best[0]:
+            best = (span, seq)
+        pos = {i: k for k, i in enumerate(seq)}
+        back = sorted(range(n), key=lambda i: (-st[i] - ops[i]["cost"], -pos[i]))
+        back = topo_fix(back, bwd)
+        sb = place(ops, back, bwd)
+        pos = {i: k for k, i in enumerate(back)}
+        seq = topo_fix(sorted(range(n), key=lambda i: (-sb[i] - ops[i]["cost"], -pos[i])), fwd)
+    return best[1]
+
+
+def topo_fix(seq, before):
+    out, seen = [], set()
+    for i in seq:
+        stack = [i]
+        while stack:
+            k = stack[-1]
+            if k in seen:
+                stack.pop()
+                continue
+            miss = [j for j, d in before[k] if j not in seen]
+            if miss:
+                stack.extend(miss)
+            else:
+                seen.add(k)
+                out.append(k)
+                stack.pop()
+    return out
+
+
+PLAN = {}
 
 
 def rank_program(g, core, T, topo):
@@ -189,7 +274,7 @@ def rank_program(g, core, T, topo):
         op("P", sum(x[3] for x in lst) * 0.417 * 1.2 + 5.0 * len(lst), f, R, W, banks)
 
     def load(out, in_, sem, W, lat, R=()):
-        op("Y", 60.0, lambda: g.sync.dma_start(out, in_), R, W, (), lat, sem, 16)
+        return op("Y", 60.0, lambda: g.sync.dma_start(out, in_), R, W, (), lat, sem, 16)
 
     def fill(ap, val, W, n=64):
         op("V", cyc(n), lambda: [V.memset(ap, val)], (), W)
@@ -200,12 +285,14 @@ def rank_program(g, core, T, topo):
     def I(k):
         return T.Is[:, 128 * IS[k]:128 * IS[k] + 128]
 
-    load(T.Dl[:], T.D[:], "ldD", ["Dl"], 7000.0)
-    load(T.Hl[:], T.H[:], "ldH", ["Hl"], 7000.0)
-    load(T.Xw[:, 6451:10240], T.X[:, 0:3789], "lxa", ["Xa"], 6500.0)
-    load(T.Xw[:, 6144:6451], T.X[:, 3789:4096], "lxb", ["Xb"], 6500.0)
-    load(T.tl[:], T.th[:], "ldt", ["tl"], 6500.0)
-    load(T.Al[:], T.A[:], "ldA", ["Al"], 6500.0)
+    loads = [load(T.Dl[:], T.D[:], "ldD", ["Dl"], 2700.0),
+             load(T.Hl[:], T.H[:], "ldH", ["Hl"], 3300.0),
+             load(T.Xw[:, 6451:10240], T.X[:, 0:3789], "lxa", ["Xa"], 8000.0),
+             load(T.Xw[:, 6144:6451], T.X[:, 3789:4096], "lxb", ["Xb"], 8000.0),
+             load(T.tl[:], T.th[:], "ldt", ["tl"], 8000.0),
+             load(T.Al[:], T.A[:], "ldA", ["Al"], 8000.0)]
+    for a, b in zip(loads, loads[1:]):
+        ops[b]["order"].add(a)
     X0 = ["Xa", "Xb"]
 
     fill(T.ones[:], 1.0, ["ones"])
@@ -245,7 +332,8 @@ def rank_program(g, core, T, topo):
         ts(T.Tri[:], T.Tri[:], 16.0, None, A.mult, None, ["Tri"], ["Tri"], 128, half=True)
         cp(T.Bh[:], T.Bb[:], ["Bb"], ["Bh"], 128, half=True)
         cp(T.Bih[:], T.Bi[:], ["Bi"], ["Bih"], 128, half=True)
-        ts(T.B256[:], T.Bb[:, 0:128:32], 256.0, None, A.mult, None, ["Bb"], ["B256"], 4)
+        ts(T.B256[:, 0:4], T.Bb[:, 0:128:32], 256.0, None, A.mult, None, ["Bb"], ["B256"], 4)
+        ts(T.B256[:, 4:8], T.Bb[:, 0:128:32], 256.0, None, A.mult, None, ["Bb"], ["B256"], 4)
         ts(T.Bd[:, 0:4], T.Bb[:, 0:128:32], 13.0 / 1024, None, A.mult, None, ["Bb"], ["Bd0"], 4)
         ts(T.Bd[:, 4:8], T.Bb[:, 0:128:32], 12.0 / 1024, None, A.mult, None, ["Bb"], ["Bd1"], 4)
         fill(T.Ce[:], 1.0, ["Ce"])
@@ -272,8 +360,9 @@ def rank_program(g, core, T, topo):
         for n in range(5):
             fill(T.rowk[0:1, n:20:5], 0.5 - 4 * (n + 1) if n < 4 else 0.0, ["rowk"])
             fill(T.rowk[0:1, 20 + n:40:5], 32.0 + 36 * n if n < 4 else 1.0, ["rowk"])
+            fill(T.rowk[0:1, 40 + n:60:5], 32.0 + 32 * n if n < 4 else 0.0, ["rowk"])
         fill(T.rs[:], 0.0, ["rs"])
-        fill(T.rs[:, 0:20:5], 1e9, ["rs"])
+        fill(T.rs[:, 0:40:5], 1e9, ["rs"])
         ts(T.thm[:], T.tl[:], -2040.0, None, A.add, None, ["tl"], ["thm"], 8)
         ts(T.Am[:], T.Al[:], 31, None, A.bitwise_and, None, ["Al"], ["Am"], 8)
         tt(T.Ab[:], T.Al[:], T.Am[:], A.subtract, ["Al", "Am"], ["Ab"], 8)
@@ -284,12 +373,11 @@ def rank_program(g, core, T, topo):
             for n in range(4):
                 if "z%d%d" % (n, q) in SCRATCH:
                     for h in range(4):
-                        if ZT[q][n][h] != "R":
+                        if ZT[q][n][h] not in "RD":
                             fill(T["d%d%d" % (n, q)][:, 512 * h:512 * h + 512], 0.0, ["d%d_%d%d" % (n, h, q)], 256)
 
     def xpart(t, q):
         K = lambda s: "%s%d" % (s, q)
-        chunk[0] = q
         xb = "x%d" % (t % 3)
         if t == 0 or not HCOPY:
             tt(T[K("xi")][:], T[K("Dp")][:], T[K("Hh")][:, 16:144], A.mult, [K("Dp"), K("Hh")], [K("xi")], 128)
@@ -359,24 +447,41 @@ def rank_program(g, core, T, topo):
             act(T[K("fi")][:], pA[:, 0:128], F.Relu, [K("e1")], [K("fi")], 128, [A_])
         tt(T[K("Pe")][:], pA[:, 128:256], T[K("fi")][:], A.mult, [K("e0"), K("fi")], [K("Pe")], 128, [A_])
         tt(T[K("PG")][:], pA[:, 256:384], T[K("fi")][:], A.mult, [K("G1"), K("fi")], [K("PG")], 128, [A_])
-        tt(T[K("Pd")][:], pA[:, 384:512], T[K("fi")][:], A.mult, [K("DT"), K("fi")], [K("Pd")], 128, [A_])
-        mms([(pN[:, 384:512], T.oneh[0:2, :], T.rowp[0:2, :], 128), (pN[:, 384:512], T[K("Pe")][:], T.Be[:], 128),
-             (pN[:, 384:512], T[K("PG")][:], T.Bg[:], 128)],
-            [K("Pe"), K("PG"), "oneh", "rowp", "Be", "Bg"], [K("pk")], [N_], True, False)
-        mms([(pN[:, 444:452], T[K("Pd")][:], T.Bd[:], 256)], [K("Pd"), "Bd0", "Bd1"], [K("pk")], [N_], False, True)
+        if not PDSEP:
+            tt(T[K("Pd")][:], pA[:, 384:512], T[K("fi")][:], A.mult, [K("DT"), K("fi")], [K("Pd")], 128, [A_])
+        mms([(pN[:, 384:512], T.oneh[0:2, :], T.rowp[0:2, :], 128)], ["oneh", "rowp"], [K("pk")], [N_], True, False)
+        mms([(pN[:, 384:512], T[K("Pe")][:], T.Be[:], 128)], [K("Pe"), "Be"], [], [N_], False, False)
+        mms([(pN[:, 384:512], T[K("PG")][:], T.Bg[:], 128)], [K("PG"), "Bg"], [K("pk")], [N_], False, PDSEP)
+        if not PDSEP:
+            mms([(pN[:, 444:452], T[K("Pd")][:], T.Bd[:], 256)], [K("Pd"), "Bd0", "Bd1"], [K("pk")], [N_], False, True)
         ts(cf[:, 0:64], pN[:, 384:448], M4, -M4, A.add, A.add, [K("pk")], [K("rnd")], 64, [N_])
         tt(cb[:, 0:60], pN[:, 452:512], cf[:, 0:60], A.subtract, [K("pk"), K("rnd")], [K("rem")], 60, [N_])
         prk = [K("pr%d" % b) for b in range(4)]
+        for b in range(L0 if t >= DIRECT else 0):
+            bs = slice(32 * b, 32 * b + 32)
+            ts(T[K("lz")][:, bs], T[K("Dp")][:, bs], cb[:, 5 * b:5 * b + 1], None, A.mult, None, [K("Dp"), K("rem")], [K("lz0_%d" % b)], 32)
         for b in range(4):
             bs = slice(32 * b, 32 * b + 32)
             ts(T[K("pr")][:, bs], T[K("Dp")][:, bs], cb[:, 5 * b:5 * b + 1], 2048.5, A.mult, A.add, [K("Dp"), K("rem")], [prk[b]], 32)
         ts(T[K("rp")][:], T[K("pr")][:], M4K, -M4K - 8192.0, A.add, A.add, prk, [K("rp")], 128)
         for n in ORDER:
             ns = slice(128 * n, 128 * n + 128)
+            if n == 0 and t >= DIRECT:
+                if L0 < 4:
+                    ts(T[K("lz")][:, 32 * L0:128], T[K("pr")][:, 32 * L0:128], -2048.5, None, A.add, None, prk,
+                       [K("lz0_%d" % b) for b in range(L0, 4)], 128 - 32 * L0)
+                continue
             mms([(pZ[:, ns], T.If[:], T[K("pr")][:], 512), (pZ[:, ns], T.nIh[:], T[K("rp")][:], 128)]
                 + ([(pZ[:, ns], T.I4[:, 128 * n - 128:128 * n], T[K("ah")][:], 128)] if n else []),
                 [K("ah"), K("rp"), "If", "nIh", "J1", "J2", "J3"] + prk, [K("Z%d" % n)], [Z_])
-            ts(T[K("lz")][:, ns], pZ[:, ns], -0.5 - WIN[n][0], None, A.add, None, [K("Z%d" % n)], [K("lz%d" % n)], 128, [Z_])
+            ts(T[K("lz")][:, ns], pZ[:, ns], -0.5 - WIN[n][0], None, A.add, None, [K("Z%d" % n)],
+               [K("lz%d_%d" % (n, b)) for b in range(4)], 128, [Z_])
+        chunk[0] = 2 * t + q
+        if PDSEP:
+            tt(T[K("Pd")][:], pA[:, 384:512], T[K("fi")][:], A.mult, [K("DT"), K("fi")], [K("Pd")], 128, [A_])
+            mms([(pN[:, 444:452], T.oneh[0:2, :], T.rowp[0:2, 60:68], 64), (pN[:, 444:452], T[K("Pe")][:], T.Be[:, 60:68], 64),
+                 (pN[:, 444:452], T[K("Pd")][:], T.Bd[:], 256)], [K("Pe"), K("Pd"), "Bd0", "Bd1"], [K("pk")], [N_])
+            ts(cf[:, 60:64], pN[:, 444:448], M4, -M4, A.add, A.add, [K("pk")], [K("rnd")], 4, [N_])
         tt(cf[:, 64:68], pN[:, 448:452], cf[:, 60:64], A.subtract, [K("pk"), K("rnd")], [K("dd")], 4, [N_])
         mms([(pN[:, 0:128], T.Bh[:], T[K("PG")][:], 128), (pN[:, 0:128], Hh[:, 16:144], I(-1), 128),
              (pN[:, 0:128], T.nTri[:], T[K("fl")][:], 128)], ["Bh", K("PG"), K("Hh"), "I-1", "nTri", K("fl")], [K("G2")], [N_])
@@ -388,44 +493,64 @@ def rank_program(g, core, T, topo):
             [K("ru"), K("fi"), "I2", "nSl"], [K("m")], [N_])
         mms([(pN[:, 256:384], T[K("fi")][:], I(1024), 128)], [K("fi"), "I1024"], [K("FI")], [N_])
         ts(cb[:, 60:80], pN[:, 0:20], 0.0, None, A.is_ge, None, [K("G2")], [K("flg")], 20, [N_])
-        mms([(pN[:, 32:52], T.ones[0:1, :], T.rowk[0:1, 20:40], 64), (pN[:, 32:52], I(1), cb[:, 0:20], 64),
-             (pN[:, 32:52], I(-4), cb[:, 40:60], 64), (pN[:, 32:52], I(128), cb[:, 60:80], 64),
-             (pN[:, 36:52:5], I(112), cb[:, 63:80:5], 64), (pN[:, 36:52:5], T[K("mo")][:], T.B256[:], 64)],
+        mms([(pN[:, 32:72], T.ones[0:1, :], T.rowk[0:1, 20:60], 64), (pN[:, 32:52], I(1), cb[:, 0:20], 64),
+             (pN[:, 32:52], I(-4), cb[:, 40:60], 64), (pN[:, 32:52], I(128), cb[:, 60:80], 64), (pN[:, 52:72], I(128), cb[:, 60:80], 64),
+             (pN[:, 36:52:5], I(112), cb[:, 63:80:5], 64), (pN[:, 56:72:5], I(128), cb[:, 63:80:5], 64),
+             (pN[:, 36:72:5], T[K("mo")][:], T.B256[:], 64)],
             ["ones", "rowk", "I1", "I-4", "I128", "I112", "B256", K("rem"), K("flg"), K("mo")], [K("key"), K("G2")], [N_], True, False)
 
     def zpart(t, q):
         K = lambda s: "%s%d" % (s, q)
         pZ, Z_, pN, N_ = T[K("pZ")], K("pZ"), T[K("pN")], K("pN")
         yb = T["y%d" % t]
+        subs = [0]
         for n in ORDER:
             win = T.Xw[:, WIN[n][0]:WIN[n][1]]
             wk = X0 + ["X%d" % k for k in range(2 * n)]
+            if n == 0 and t >= DIRECT:
+                win = T.Xw[:, 2048:18560]
+                wk = X0 + ["X%d" % k for k in range(8)]
             d, r = T["d%d%d" % (n, q)], T["r%d%d" % (n, q)]
-            two = "R" in ZT[q][n]
+            two = "R" in ZT[q][n] or "D" in ZT[q][n]
             h = 0
             while h < 4:
                 ty = ZT[q][n][h]
                 m = 1
-                while m < (GS if ty == "S" else GV) and h + m < 4 and ZT[q][n][h + m] == ty:
+                while m < {"S": GS, "D": GD, "E": GD}.get(ty, GV) and h + m < 4 and ZT[q][n][h + m] == ty:
                     m += 1
                 hs = range(h, h + m)
                 cs = slice(512 * h, 512 * (h + m))
                 ys = slice(2048 * q + cs.start, 2048 * q + cs.stop)
                 yk = ["y%d_%d%d" % (t, q, k * XP // 4) for k in hs]
                 src = win.indirect(T[K("lz")][:, 128 * n + 32 * h:128 * n + 32 * (h + m)])
-                nm = "z" if two and ty != "R" else "d"
+                nm = "z" if two and ty not in "RD" else "d"
                 z, zk, rk = T["%s%d%d" % (nm, n, q)], [K("%s%d_%d" % (nm, n, k)) for k in hs], [K("r%d_%d" % (n, k)) for k in hs]
                 sc = 0.5 if two else None
-                if ty == "S":
-                    op("S", 80.0 + 512 * m * GC * CY, lambda cs=cs, src=src, z=z: [S.activation(z[:, cs], src, F.Copy)], wk + [K("lz%d" % n)], zk)
+                lk = [K("lz%d_%d" % (n, k)) for k in hs]
+                if ty in "DE":
+                    op("S", 80.0 + 512 * m * GC * CY, lambda cs=cs, src=src, z=z: [S.activation(z[:, cs], src, F.Copy, 0.0, -1.0)],
+                       wk + lk, zk)
+                    op("G", GDMA, lambda cs=cs, ys=ys, z=z: g.dma_start(z[:, cs], yb[:, ys], accum_op=A.add), zk + yk, zk, (),
+                       ACC0 + ACC1 * m, "ac%d%d%d" % (q, n, h), 16)
+                    for k in range(0, m, GV):
+                        c5 = slice(cs.start + 512 * k, cs.start + 512 * min(k + GV, m))
+                        if ty == "D":
+                            ts(r[:, c5], z[:, c5], 0.0, None, A.max, None, zk, rk[k:k + GV], c5.stop - c5.start, half=True)
+                        else:
+                            act(r[:, c5], z[:, c5], F.Abs, zk, rk[k:k + GV], c5.stop - c5.start, (), sc)
+                elif ty == "S":
+                    op("S", 80.0 + 512 * m * GC * CY, lambda cs=cs, src=src, z=z: [S.activation(z[:, cs], src, F.Copy)], wk + lk, zk)
                     for k in range(m):
                         c5 = slice(cs.start + 512 * k, cs.start + 512 * k + 512)
                         y5 = slice(ys.start + 512 * k, ys.start + 512 * k + 512)
-                        mms([(T[K("pS")][:], I(1), z[:, c5], 512), (T[K("pS")][:], I(-1), yb[:, y5], 512)], ["I1", "I-1", zk[k], yk[k]], [K("sub")], [K("pS")])
-                        act(r[:, c5], T[K("pS")][:], F.Abs, [K("sub")], [rk[k]], 512, [K("pS")], sc)
+                        subs[0] += 1
+                        other = subs[0] > TWOB and subs[0] % 2 == 0
+                        bk, ks = (K("pA"), [K("e1"), K("e0"), K("G1"), K("DT")]) if other else (K("pS"), [K("sub")])
+                        mms([(T[bk][:], I(1), z[:, c5], 512), (T[bk][:], I(-1), yb[:, y5], 512)], ["I1", "I-1", zk[k], yk[k]], ks, [bk])
+                        act(r[:, c5], T[bk][:], F.Abs, ks, [rk[k]], 512, [bk], sc)
                 else:
                     op("V", 60.0 + 512 * m * GC * CY, lambda cs=cs, ys=ys, src=src, z=z: [V.tensor_tensor(z[:, cs], src, yb[:, ys], A.subtract)],
-                       wk + yk + [K("lz%d" % n)], zk)
+                       wk + yk + lk, zk)
                     if ty == "R":
                         ts(r[:, cs], z[:, cs], 0.0, None, A.max, None, zk, rk, 512 * m, half=True)
                     else:
@@ -436,10 +561,13 @@ def rank_program(g, core, T, topo):
             if two:
                 lst += [(pZ[:, 128 * n + i:128 * n + 128:16], d[:, i:2048:16], T.seln[:], 64) for i in range(16)]
             lst += [(pZ[:, 128 * n + i:128 * n + 128:16], r[:, i:2048:16], T.sel2[:] if two else T.sel[:, 0:8], 64) for i in range(16)]
-            mms(lst, ["ones", "rowm", "sel", "sel2", "seln"] + [K("r%d_%d" % (n, s)) for s in range(4)]
-                + [K("d%d_%d" % (n, s)) for s in range(4) if two], [K("Z%d" % n)], [Z_])
+            cuts = [0] + list(range(1 + PS, len(lst), PS)) + [len(lst)]
+            for a, b in zip(cuts, cuts[1:]):
+                R = [K("d%d_%d" % (n, s)) for s in range(4) if two and a < 17] + [K("r%d_%d" % (n, s)) for s in range(4) if b > 17 or not two]
+                mms(lst[a:b], ["ones", "rowm", "sel", "sel2", "seln"] + R, [K("Z%d" % n)] if a == 0 or b == len(lst) else [], [Z_],
+                    a == 0, b == len(lst))
             tt(T[K("mz")][:, ns], pZ[:, ns], T[K("ru")][:], A.mult, [K("Z%d" % n), K("ru")], [K("mz%d" % n)], 128, [Z_])
-            mms([(pN[:, 32 + n:52:5], T[K("mz")][:, ns], T.B256[:], 64)], ["B256", K("mz%d" % n)], [K("key")], [N_], False, n == ORDER[3])
+            mms([(pN[:, 32 + n:72:5], T[K("mz")][:, ns], T.B256[:], 64)], ["B256", K("mz%d" % n)], [K("key")], [N_], False, n == ORDER[3])
 
     def fin(t, q):
         K = lambda s: "%s%d" % (s, q)
@@ -450,11 +578,10 @@ def rank_program(g, core, T, topo):
             ts(T[K("oD")][:], Dp[:], -FR, None, A.add, None, [K("Dp")], [K("oD")], 128)
             ts(T[K("oH")][:], Hh[:, 16:144], -0.5, None, A.add, None, [K("Hh")], [K("oH")], 128)
             tt(T[K("oA")][:], T.Ab[:, 4 * q:4 * q + 4], ch[:, 0:4], A.add, ["Ab", K("a")], [K("oA")], 4)
-        op("V", cyc(64), lambda: [V.tensor_tensor_scan(cf[:, 72:92], T.rs[:], pN[:, 32:52], 0.0, A.add, A.min)],
+        op("V", cyc(64), lambda: [V.tensor_tensor_scan(cf[:, 104:144], T.rs[:], pN[:, 32:72], 0.0, A.add, A.min)],
            [K("key"), "rs"], [K("sc")], [N_])
-        ts(cf[:, 96:100], cf[:, 76:92:5], M32, -M32, A.add, A.add, [K("sc")], [K("r32")], 4)
-        tt(cf[:, 92:96], cf[:, 75:92:5], cf[:, 76:92:5], A.is_gt, [K("sc")], [K("mut")], 4)
-        tt(cf[:, 100:104], cf[:, 76:92:5], cf[:, 96:100], A.subtract, [K("sc"), K("r32")], [K("df")], 4)
+        tt(cf[:, 92:96], cf[:, 107:124:5], cf[:, 108:124:5], A.is_gt, [K("sc")], [K("mut")], 4)
+        tt(cf[:, 100:104], cf[:, 108:124:5], cf[:, 128:144:5], A.subtract, [K("sc")], [K("df")], 4)
         fik = [K("f%d" % b) for b in range(4)]
         for b in range(4):
             ps = pN[:, 256 + 32 * b:288 + 32 * b]
@@ -478,32 +605,42 @@ def rank_program(g, core, T, topo):
         tt(ch[:, 0:4], ch[:, 0:4], cf[:, 92:96], A.add, [K("a"), K("mut")], [K("a")], 4)
 
     for q in range(2):
+        chunk[0] = q - LEAD
         xpart(0, q)
-    chunk[0] = 0
+    chunk[0] = 2
     konst()
+    if DIRECT < RO:
+        cp(T.Xw[:, 16384:18432], T.Xw[:, 8192:10240], X0, ["X6"], 2048, half=True)
+        cp(T.Xw[:, 18432:18560], T.Xw[:, 6144:6272], X0, ["X7"], 128, half=True)
     for k in range(6):
         a = 4096 - 2048 * (k // 2) if k % 2 == 0 else 10240 + 2048 * (k // 2)
         c = 6144 + (a - 6144) % 4096
         out, src = T.Xw[:, a:a + 2048], T.Xw[:, c:c + 2048]
         if COPY[k] == "V":
-            cp(out, src, X0, ["X%d" % k], 2048, half=True)
+            for o in range(0, 2048, CW):
+                cp(T.Xw[:, a + o:a + o + CW], T.Xw[:, c + o:c + o + CW], X0, ["X%d" % k], CW, half=True)
         elif COPY[k] == "S":
-            act(out, src, F.Copy, X0, ["X%d" % k], 2048)
+            for o in range(0, 2048, CW // 2):
+                act(T.Xw[:, a + o:a + o + CW // 2], T.Xw[:, c + o:c + o + CW // 2], F.Copy, X0, ["X%d" % k], CW // 2)
         else:
             load(out, src, "lc%d" % k, ["X%d" % k], 6000.0, X0)
     for t in range(RO):
         for q in range(2):
-            chunk[0] = q
+            chunk[0] = 2 * t + q - LEAD
             if t:
                 xpart(t, q)
             gpart(t, q)
             epart(t, q)
+            chunk[0] = 2 * t + q
             zpart(t, q)
+            chunk[0] = 2 * t + q + 2 - LEAD
             fin(t, q)
         if t < RO - 1:
             op("loc%d" % t, 0.0, None, (), ["loc%d" % t], (), 1000.0, "loc%d" % t, 16 * 2 * XP)
 
-    seq = schedule(ops)
+    if "seq" not in PLAN:
+        PLAN["seq"] = tighten(ops, schedule(ops))
+    seq = PLAN["seq"]
     SEM = {"V": "sv", "S": "ss", "P": "sp", "G": "sg"}
     ENG = {"V": g.vector, "S": g.scalar, "P": g.tensor, "G": g, "Y": g.sync}
     count = {"sv": 0, "ss": 0, "sp": 0, "sg": 0, "out": 0}

@@ -10,40 +10,58 @@ TWOB = 1
 DIRECT = 1
 PDSEP = False
 CW = 512
-L0 = 4
-XW = 18560
+SUMO = (0, 1, 2, 3)
+JOIN = (1, 0)
+EB = "SNZS"
+ETAIL = False
+PEC = 0.43
+ISSUE = 600.0
+L0 = 2
+MORE = "YYYY"
+FAR = ((2048, 18560, 0.0, 8), (0, 20576, 0.0, 8), (2048, 26720, 4096.0, 10), (0, 28768, 4096.0, 10))
+XW = 28768
 WIN = [(6144 - 2048 * n, 10240 + 2048 * n) for n in range(4)]
 FR = 613.0 + 1.0 / 32
 M4 = 1.5 * 2 ** 25
 M32 = 1.5 * 2 ** 28
 M1K = 1.5 * 2 ** 33
 M4K = 1.5 * 2 ** 35
-GV = 1
-GS = 1
-GD = 2
+LAG = 9
+UW = {"V": 512, "S": 512}
+UO = 55.0
+UMAX = 512
 XP = 4
-XT = ("VSSS", "SSSS")
-XT0 = ("SVSV", "SVSV")
-ZT = (("RRRR", "SSSS", "RRRR", "ASSS"), ("RRRR", "SSSS", "RRRR", "ASSS"))
+XT = ("VVSS", "VVSS")
+XT0 = ("SVSV", "VSVS")
+ZT = (("SSSS", "RRRR", "RRRR", "SSSS"), ("SSSS", "RRRR", "RRRR", "SSSS"))
 ORDER = (0, 1, 2, 3)
-COPY = "VVVVVV"
-FI_ON = "V"
+COPY = "SSVVVV"
+FI_ON = "S"
+OV_ON = "V"
+FL_ON = "V"
+R_ON = "V"
+RU_ON = "V"
+TH_ON = "S"
+TR_ON = "S"
+MZ_ON = "V"
 HCOPY = True
 
 SCRATCH = {"Xw": ("sbuf", [128, XW], "bfloat16"),
            "Dl": ("sbuf", [128, 256], "int32"), "Hl": ("sbuf", [128, 256], "int32"),
            "tl": ("sbuf", [128, 8], "int32"), "Al": ("sbuf", [128, 8], "int32"), "Am": ("sbuf", [128, 8], "int32"),
-           "Ab": ("sbuf", [128, 8], "float32"), "thm": ("sbuf", [128, 8], "float16")}
+           "Ab": ("sbuf", [128, 8], "float32"), "thm": ("sbuf", [128, 24], "bfloat16"),
+           "thf": ("sbuf", [128, 16], "float32")}
 for _t in range(3):
     SCRATCH["x%d" % _t] = ("sbuf", [128, 4096], "bfloat16")
 for _t in range(RO):
     SCRATCH["y%d" % _t] = ("sbuf", [128, 4096], "bfloat16")
-for _n in ("ones", "Bt", "Bb", "Ss", "V1", "Tri", "nSl", "Bi", "Bp", "Ce", "Cg"):
+for _n in ("ones", "Bt", "Bb", "Ss", "V1", "Tri", "nSl", "Bi", "Bp", "Ce", "Cg", "rowp"):
     SCRATCH[_n] = ("sbuf", [128, 128], "bfloat16")
-IS = {1: 0, -1: 1, 2: 2, 1024: 3, 4: 4, -4: 5, 128: 6, 112: 7}
+SCRATCH["bias"] = ("sbuf", [128, 4], "float32")
+IS = {1: 0, -1: 1, 2: 2, 1024: 3, 4: 4, -4: 5, 128: 6, 112: 7, 4096: 8, 16: 9}
 SCRATCH["Is"] = ("sbuf", [128, 128 * len(IS)], "bfloat16")
 SCRATCH["nTri"] = ("sbuf", [128, 128], "bfloat16")
-for _n in ("nIh", "Bh", "Bih", "Be", "Bg", "oneh", "rowp"):
+for _n in ("nIh", "Bh", "Be", "Bg"):
     SCRATCH[_n] = ("sbuf", [128, 128], "float16")
 SCRATCH["I4"] = ("sbuf", [128, 384], "float16")
 SCRATCH["B256"] = ("sbuf", [128, 8], "float16")
@@ -51,7 +69,7 @@ SCRATCH["Bd"] = ("sbuf", [128, 8], "float32")
 SCRATCH["sel"] = ("sbuf", [128, 16], "bfloat16")
 for _n in ("selt", "sel2", "seln"):
     SCRATCH[_n] = ("sbuf", [128, 8], "bfloat16")
-SCRATCH["rowm"] = ("sbuf", [128, 128], "bfloat16")
+SCRATCH["rowm"] = ("sbuf", [128, 256], "bfloat16")
 SCRATCH["rowk"] = ("sbuf", [128, 60], "bfloat16")
 SCRATCH["rs"] = ("sbuf", [128, 40], "float32")
 SCRATCH["If"] = ("sbuf", [128, 128], "float32")
@@ -62,32 +80,48 @@ for _q in range(2):
         if set(ZT[_q][_n]) & set("RD") and set(ZT[_q][_n]) - set("RD"):
             SCRATCH["z%d%d" % (_n, _q)] = ("sbuf", [128, 2048], "bfloat16")
     for _n, _w, _d in (("ab", 2048, "bfloat16"), ("Dp", 128, "float32"), ("Hh", 144, "bfloat16"), ("fl", 128, "bfloat16"),
-                       ("TR", 256, "float16"), ("ov", 128, "bfloat16"), ("fi", 128, "bfloat16"), ("PG", 128, "float16"),
+                       ("TR", 256, "bfloat16"), ("ov", 128, "bfloat16"), ("fi", 128, "bfloat16"), ("PG", 128, "float16"),
                        ("Pe", 128, "float16"), ("Pd", 128, "float32"), ("ru", 128, "bfloat16"), ("mo", 128, "float16"),
                        ("mz", 512, "float16"), ("pr", 128, "float32"), ("lz", 512, "uint16"), ("lx", 128, "uint16"),
                        ("ah", 128, "float16"), ("rp", 128, "float16"), ("xi", 128, "int32"), ("cf", 144, "float32"), ("cb", 80, "bfloat16"),
-                       ("ch", 8, "float16"), ("oD", 128, "float32"), ("oH", 128, "float32"), ("oA", 4, "float32")):
+                       ("ch", 8, "bfloat16"), ("oD", 128, "float32"), ("oH", 128, "float32"), ("oA", 4, "float32")):
         SCRATCH["%s%d" % (_n, _q)] = ("sbuf", [128, _w], _d)
     for _n in ("pA", "pZ", "pN", "pS"):
         SCRATCH["%s%d" % (_n, _q)] = ("psum", [128, 512], "float32")
 
-SEMAPHORES = ["sv", "ss", "sp", "sg", "out", "ldD", "ldH", "ldt", "ldA", "lxa", "lxb"]
-SEMAPHORES += ["lc%d" % k for k in range(6)] + ["loc%d" % t for t in range(RO)]
+SEMAPHORES = ["sv", "ss", "sp", "sg", "out", "ldD", "ldH", "ldE", "ldI", "ldt", "ldA", "lxa", "lxb"]
+SEMAPHORES += ["lb%d" % k for k in range(6)] + ["lc%d" % k for k in range(4)] + ["loc%d" % t for t in range(RO)]
 SEMAPHORES += ["ar%d%d%d" % (t, q, h) for t in range(RO) for q in range(2) for h in range(XP)]
-SEMAPHORES += ["ac%d%d%d" % (q, n, h) for q in range(2) for n in range(4) for h in range(4) if ZT[q][n][h] in "DE"]
+SEMAPHORES += ["ac%d%d%d" % (q, n, h) for q in range(2) for n in range(4) for h in range(4) if ZT[q][n][h] == "D"]
 
+GD = 2
 GDMA = 1000.0
-ACC0 = 2000.0
-ACC1 = 1300.0
-CY = 0.9
+DMA = 600.0
+ACC = 2000.0
+CY = 0.86
 GC = 1.56
-HOP = 250.0
-OWN = 250.0
+HOP = 230.0
+OWN = 230.0
 ARR = 3200.0
-PASSES = 4
+XLAT = 7000.0
+PASSES = 2
 LEAD = 1.5
+LATE = -0.5
+LOADS = (0, 1, 2, 3, 4, 5, 6, 7)
+CPL = 1300.0
+CPH = 1
+ZL = None
+FEW = 1
+FROM = 1
+BEAT = ("pr3 -mz2 -mz3 ru lz0_2 -sc lz1_0 -mut mo -df -f0 -f1 -f2 -f3 -m0 -m1 -m2 -m3 -Dp -m -a +xi +xi' lz2_0 +lx flg +x0 +x1 d1_0 lz3_0 +fl d1_1 +Z2 d1_2 r1_0 +ah d2_0 r1_1 d1_3 mz0 d2_1 r1_2 r1_3 d2_2 +ov d2_3 mz1 r2_1 +Pe +PG +Pd r2_0 r2_2 +rnd r2_3 +rem +dd +lz0_0 +lz0_1 +pr1 +pr2 +pr0", "d0_0 d0_1 d0_2 r0_0 d0_3 +Hh +w r0_1 +x2 +TR +x3 r0_2 r0_3 d3_0 d3_1 d3_2 +ab0 +ab2 +ab1 +ab3 d3_3 r3_0 r3_1 +fi r3_2 r3_3")
+LOOK = 500.0
+TOL = 50.0
+WAIT = 0.0
+NOISE = 0.0
+SEED = 1
+SERIAL = False
 BIAS = 1000000.0
-SLACK = 150.0
+SLACK = 100.0
 
 
 def schedule(ops):
@@ -100,9 +134,11 @@ def schedule(ops):
     for i in range(n - 1, -1, -1):
         prio[i] = ops[i]["cost"] + ops[i]["lat"] + max([prio[j] + HOP for j in succ[i]], default=0.0)
     for i in range(n):
-        prio[i] -= BIAS * ops[i]["ch"]
+        prio[i] -= BIAS * ops[i]["ch"] + NOISE * ((i * SEED * 0.6180339887) % 1.0)
     for i in range(n - 1, -1, -1):
         prio[i] = max([prio[i]] + [prio[j] + 1.0 for j in succ[i]])
+    if SERIAL:
+        return sorted(range(n), key=lambda i: -prio[i])
     left = [len(o["hard"] | o["order"]) for o in ops]
     ready = [0.0] * n
     avail = {}
@@ -119,6 +155,21 @@ def schedule(ops):
             av = avail.get(q, 0.0)
             m = min(max(av, ready[i]) for i in lst)
             c = max((i for i in lst if max(av, ready[i]) <= m + SLACK), key=lambda i: prio[i])
+            if q in ("V", "S"):
+                soon = [(ready[i], i) for i in lst if m + SLACK < ready[i] <= m + LOOK and prio[i] > prio[c] + BIAS / 4]
+                far = []
+                for k in pend.get("P", ()):
+                    e = max(avail.get("P", 0.0), ready[k]) + ops[k]["cost"] + HOP
+                    far += [e for j in succ[k] if ops[j]["q"] == q and left[j] == 1 and m < e <= m + LOOK and prio[j] > prio[c] + BIAS / 4]
+                if soon or far:
+                    when = min([x[0] for x in soon] + far)
+                    fit = [i for i in lst if max(av, ready[i]) + ops[i]["cost"] <= when + TOL]
+                    if fit:
+                        c = max(fit, key=lambda i: prio[i])
+                    elif soon and min(soon)[0] == when:
+                        c = min(soon)[1]
+                    elif when - m <= WAIT and pend.get("P"):
+                        continue
             st = max(av, ready[c])
             if best is None or st < best[0]:
                 best = (st, c)
@@ -215,6 +266,10 @@ def rank_program(g, core, T, topo):
     ops = []
     lastw, readers, bankacc = {}, {}, {}
     chunk = [0]
+    sent = [0]
+    left = [0] * RO
+    named = {}
+    where = [None, "start", 0]
 
     def op(q, cost, fn, R=(), W=(), banks=(), lat=0.0, sem=None, inc=1):
         i = len(ops)
@@ -240,7 +295,15 @@ def rank_program(g, core, T, topo):
             lastw[k] = i
             readers[k] = []
         hard.discard(i)
-        ops.append({"q": q, "cost": cost, "fn": fn, "hard": hard, "order": order - hard, "lat": lat, "sem": sem, "inc": inc, "ch": chunk[0]})
+        ops.append({"q": q, "cost": cost, "fn": fn, "hard": hard, "order": order - hard, "lat": lat, "sem": sem, "inc": inc, "ch": chunk[0],
+                    "at": tuple(where)})
+        where[2] += 1
+        if q in ("V", "S") and where[0] is not None:
+            nm = W[0]
+            nm = "x" + nm[-1] if nm[0] == "x" and "_" in nm else (nm[:-3] if nm.endswith("u0") else nm[:-1])
+            while (where[0], nm) in named:
+                nm += "'"
+            named[where[0], nm] = i
         return i
 
     V, S, P = g.vector, g.scalar, g.tensor
@@ -271,7 +334,20 @@ def rank_program(g, core, T, topo):
     def mms(lst, R, W, banks, start=True, stop=True):
         def f():
             return [P.matmul(o, l, r, start and i == 0, stop and i == len(lst) - 1) for i, (o, l, r, c) in enumerate(lst)]
-        op("P", sum(x[3] for x in lst) * 0.417 * 1.2 + 5.0 * len(lst), f, R, W, banks)
+        i = op("P", sum(x[3] for x in lst) * PEC, f, R, W, banks)
+        if not start:
+            same = {j for j in ops[i]["hard"] if ops[j]["q"] == "P"}
+            ops[i]["hard"] -= same
+            ops[i]["order"] |= same
+
+    def gather(q, run, lo, hi, make, R, W):
+        for k, a in enumerate(range(lo, hi, UW[q])):
+            i = op(q, UO + UW[q] * GC * CY, None, R, [w + "u%d" % k for w in W])
+            ops[i]["run"] = (run, a, a + UW[q], make)
+            if run in lastw:
+                ops[i]["order"].add(lastw[run])
+            lastw[run] = i
+        return [w + "u%d" % k for w in W for k in range((hi - lo) // UW[q])]
 
     def load(out, in_, sem, W, lat, R=()):
         return op("Y", 60.0, lambda: g.sync.dma_start(out, in_), R, W, (), lat, sem, 16)
@@ -279,18 +355,26 @@ def rank_program(g, core, T, topo):
     def fill(ap, val, W, n=64):
         op("V", cyc(n), lambda: [V.memset(ap, val)], (), W)
 
+    def sfill(ap, like, val, W):
+        act(ap, like, F.Copy, ["ones"], W, 64, (), val)
+
     def sel(out, in_, pat, cmp, base, cm, R, W, n):
         op("G", 200.0 + 2 * n * CY, lambda: [g.affine_select(out, in_, pat, cmp, 0.0, base, cm)], R, W)
 
     def I(k):
         return T.Is[:, 128 * IS[k]:128 * IS[k] + 128]
 
-    loads = [load(T.Dl[:], T.D[:], "ldD", ["Dl"], 2700.0),
-             load(T.Hl[:], T.H[:], "ldH", ["Hl"], 3300.0),
-             load(T.Xw[:, 6451:10240], T.X[:, 0:3789], "lxa", ["Xa"], 8000.0),
-             load(T.Xw[:, 6144:6451], T.X[:, 3789:4096], "lxb", ["Xb"], 8000.0),
-             load(T.tl[:], T.th[:], "ldt", ["tl"], 8000.0),
-             load(T.Al[:], T.A[:], "ldA", ["Al"], 8000.0)]
+    loads = [load(T.Dl[:, 0:128], T.D[:, 0:128], "ldD", ["Dl0"], 2400.0),
+             load(T.Hl[:, 0:128], T.H[:, 0:128], "ldH", ["Hl0"], 2700.0),
+             load(T.Xw[:, 6451:10240], T.X[:, 0:3789], "lxa", ["Xa"], XLAT),
+             load(T.Xw[:, 6144:6451], T.X[:, 3789:4096], "lxb", ["Xb"], XLAT),
+             load(T.Dl[:, 128:256], T.D[:, 128:256], "ldE", ["Dl1"], XLAT + 300.0),
+             load(T.Hl[:, 128:256], T.H[:, 128:256], "ldI", ["Hl1"], XLAT + 600.0),
+             load(T.tl[:], T.th[:], "ldt", ["tl"], XLAT + 600.0),
+             load(T.Al[:], T.A[:], "ldA", ["Al"], XLAT + 600.0)]
+    loads = [loads[k] for k in LOADS]
+    for k, i in enumerate(loads):
+        ops[i]["lat"] = 2400.0 + 300.0 * k if k < LOADS.index(2) else XLAT + 200.0 * k
     for a, b in zip(loads, loads[1:]):
         ops[b]["order"].add(a)
     X0 = ["Xa", "Xb"]
@@ -302,8 +386,10 @@ def rank_program(g, core, T, topo):
     sel(T.Bt[:], T.ones[:], [[-32, 4], [0, 32]], A.is_ge, 0, 1, ["ones"], ["Bt"], 128)
     sel(T.Bb[:], T.Bt[:], [[32, 4], [0, 32]], A.is_ge, 31, -1, ["Bt"], ["Bb"], 128)
     sel(T.Ss[:], T.Bb[:], [[1, 128]], A.is_ge, -1, -1, ["Bb"], ["Ss"], 128)
-    sel(T.Bt[:], T.ones[:], [[1, 128]], A.is_ge, 0, -32, ["ones"], ["Bt"], 128)
-    sel(T.Bi[:], T.Bt[:], [[-1, 128]], A.is_ge, 31, 32, ["Bt"], ["Bi"], 128)
+    sel(T.Bi[:], T.ones[:], [[-1, 4], [0, 32]], A.not_equal, 0, 1, ["ones"], ["Bi"], 128)
+    sel(T.Bi[:], T.Bi[:], [[-1, 4], [0, 32]], A.not_equal, -4, 1, ["Bi"], ["Bi"], 128)
+    sel(T.Bi[:], T.Bi[:], [[-1, 4], [0, 32]], A.not_equal, -8, 1, ["Bi"], ["Bi"], 128)
+    ts(T.Bi[:], T.Bi[:], -1.0, 1.0, A.mult, A.add, ["Bi"], ["Bi"], 128, half=True)
     for c0, rep, w in ((0, 3, 5), (60, 2, 1), (68, 3, 5)):
         cs = slice(c0, c0 + 4 * rep * w)
         sel(T.Bt[:, cs], T.ones[:, cs], [[0, rep], [-32, 4], [0, w]], A.is_ge, 0, 1, ["ones"], ["Bt"], 64)
@@ -311,12 +397,12 @@ def rank_program(g, core, T, topo):
 
     for q in range(2):
         c0 = slice(128 * q, 128 * q + 128)
-        ts(T["Dp%d" % q][:], T.Dl[:, c0], FR, None, A.add, None, ["Dl"], ["Dp%d" % q], 128)
-        ts(T["Hh%d" % q][:, 16:144], T.Hl[:, c0], 0.5, None, A.add, None, ["Hl"], ["Hh%d" % q], 128)
+        ts(T["Dp%d" % q][:], T.Dl[:, c0], FR, None, A.add, None, ["Dl%d" % q], ["Dp%d" % q], 128)
+        ts(T["Hh%d" % q][:, 16:144], T.Hl[:, c0], 0.5, None, A.add, None, ["Hl%d" % q], ["Hh%d" % q], 128)
 
     def konst():
         for k in IS:
-            if k != 1:
+            if k != 1 and (k != 4096 or MZ_ON == "S"):
                 ts(I(k), I(1), float(k), None, A.mult, None, ["I1"], ["I%d" % k], 128, half=True)
         ts(T.nIh[:], I(1), -1.0, None, A.mult, None, ["I1"], ["nIh"], 128, half=True)
         cp(T.If[:], I(1), ["I1"], ["If"], 128)
@@ -326,49 +412,65 @@ def rank_program(g, core, T, topo):
         ts(T.sel2[:], T.sel[:, 0:8], 2.0, None, A.mult, None, ["sel"], ["sel2"], 8)
         ts(T.seln[:], T.sel[:, 0:8], -1.0, None, A.mult, None, ["sel"], ["seln"], 8)
         tt(T.V1[:], I(1), T.Ss[:], A.subtract, ["I1", "Ss"], ["V1"], 128)
+        ts(T.V1[:], T.V1[:], 0.5, None, A.mult, None, ["V1"], ["V1"], 128, half=True)
+        fill(T.bias[:, 0:1], -2040.5, ["bias"])
+        fill(T.bias[:, 1:2], -31.5, ["bias"])
+        fill(T.bias[:, 2:3], M1K, ["bias"])
+        fill(T.bias[:, 3:4], -M1K, ["bias"])
+        for o in (0, 4) if MZ_ON == "S" else ():
+            fill(T.rowb[0:1, :], -4096.0, ["rowb"])
+            ts(T.B256f[:, o:o + 4], T.Bb[:, 0:128:32], 256.0, None, A.mult, None, ["Bb"], ["B256f"], 4)
+            ts(T.Bneg[:, o:o + 4], T.Bb[:, 0:128:32], -2040.0 * 256, None, A.mult, None, ["Bb"], ["Bneg"], 4)
         tt(T.Tri[:], I(1), T.Ss[:], A.add, ["I1", "Ss"], ["Tri"], 128)
         tt(T.nSl[:], T.Tri[:], T.Bb[:], A.subtract, ["Tri", "Bb"], ["nSl"], 128)
         ts(T.nTri[:], T.Tri[:], -16.0, None, A.mult, None, ["Tri"], ["nTri"], 128, half=True)
         ts(T.Tri[:], T.Tri[:], 16.0, None, A.mult, None, ["Tri"], ["Tri"], 128, half=True)
         cp(T.Bh[:], T.Bb[:], ["Bb"], ["Bh"], 128, half=True)
-        cp(T.Bih[:], T.Bi[:], ["Bi"], ["Bih"], 128, half=True)
         ts(T.B256[:, 0:4], T.Bb[:, 0:128:32], 256.0, None, A.mult, None, ["Bb"], ["B256"], 4)
         ts(T.B256[:, 4:8], T.Bb[:, 0:128:32], 256.0, None, A.mult, None, ["Bb"], ["B256"], 4)
         ts(T.Bd[:, 0:4], T.Bb[:, 0:128:32], 13.0 / 1024, None, A.mult, None, ["Bb"], ["Bd0"], 4)
         ts(T.Bd[:, 4:8], T.Bb[:, 0:128:32], 12.0 / 1024, None, A.mult, None, ["Bb"], ["Bd1"], 4)
-        fill(T.Ce[:], 1.0, ["Ce"])
-        fill(T.Ce[:, 60:68], 1.0 / 1024, ["Ce"])
-        fill(T.Cg[:], 0.0, ["Cg"])
-        fill(T.rowp[0:2, :], 0.0, ["rowp"])
+        def cols(buf, rows, cs, v):
+            sfill(T[buf][rows, cs], T.ones[rows, cs], v, [buf])
+        every, first, both = slice(0, 128), slice(0, 1), slice(0, 2)
+        cols("Ce", every, every, 1.0)
+        cols("Cg", every, every, 0.0)
+        cols("rowp", both, every, 0.0)
+        cols("Ce", every, slice(60, 68), 1.0 / 1024)
         for c in (0, 68):
-            fill(T.Ce[:, c + 24:c + 40:5], 0.0, ["Ce"])
-            fill(T.Ce[:, c + 40:c + 60], 0.0, ["Ce"])
-            fill(T.Cg[:, c:c + 20], 1.0, ["Cg"])
-            fill(T.Cg[:, c + 40:c + 60], 0.25, ["Cg"])
-            fill(T.Cg[:, c + 4:c + 60:5], 0.0, ["Cg"])
-            fill(T.Cg[:, c + 24:c + 40:5], -0.25, ["Cg"])
+            cols("Ce", every, slice(c + 24, c + 40, 5), 0.0)
+            cols("Ce", every, slice(c + 40, c + 60), 0.0)
+            cols("Cg", every, slice(c, c + 20), 1.0)
+            cols("Cg", every, slice(c + 40, c + 60), 0.25)
+            cols("Cg", every, slice(c + 4, c + 60, 5), 0.0)
+            cols("Cg", every, slice(c + 24, c + 40, 5), -0.25)
         Bp = ["Bp0", "Bp60", "Bp68"]
         tt(T.Be[:], T.Bp[:], T.Ce[:], A.mult, Bp + ["Ce"], ["Be"], 128)
         tt(T.Bg[:], T.Bp[:], T.Cg[:], A.mult, Bp + ["Cg"], ["Bg"], 128)
-        fill(T.rowp[0:2, 64:68], 3.625 / 1024, ["rowp"])
+        cols("rowp", both, slice(64, 68), 11.625 / 1024)
         for cs, v in ((slice(0, 20), -1.0), (slice(20, 40), -1.5), (slice(40, 60), -1.9375), (slice(4, 20, 5), -1.5),
                       (slice(24, 40, 5), 1.9375), (slice(44, 60, 5), 0.0), (slice(60, 64), 215.0 / 1024),
-                      (slice(64, 68), 2872.0 / 1024), (slice(68, 88), 1.0), (slice(72, 88, 5), 0.0)):
-            fill(T.rowp[0:1, cs], v, ["rowp"])
-        fill(T.oneh[0:2, :], 1.0, ["oneh"])
+                      (slice(64, 68), 2864.0 / 1024), (slice(68, 88), 1.0), (slice(72, 88, 5), 0.0)):
+            cols("rowp", first, cs, v)
         fill(T.rowm[0:1, :], -2040.0, ["rowm"])
         for n in range(5):
-            fill(T.rowk[0:1, n:20:5], 0.5 - 4 * (n + 1) if n < 4 else 0.0, ["rowk"])
-            fill(T.rowk[0:1, 20 + n:40:5], 32.0 + 36 * n if n < 4 else 1.0, ["rowk"])
-            fill(T.rowk[0:1, 40 + n:60:5], 32.0 + 32 * n if n < 4 else 0.0, ["rowk"])
+            cols("rowk", first, slice(n, 20, 5), 0.5 - 4 * (n + 1) if n < 4 else 0.0)
+            cols("rowk", first, slice(20 + n, 40, 5), 32.0 + 36 * n if n < 4 else 1.0)
+            cols("rowk", first, slice(40 + n, 60, 5), 32.0 + 32 * n if n < 4 else 0.0)
         fill(T.rs[:], 0.0, ["rs"])
         fill(T.rs[:, 0:40:5], 1e9, ["rs"])
-        ts(T.thm[:], T.tl[:], -2040.0, None, A.add, None, ["tl"], ["thm"], 8)
+        ts(T.thf[:, 0:8], T.tl[:], -1.0, 2056.0 if TH_ON == "S" else 2040.0, A.mult, A.add, ["tl"], ["thf"], 8)
+        ts(T.thf[:, 8:16], T.thf[:, 0:8], M32, -M32, A.add, A.add, ["thf"], ["thg"], 8)
+        fill(T.thm[:], 0.0, ["thm"])
+        for q in range(2):
+            cp(T.thm[:, 12 * q + 4:12 * q + 8], T.thf[:, 8 + 4 * q:12 + 4 * q], ["thg"], ["thm"], 4)
+            tt(T.thm[:, 12 * q + 8:12 * q + 12], T.thf[:, 4 * q:4 * q + 4], T.thf[:, 8 + 4 * q:12 + 4 * q], A.subtract, ["thf", "thg"], ["thm"], 4)
         ts(T.Am[:], T.Al[:], 31, None, A.bitwise_and, None, ["Al"], ["Am"], 8)
         tt(T.Ab[:], T.Al[:], T.Am[:], A.subtract, ["Al", "Am"], ["Ab"], 8)
         for q in range(2):
             cp(T["ch%d" % q][:, 0:4], T.Am[:, 4 * q:4 * q + 4], ["Am"], ["a%d" % q], 4)
             fill(T["Hh%d" % q][:, 0:16], 0.0, ["H0%d" % q])
+            fill(T["TR%d" % q][0:12, 128:256], 0.0, ["TRc%d" % q])
             fill(T["TR%d" % q][0:4, 128:256], -2040.0, ["TRc%d" % q])
             for n in range(4):
                 if "z%d%d" % (n, q) in SCRATCH:
@@ -399,24 +501,44 @@ def rank_program(g, core, T, topo):
             else:
                 op("S", 80.0 + w * GC * CY, lambda src=src, cs=cs: [S.activation(T[xb][:, cs], src, F.Copy)], R, W)
             ar = "ar%d%d%d" % (t, q, h)
-            i = op("G", 900.0, lambda cs=cs, ar=ar: g.remote_dma(T["y%d" % t][:, cs], T[xb][:, cs], T.sem[ar], T.sem["loc%d" % t],
-                                                                  pid, rid, topo.mask(core, dst)),
+            eng = topo.engines(core, dst)[::FEW if (t, q) == (0, 0) else 1]
+            left[t] += len(eng)
+            i = op("G", ISSUE, lambda cs=cs, ar=ar, eng=eng: g.remote_dma(T["y%d" % t][:, cs], T[xb][:, cs], T.sem[ar], T.sem["loc%d" % t],
+                                                                           pid, rid, sum(1 << e for e in eng)),
                    ["%s_%d%d" % (xb, q, h)], [], (), 0.0, None, 0)
-            a = op("arr%s" % ar, 0.0, None, (), ["y%d_%d%d" % (t, q, h)], (), ARR, ar, len(topo.engines(core, dst)))
-            ops[a]["order"].add(i)
+            a = op("D", DMA, None, (), ["y%d_%d%d" % (t, q, h)], (), ARR - ISSUE - DMA - HOP, ar, len(eng))
+            ops[a]["hard"].add(i)
+            sent[0] = i
 
     def gpart(t, q):
         K = lambda s: "%s%d" % (s, q)
         pA, pZ, A_, Z_ = T[K("pA")], T[K("pZ")], K("pA"), K("pZ")
         Hh, ch = T[K("Hh")], T[K("ch")]
-        ts(ch[:, 4:8], ch[:, 0:4], 31.5, -32.0, A.is_gt, A.mult, [K("a")], [K("w")], 4)
-        mms([(pZ[0:4, 128:256], T.thm[:, 4 * q:4 * q + 4], T.nIh[:], 128), (pZ[0:4, 128:256], ch[:, 0:4], T.nIh[:], 128),
-             (pZ[0:4, 128:256], ch[:, 4:8], T.nIh[:], 128)], ["thm", "nIh", K("a"), K("w")], [K("Z1")], [Z_])
+        if t == 0:
+            mms([(pZ[0:12, 384:512], T.thm[:, 12 * q:12 * q + 12], I(1), 128)], ["thm", "I1"], [K("Z3")], [Z_])
+            cp(T[K("TR")][0:12, 0:128], pZ[0:12, 384:512], [K("Z3")], [K("TR")], 128, [Z_])
+        if TH_ON == "S":
+            op("S", cyc(64), lambda: [S.activation(ch[:, 4:8], ch[:, 0:4], F.Sign, T.bias[:, 1:2])], [K("a"), "bias"], [K("w")])
+        else:
+            ts(ch[:, 4:8], ch[:, 0:4], 31.5, 2.0, A.is_gt, A.mult, [K("a")], [K("w")], 4)
+        mms([(pZ[0:4, 128:256], ch[:, 0:4], I(-1), 128), (pZ[0:4, 128:256], ch[:, 4:8], I(16), 128)],
+            ["I-1", "I16", K("a"), K("w")], [K("Z1")], [Z_])
         mms([(pZ[:, 0:128], Hh[:, 16:144], I(1), 128), (pZ[:, 0:128], Hh[:, 15:143], I(-1), 128)],
             ["I1", "I-1", K("Hh"), K("H0")], [K("Z0")], [Z_])
-        cp(T[K("TR")][0:4, 0:128], pZ[0:4, 128:256], [K("Z1")], [K("TR")], 128, [Z_])
-        ts(T[K("fl")][:], pZ[:, 0:128], 0.0, None, A.not_equal, None, [K("Z0")], [K("fl")], 128, [Z_])
-        ts(pZ[:, 256:384], T[K("Dp")][:], M1K, -M1K, A.add, A.add, [K("Dp")], [K("Z2")], 128, [Z_])
+        if TR_ON == "S":
+            act(T[K("TR")][0:4, 0:128], pZ[0:4, 128:256], F.Copy, [K("Z1")], [K("TR")], 128, [Z_])
+        else:
+            cp(T[K("TR")][0:4, 0:128], pZ[0:4, 128:256], [K("Z1")], [K("TR")], 128, [Z_])
+        if FL_ON == "S":
+            act(T[K("fs")][:], pZ[:, 0:128], F.Sign, [K("Z0")], [K("fs")], 128, [Z_])
+            act(T[K("fl")][:], T[K("fs")][:], F.Abs, [K("fs")], [K("fl")], 128)
+        else:
+            ts(T[K("fl")][:], pZ[:, 0:128], 0.0, None, A.not_equal, None, [K("Z0")], [K("fl")], 128, [Z_])
+        if R_ON == "S":
+            op("S", cyc(128), lambda: [S.activation(T[K("rm")][:], T[K("Dp")][:], F.Identity, T.bias[:, 2:3])], [K("Dp"), "bias"], [K("rm")])
+            op("S", cyc(128), lambda: [S.activation(pZ[:, 256:384], T[K("rm")][:], F.Identity, T.bias[:, 3:4])], [K("rm"), "bias"], [K("Z2")], [Z_])
+        else:
+            ts(pZ[:, 256:384], T[K("Dp")][:], M1K, -M1K, A.add, A.add, [K("Dp")], [K("Z2")], 128, [Z_])
         tt(T[K("ah")][:], T[K("Dp")][:], pZ[:, 256:384], A.subtract, [K("Dp"), K("Z2")], [K("ah")], 128, [Z_])
         mms([(pA[:, 384:512], T[K("Dp")][:], T.If[:], 512)], [K("Dp"), "If"], [K("DT")], [A_])
         mms([(pA[:, 256:384], Hh[:, 16:144], I(1), 128), (pA[:, 256:384], T.Tri[:], T[K("fl")][:], 128)],
@@ -431,16 +553,26 @@ def rank_program(g, core, T, topo):
         for s in range(4):
             cs = slice(2048 * q + 512 * s, 2048 * q + 512 * s + 512)
             h = s * XP // 4
-            bk = K("pS") if s % 2 == 0 else N_
-            ks = NK if s % 2 else [K("sub")]
+            bk = K("p" + EB[s])
+            ks = {"S": [K("sub")], "N": NK, "Z": [K("Z%d" % k) for k in range(4)]}[EB[s]]
             mms([(T[bk][:], I(1), xb[:, cs], 512), (T[bk][:], I(-1), yb[:, cs], 512)],
                 ["I1", "I-1", "x%d_%d%d" % (t % 3, q, h), "y%d_%d%d" % (t, q, h)], ks, [bk])
             act(ab[:, 512 * s:512 * s + 512], T[bk][:], F.Abs, ks, [K("ab%d" % s)], 512, [bk])
-        mms([(pA[:, 0:256], T.Bih[0:4, :], T[K("TR")][0:4, :], 256)], ["Bih", K("TR"), K("TRc")], [K("e1"), K("e0")], [A_], True, False)
-        mms([(pA[:, i:256:16], ab[:, i:2048:16], T.sel[:], 64) for i in range(16)],
-            ["sel", "selb"] + [K("ab%d" % s) for s in range(4)], [K("e1"), K("e0")], [A_], False, True)
-        ts(T[K("ov")][:], pA[:, 0:128], 2040.0, None, A.is_gt, None, [K("e1")], [K("ov")], 128, [A_])
-        mms([(pA[:, 0:128], T.V1[:], T[K("ov")][:], 128)], ["V1", K("ov")], [K("e1")], [A_])
+        mms([(pA[:, 0:256], T.Bi[0:12, :], T[K("TR")][0:12, :], 256)], ["Bi", K("TR"), K("TRc")], [K("e1"), K("e0")], [A_], True, False)
+        if ETAIL:
+            mms([(pA[0:96, i:256:16], ab[:, i:1536:16], T.sel[:], 64) for i in range(16)],
+                ["sel", "selb"] + [K("ab%d" % s) for s in range(3)], [], [A_], False, False)
+            mms([(pA[96:128, i:256:16], ab[:, 1536 + i:2048:16], T.sel[:], 32) for i in range(16)],
+                ["sel", "selb", K("ab3")], [K("e1"), K("e0")], [A_], False, True)
+        else:
+            mms([(pA[:, i:256:16], ab[:, i:2048:16], T.sel[:], 64) for i in range(16)],
+                ["sel", "selb"] + [K("ab%d" % s) for s in range(4)], [K("e1"), K("e0")], [A_], False, True)
+        if OV_ON == "V":
+            ts(T[K("ov")][:], pA[:, 0:128], 2040.0, 2.0, A.is_gt, A.mult, [K("e1")], [K("ov")], 128, [A_])
+            mms([(pA[:, 0:128], T.V1[:], T[K("ov")][:], 128)], ["V1", K("ov")], [K("e1")], [A_])
+        else:
+            op("S", cyc(128), lambda: [S.activation(T[K("ov")][:], pA[:, 0:128], F.Sign, T.bias[:, 0:1])], [K("e1"), "bias"], [K("ov")], [A_])
+            mms([(pA[:, 0:128], T.V1[:], T.ones[:], 128), (pA[:, 0:128], T.V1[:], T[K("ov")][:], 128)], ["V1", "ones", K("ov")], [K("e1")], [A_])
         if FI_ON == "V":
             ts(T[K("fi")][:], pA[:, 0:128], 0.0, None, A.max, None, [K("e1")], [K("fi")], 128, [A_])
         else:
@@ -449,7 +581,7 @@ def rank_program(g, core, T, topo):
         tt(T[K("PG")][:], pA[:, 256:384], T[K("fi")][:], A.mult, [K("G1"), K("fi")], [K("PG")], 128, [A_])
         if not PDSEP:
             tt(T[K("Pd")][:], pA[:, 384:512], T[K("fi")][:], A.mult, [K("DT"), K("fi")], [K("Pd")], 128, [A_])
-        mms([(pN[:, 384:512], T.oneh[0:2, :], T.rowp[0:2, :], 128)], ["oneh", "rowp"], [K("pk")], [N_], True, False)
+        mms([(pN[:, 384:512], T.ones[0:2, :], T.rowp[0:2, :], 128)], ["ones", "rowp"], [K("pk")], [N_], True, False)
         mms([(pN[:, 384:512], T[K("Pe")][:], T.Be[:], 128)], [K("Pe"), "Be"], [], [N_], False, False)
         mms([(pN[:, 384:512], T[K("PG")][:], T.Bg[:], 128)], [K("PG"), "Bg"], [K("pk")], [N_], False, PDSEP)
         if not PDSEP:
@@ -463,7 +595,9 @@ def rank_program(g, core, T, topo):
         for b in range(4):
             bs = slice(32 * b, 32 * b + 32)
             ts(T[K("pr")][:, bs], T[K("Dp")][:, bs], cb[:, 5 * b:5 * b + 1], 2048.5, A.mult, A.add, [K("Dp"), K("rem")], [prk[b]], 32)
-        ts(T[K("rp")][:], T[K("pr")][:], M4K, -M4K - 8192.0, A.add, A.add, prk, [K("rp")], 128)
+        near = t < DIRECT
+        if near:
+            ts(T[K("rp")][:], T[K("pr")][:], M4K, -M4K - 8192.0, A.add, A.add, prk, [K("rp")], 128)
         for n in ORDER:
             ns = slice(128 * n, 128 * n + 128)
             if n == 0 and t >= DIRECT:
@@ -471,25 +605,29 @@ def rank_program(g, core, T, topo):
                     ts(T[K("lz")][:, 32 * L0:128], T[K("pr")][:, 32 * L0:128], -2048.5, None, A.add, None, prk,
                        [K("lz0_%d" % b) for b in range(L0, 4)], 128 - 32 * L0)
                 continue
-            mms([(pZ[:, ns], T.If[:], T[K("pr")][:], 512), (pZ[:, ns], T.nIh[:], T[K("rp")][:], 128)]
+            mms([(pZ[:, ns], T.If[:], T[K("pr")][:], 512)] + ([(pZ[:, ns], T.nIh[:], T[K("rp")][:], 128)] if near else [])
                 + ([(pZ[:, ns], T.I4[:, 128 * n - 128:128 * n], T[K("ah")][:], 128)] if n else []),
-                [K("ah"), K("rp"), "If", "nIh", "J1", "J2", "J3"] + prk, [K("Z%d" % n)], [Z_])
-            ts(T[K("lz")][:, ns], pZ[:, ns], -0.5 - WIN[n][0], None, A.add, None, [K("Z%d" % n)],
+                [K("ah"), "If", "nIh", "J1", "J2", "J3"] + prk + ([K("rp")] if near else []), [K("Z%d" % n)], [Z_])
+            ts(T[K("lz")][:, ns], pZ[:, ns], -0.5 - WIN[n][0] if near else FAR[n][2] - 0.5 - FAR[n][0], None, A.add, None, [K("Z%d" % n)],
                [K("lz%d_%d" % (n, b)) for b in range(4)], 128, [Z_])
         chunk[0] = 2 * t + q
         if PDSEP:
             tt(T[K("Pd")][:], pA[:, 384:512], T[K("fi")][:], A.mult, [K("DT"), K("fi")], [K("Pd")], 128, [A_])
-            mms([(pN[:, 444:452], T.oneh[0:2, :], T.rowp[0:2, 60:68], 64), (pN[:, 444:452], T[K("Pe")][:], T.Be[:, 60:68], 64),
+            mms([(pN[:, 444:452], T.ones[0:2, :], T.rowp[0:2, 60:68], 64), (pN[:, 444:452], T[K("Pe")][:], T.Be[:, 60:68], 64),
                  (pN[:, 444:452], T[K("Pd")][:], T.Bd[:], 256)], [K("Pe"), K("Pd"), "Bd0", "Bd1"], [K("pk")], [N_])
             ts(cf[:, 60:64], pN[:, 444:448], M4, -M4, A.add, A.add, [K("pk")], [K("rnd")], 4, [N_])
         tt(cf[:, 64:68], pN[:, 448:452], cf[:, 60:64], A.subtract, [K("pk"), K("rnd")], [K("dd")], 4, [N_])
         mms([(pN[:, 0:128], T.Bh[:], T[K("PG")][:], 128), (pN[:, 0:128], Hh[:, 16:144], I(-1), 128),
              (pN[:, 0:128], T.nTri[:], T[K("fl")][:], 128)], ["Bh", K("PG"), K("Hh"), "I-1", "nTri", K("fl")], [K("G2")], [N_])
-        ts(T[K("ru")][:], pN[:, 0:128], 0.0, None, A.is_equal, None, [K("G2")], [K("ru")], 128, [N_])
+        if RU_ON == "S":
+            act(T[K("rm")][:], pN[:, 0:128], F.Abs, [K("G2")], [K("ra")], 128, [N_])
+            op("S", cyc(128), lambda: [S.activation(T[K("ru")][:], T[K("rm")][:], F.Relu, 1.0, -2.0)], [K("ra")], [K("ru")])
+        else:
+            ts(T[K("ru")][:], pN[:, 0:128], 0.0, None, A.is_equal, None, [K("G2")], [K("ru")], 128, [N_])
         tt(T[K("mo")][:], pA[:, 128:256], T[K("ru")][:], A.mult, [K("e0"), K("ru")], [K("mo")], 128, [A_])
         mms([(pN[:, 0:20], T.ones[0:1, :], T.rowk[0:1, 0:20], 64), (pN[:, 0:20], I(1), cb[:, 20:40], 64),
              (pN[:, 0:20], I(4), cb[:, 40:60], 64)], ["ones", "rowk", "I1", "I4", K("rem")], [K("G2")], [N_])
-        mms([(pN[:, 128:256], T[K("ru")][:], I(2), 128), (pN[:, 128:256], T[K("fi")][:], T.nSl[:], 128)],
+        mms([(pN[:, 128:256], T[K("ru")][:], I(2), 128),  (pN[:, 128:256], T[K("fi")][:], T.nSl[:], 128)],
             [K("ru"), K("fi"), "I2", "nSl"], [K("m")], [N_])
         mms([(pN[:, 256:384], T[K("fi")][:], I(1024), 128)], [K("fi"), "I1024"], [K("FI")], [N_])
         ts(cb[:, 60:80], pN[:, 0:20], 0.0, None, A.is_ge, None, [K("G2")], [K("flg")], 20, [N_])
@@ -504,70 +642,117 @@ def rank_program(g, core, T, topo):
         pZ, Z_, pN, N_ = T[K("pZ")], K("pZ"), T[K("pN")], K("pN")
         yb = T["y%d" % t]
         subs = [0]
+        held = []
+        sizes = []
+        later = {}
+
+        def joined():
+            ZK = [K("Z2"), K("Z3")]
+            if MZ_ON == "V":
+                mms([(pZ[:, 256:512], T.ones[0:1, :], T.rowm[0:1, :], 256)], ["ones", "rowm"], ZK, [Z_], True, False)
+            else:
+                mms([(pZ[:, 256:512], T.ones[0:1, :], T.rowb[0:1, :], 256), (pZ[:, 256:384], I(4096), T[K("ru")][:], 128),
+                     (pZ[:, 384:512], I(4096), T[K("ru")][:], 128)], ["ones", "rowb", "I4096", K("ru")], ZK, [Z_], True, False)
+                mms([(pN[:, 32 + k:72:5], T[K("ru")][:], T.Bneg[:], 64) for k in (2, 3)], ["Bneg", K("ru")], [], [N_], False, False)
+            for l, dk, rk, tw in held:
+                if tw:
+                    mms(l[1:9], ["seln"] + dk, [], [Z_], False, False)
+                    mms(l[9:17], ["seln"] + dk, [], [Z_], False, False)
+            for k in JOIN:
+                l, dk, rk, tw = held[k]
+                mms(l[-16:-8], ["sel", "sel2"] + rk, [], [Z_], False, False)
+                mms(l[-8:], ["sel", "sel2"] + rk, ZK if k == JOIN[-1] else [], [Z_], False, k == JOIN[-1])
+            if MZ_ON == "S":
+                act(T[K("mf")][:], pZ[:, 256:512], F.Relu, ZK, [K("mf")], 256, [Z_])
+                mms([(pN[:, 32 + k:72:5], T[K("mf")][:, 128 * k - 256:128 * k - 128], T.B256f[:], 256) for k in (2, 3)],
+                    ["B256f", K("mf")], [K("key")], [N_], False, True)
+                return
+            for k in (2, 3):
+                ks = slice(128 * k, 128 * k + 128)
+                tt(T[K("mz")][:, ks], pZ[:, ks], T[K("ru")][:], A.mult, ZK + [K("ru")], [K("mz%d" % k)], 128, [Z_])
+                mms([(pN[:, 32 + k:72:5], T[K("mz")][:, ks], T.B256[:], 64)], ["B256", K("mz%d" % k)], [K("key")] if k == 3 else [], [N_],
+                    False, k == 3)
+
         for n in ORDER:
             win = T.Xw[:, WIN[n][0]:WIN[n][1]]
             wk = X0 + ["X%d" % k for k in range(2 * n)]
-            if n == 0 and t >= DIRECT:
-                win = T.Xw[:, 2048:18560]
-                wk = X0 + ["X%d" % k for k in range(8)]
+            if t >= DIRECT:
+                win = T.Xw[:, FAR[n][0]:FAR[n][1]]
+                wk = X0 + ["X%d" % k for k in range(FAR[n][3])]
             d, r = T["d%d%d" % (n, q)], T["r%d%d" % (n, q)]
             two = "R" in ZT[q][n] or "D" in ZT[q][n]
-            h = 0
-            while h < 4:
+            dks = []
+            pend = []
+            for h in range(4):
                 ty = ZT[q][n][h]
-                m = 1
-                while m < {"S": GS, "D": GD, "E": GD}.get(ty, GV) and h + m < 4 and ZT[q][n][h + m] == ty:
-                    m += 1
-                hs = range(h, h + m)
-                cs = slice(512 * h, 512 * (h + m))
+                cs = slice(512 * h, 512 * h + 512)
                 ys = slice(2048 * q + cs.start, 2048 * q + cs.stop)
-                yk = ["y%d_%d%d" % (t, q, k * XP // 4) for k in hs]
-                src = win.indirect(T[K("lz")][:, 128 * n + 32 * h:128 * n + 32 * (h + m)])
+                yk = "y%d_%d%d" % (t, q, h * XP // 4)
                 nm = "z" if two and ty not in "RD" else "d"
-                z, zk, rk = T["%s%d%d" % (nm, n, q)], [K("%s%d_%d" % (nm, n, k)) for k in hs], [K("r%d_%d" % (n, k)) for k in hs]
+                z, zk, rk = T["%s%d%d" % (nm, n, q)], K("%s%d_%d" % (nm, n, h)), K("r%d_%d" % (n, h))
                 sc = 0.5 if two else None
-                lk = [K("lz%d_%d" % (n, k)) for k in hs]
-                if ty in "DE":
-                    op("S", 80.0 + 512 * m * GC * CY, lambda cs=cs, src=src, z=z: [S.activation(z[:, cs], src, F.Copy, 0.0, -1.0)],
-                       wk + lk, zk)
-                    op("G", GDMA, lambda cs=cs, ys=ys, z=z: g.dma_start(z[:, cs], yb[:, ys], accum_op=A.add), zk + yk, zk, (),
-                       ACC0 + ACC1 * m, "ac%d%d%d" % (q, n, h), 16)
-                    for k in range(0, m, GV):
-                        c5 = slice(cs.start + 512 * k, cs.start + 512 * min(k + GV, m))
-                        if ty == "D":
-                            ts(r[:, c5], z[:, c5], 0.0, None, A.max, None, zk, rk[k:k + GV], c5.stop - c5.start, half=True)
-                        else:
-                            act(r[:, c5], z[:, c5], F.Abs, zk, rk[k:k + GV], c5.stop - c5.start, (), sc)
+                lk = K("lz%d_%d" % (n, h))
+
+                def src(a, b, n=n, win=win):
+                    return win.indirect(T[K("lz")][:, 128 * n + a // 16:128 * n + b // 16])
+                if ty == "D":
+                    zk = gather("S", (t, q, n, nm, "S"), cs.start, cs.stop,
+                                lambda a, b, z=z, src=src: [S.activation(z[:, a:b], src(a, b), F.Copy, 0.0, -1.0)], wk + [lk], [zk])
+                    pend.append((h, zk, yk, rk))
+                    if len(pend) == GD or h == 3 or ZT[q][n][h + 1] != "D":
+                        c2 = slice(512 * pend[0][0], cs.stop)
+                        zs = [k for p in pend for k in p[1]]
+                        i = op("G", GDMA, lambda c2=c2, z=z: g.dma_start(z[:, c2], yb[:, 2048 * q + c2.start:2048 * q + c2.stop], accum_op=A.add),
+                               zs + [p[2] for p in pend], zs, (), 0.0, "ac%d%d%d" % (q, n, h), 16)
+                        op("D", 2 * DMA * len(pend), None, zs, zs, (), ACC)
+                        ops[-1]["same"] = i
+                        for p in pend:
+                            c5 = slice(512 * p[0], 512 * p[0] + 512)
+                            ts(r[:, c5], z[:, c5], 0.0, None, A.max, None, p[1], [p[3]], 512, half=True)
+                        pend = []
                 elif ty == "S":
-                    op("S", 80.0 + 512 * m * GC * CY, lambda cs=cs, src=src, z=z: [S.activation(z[:, cs], src, F.Copy)], wk + lk, zk)
-                    for k in range(m):
-                        c5 = slice(cs.start + 512 * k, cs.start + 512 * k + 512)
-                        y5 = slice(ys.start + 512 * k, ys.start + 512 * k + 512)
-                        subs[0] += 1
-                        other = subs[0] > TWOB and subs[0] % 2 == 0
-                        bk, ks = (K("pA"), [K("e1"), K("e0"), K("G1"), K("DT")]) if other else (K("pS"), [K("sub")])
-                        mms([(T[bk][:], I(1), z[:, c5], 512), (T[bk][:], I(-1), yb[:, y5], 512)], ["I1", "I-1", zk[k], yk[k]], ks, [bk])
-                        act(r[:, c5], T[bk][:], F.Abs, ks, [rk[k]], 512, [bk], sc)
+                    zk = gather("S", (t, q, n, nm, "S"), cs.start, cs.stop,
+                                lambda a, b, z=z, src=src: [S.activation(z[:, a:b], src(a, b), F.Copy)], wk + [lk], [zk])
+                    if len(sizes) >= LAG:
+                        ops[lastw[zk[0]]]["order"].add(sizes[-LAG])
+                    subs[0] += 1
+                    other = subs[0] > TWOB and subs[0] % 2 == 0
+                    bk, ks = (K("pA"), [K("e1"), K("e0"), K("G1"), K("DT")]) if other else (K("pS"), [K("sub")])
+                    mms([(T[bk][:], I(1), z[:, cs], 512), (T[bk][:], I(-1), yb[:, ys], 512)], ["I1", "I-1", yk] + zk, ks, [bk])
+                    act(r[:, cs], T[bk][:], F.Abs, ks, [rk], 512, [bk], sc)
+                    sizes.append(len(ops) - 1)
                 else:
-                    op("V", 60.0 + 512 * m * GC * CY, lambda cs=cs, ys=ys, src=src, z=z: [V.tensor_tensor(z[:, cs], src, yb[:, ys], A.subtract)],
-                       wk + yk + lk, zk)
+                    zk = gather("V", (t, q, n, nm, "V"), cs.start, cs.stop,
+                                lambda a, b, z=z, src=src: [V.tensor_tensor(z[:, a:b], src(a, b), yb[:, 2048 * q + a:2048 * q + b], A.subtract)],
+                                wk + [yk, lk], [zk])
                     if ty == "R":
-                        ts(r[:, cs], z[:, cs], 0.0, None, A.max, None, zk, rk, 512 * m, half=True)
+                        ts(r[:, cs], z[:, cs], 0.0, None, A.max, None, zk, [rk], 512, half=True)
                     else:
-                        act(r[:, cs], z[:, cs], F.Abs, zk, rk, 512 * m, (), sc)
-                h += m
+                        act(r[:, cs], z[:, cs], F.Abs, zk, [rk], 512, (), sc)
+                dks += zk if ty in "RD" else [K("d%d_%d" % (n, h))]
             ns = slice(128 * n, 128 * n + 128)
-            lst = [(pZ[:, ns], T.ones[0:1, :], T.rowm[0:1, :], 128)]
+            lst = [(pZ[:, ns], T.ones[0:1, :], T.rowm[0:1, 0:128], 128)]
             if two:
                 lst += [(pZ[:, 128 * n + i:128 * n + 128:16], d[:, i:2048:16], T.seln[:], 64) for i in range(16)]
             lst += [(pZ[:, 128 * n + i:128 * n + 128:16], r[:, i:2048:16], T.sel2[:] if two else T.sel[:, 0:8], 64) for i in range(16)]
+            if JOIN and n >= 2:
+                held.append((lst, dks, [K("r%d_%d" % (n, s)) for s in range(4)], two))
+                continue
+            later[n] = (lst, dks, two)
+        for n in SUMO:
+            if n not in later:
+                continue
+            lst, dks, two = later[n]
+            ns = slice(128 * n, 128 * n + 128)
             cuts = [0] + list(range(1 + PS, len(lst), PS)) + [len(lst)]
             for a, b in zip(cuts, cuts[1:]):
-                R = [K("d%d_%d" % (n, s)) for s in range(4) if two and a < 17] + [K("r%d_%d" % (n, s)) for s in range(4) if b > 17 or not two]
+                R = (dks if two and a < 17 else []) + [K("r%d_%d" % (n, s)) for s in range(4) if b > 17 or not two]
                 mms(lst[a:b], ["ones", "rowm", "sel", "sel2", "seln"] + R, [K("Z%d" % n)] if a == 0 or b == len(lst) else [], [Z_],
                     a == 0, b == len(lst))
             tt(T[K("mz")][:, ns], pZ[:, ns], T[K("ru")][:], A.mult, [K("Z%d" % n), K("ru")], [K("mz%d" % n)], 128, [Z_])
-            mms([(pN[:, 32 + n:72:5], T[K("mz")][:, ns], T.B256[:], 64)], ["B256", K("mz%d" % n)], [K("key")], [N_], False, n == ORDER[3])
+            mms([(pN[:, 32 + n:72:5], T[K("mz")][:, ns], T.B256[:], 64)], ["B256", K("mz%d" % n)], [K("key")], [N_], False, n == SUMO[3] and not JOIN)
+        if JOIN:
+            joined()
 
     def fin(t, q):
         K = lambda s: "%s%d" % (s, q)
@@ -609,9 +794,6 @@ def rank_program(g, core, T, topo):
         xpart(0, q)
     chunk[0] = 2
     konst()
-    if DIRECT < RO:
-        cp(T.Xw[:, 16384:18432], T.Xw[:, 8192:10240], X0, ["X6"], 2048, half=True)
-        cp(T.Xw[:, 18432:18560], T.Xw[:, 6144:6272], X0, ["X7"], 128, half=True)
     for k in range(6):
         a = 4096 - 2048 * (k // 2) if k % 2 == 0 else 10240 + 2048 * (k // 2)
         c = 6144 + (a - 6144) % 4096
@@ -623,21 +805,47 @@ def rank_program(g, core, T, topo):
             for o in range(0, 2048, CW // 2):
                 act(T.Xw[:, a + o:a + o + CW // 2], T.Xw[:, c + o:c + o + CW // 2], F.Copy, X0, ["X%d" % k], CW // 2)
         else:
-            load(out, src, "lc%d" % k, ["X%d" % k], 6000.0, X0)
+            load(out, src, "lb%d" % k, ["X%d" % k], 3500.0 + CPL * k, X0 + ["y0_0%d" % CPH])
     for t in range(RO):
         for q in range(2):
             chunk[0] = 2 * t + q - LEAD
             if t:
+                where[:] = [2 * t + q, "x", 0]
                 xpart(t, q)
+            where[:] = [2 * t + q, "g" if t else "g0", 0]
             gpart(t, q)
+            where[:] = [2 * t + q, "e" if t else "e0", 0]
+            if (t, q) == (0, 1):
+                chunk[0] = LATE
             epart(t, q)
             chunk[0] = 2 * t + q
+            where[:] = [2 * t + q, "z", 0]
             zpart(t, q)
             chunk[0] = 2 * t + q + 2 - LEAD
+            where[:] = [2 * t + q, "f" if t < RO - 1 else "f9", 0]
             fin(t, q)
+        where[:] = [None, "end%d" % t, 0]
         if t < RO - 1:
-            op("loc%d" % t, 0.0, None, (), ["loc%d" % t], (), 1000.0, "loc%d" % t, 16 * 2 * XP)
+            op("loc%d" % t, 0.0, None, (), ["loc%d" % t], (), 1000.0, "loc%d" % t, left[t])
+            ops[-1]["order"].add(sent[0])
+        if t == 0:
+            for k, (a, b, c) in enumerate(((16384, 18432, 8192), (18432, 22528, 6144), (22528, 26624, 6144), (26624, XW, 6144))):
+                if MORE[k] == "Y":
+                    load(T.Xw[:, a:b], T.Xw[:, c:c + b - a], "lc%d" % k, ["X%d" % (6 + k)], 5000.0 + 4000.0 * k, X0 + ["loc0"])
+                else:
+                    for o in range(0, b - a, CW):
+                        e = min(o + CW, b - a)
+                        cp(T.Xw[:, a + o:a + e], T.Xw[:, c + o:c + e], X0, ["X%d" % (6 + k)], e - o, half=True)
 
+    for beat in BEAT:
+        prev = None
+        for h in range(FROM, 2 * RO + 1):
+            for w in beat.split():
+                i = named.get((h + {"-": -1, "+": 1}.get(w[0], 0), w.lstrip("+-")))
+                if i is not None:
+                    if prev is not None:
+                        ops[i]["order"].add(prev)
+                    prev = i
     if "seq" not in PLAN:
         PLAN["seq"] = tighten(ops, schedule(ops))
     seq = PLAN["seq"]
@@ -648,16 +856,36 @@ def rank_program(g, core, T, topo):
     clock = {q: {} for q in ENG}
     tail = {q: {} for q in ENG}
     fin_clock = {}
+    after, prev = {}, {}
+    for i in seq:
+        q = ops[i]["q"]
+        after[prev.get(q)] = i
+        prev[q] = i
     for i in seq:
         o = ops[i]
         q = o["q"]
+        if i in val:
+            continue
+        if "same" in o:
+            val[i], fin_clock[i] = val[o["same"]], fin_clock[o["same"]]
+            continue
         if q not in ENG:
             val[i] = (o["sem"], o["inc"])
             fin_clock[i] = {o["sem"]: o["inc"]}
             continue
+        parts = [i]
+        if "run" in o:
+            run, lo, hi, make = o["run"]
+            j = after.get(i)
+            while (j is not None and "run" in ops[j] and ops[j]["run"][0] == run and ops[j]["run"][1] == hi and hi - lo < UMAX
+                   and all(k in val for k in ops[j]["hard"])):
+                parts.append(j)
+                hi = ops[j]["run"][2]
+                j = after.get(j)
+            o["fn"] = lambda: make(lo, hi)
         cur = clock[q]
         need = {}
-        for j in o["hard"]:
+        for j in set().union(*[ops[k]["hard"] for k in parts]):
             if j in val:
                 s, v = val[j]
                 if cur.get(s, 0) < v and need.get(s, (0, 0))[0] < v:
@@ -688,8 +916,10 @@ def rank_program(g, core, T, topo):
                     d[a] = b
             d[s] = count[s]
             fin_clock[i] = dict(d)
+            for k in parts[1:]:
+                val[k], fin_clock[k] = val[i], fin_clock[i]
     g.sync.wait_ge(T.sem.out, count["out"])
     for s in ("sv", "ss", "sp", "sg"):
         g.wait_ge(T.sem[s], count[s])
     for t in range(RO):
-        g.wait_ge(T.sem["loc%d" % t], 16 * 2 * XP)
+        g.wait_ge(T.sem["loc%d" % t], left[t])

from concourse.bass import DstId, RemoteDMATransfer
from concourse.mybir import dt, AluOpType, AxisListType, ActivationFunctionType

A = AluOpType
F = ActivationFunctionType
RO = 5
DIST = (1, 3, 6)
PS = 8
TWOB = 1
DIRECT = 1
PDSEP = False
CW = 512
SUMO = (0, 1, 2, 3)
JOIN = (1, 0)
EB = "SNZS"
ETAIL = False
PEC = 0.43
ISSUE = 600.0
L0 = 2
MORE = "YYYY"
FAR = ((2048, 18560, 0.0, 8), (0, 20576, 0.0, 8), (2048, 26720, 4096.0, 10), (0, 28768, 4096.0, 10))
XW = 28768
WIN = [(6144 - 2048 * n, 10240 + 2048 * n) for n in range(4)]
FR = 613.0 + 1.0 / 32
M4 = 1.5 * 2 ** 25
M32 = 1.5 * 2 ** 28
M1K = 1.5 * 2 ** 33
M4K = 1.5 * 2 ** 35
LAG = 9
UW = {"V": 512, "S": 512}
UO = 55.0
UMAX = 512
XP = 4
XT = ("VVSS", "VVSS")
XT0 = ("SVSV", "VSVS")
ZT = (("SSSS", "RRRR", "RRRR", "SSSS"), ("SSSS", "RRRR", "RRRR", "SSSS"))
ORDER = (0, 1, 2, 3)
COPY = "SSVVVV"
FI_ON = "S"
OV_ON = "V"
FL_ON = "V"
R_ON = "V"
RU_ON = "V"
TH_ON = "S"
TR_ON = "S"
MZ_ON = "V"
HCOPY = True

SCRATCH = {"Xw": ("sbuf", [128, XW], "bfloat16"),
           "Dl": ("sbuf", [128, 256], "int32"), "Hl": ("sbuf", [128, 256], "int32"),
           "tl": ("sbuf", [128, 8], "int32"), "Al": ("sbuf", [128, 8], "int32"), "Am": ("sbuf", [128, 8], "int32"),
           "Ab": ("sbuf", [128, 8], "float32"), "thm": ("sbuf", [128, 24], "bfloat16"),
           "thf": ("sbuf", [128, 16], "float32")}
for _t in range(3):
    SCRATCH["x%d" % _t] = ("sbuf", [128, 4096], "bfloat16")
for _t in range(RO):
    SCRATCH["y%d" % _t] = ("sbuf", [128, 4096], "bfloat16")
for _n in ("ones", "Bt", "Bb", "Ss", "V1", "Tri", "nSl", "Bi", "Bp", "Ce", "Cg", "rowp"):
    SCRATCH[_n] = ("sbuf", [128, 128], "bfloat16")
SCRATCH["bias"] = ("sbuf", [128, 4], "float32")
IS = {1: 0, -1: 1, 2: 2, 1024: 3, 4: 4, -4: 5, 128: 6, 112: 7, 4096: 8, 16: 9}
SCRATCH["Is"] = ("sbuf", [128, 128 * len(IS)], "bfloat16")
SCRATCH["nTri"] = ("sbuf", [128, 128], "bfloat16")
for _n in ("nIh", "Bh", "Be", "Bg"):
    SCRATCH[_n] = ("sbuf", [128, 128], "float16")
SCRATCH["I4"] = ("sbuf", [128, 384], "float16")
SCRATCH["B256"] = ("sbuf", [128, 8], "float16")
SCRATCH["Bd"] = ("sbuf", [128, 8], "float32")
SCRATCH["sel"] = ("sbuf", [128, 16], "bfloat16")
for _n in ("selt", "sel2", "seln"):
    SCRATCH[_n] = ("sbuf", [128, 8], "bfloat16")
SCRATCH["rowm"] = ("sbuf", [128, 256], "bfloat16")
SCRATCH["rowk"] = ("sbuf", [128, 60], "bfloat16")
SCRATCH["rs"] = ("sbuf", [128, 40], "float32")
SCRATCH["If"] = ("sbuf", [128, 128], "float32")
for _q in range(2):
    for _n in range(4):
        SCRATCH["d%d%d" % (_n, _q)] = ("sbuf", [128, 2048], "bfloat16")
        SCRATCH["r%d%d" % (_n, _q)] = ("sbuf", [128, 2048], "bfloat16")
        if set(ZT[_q][_n]) & set("RD") and set(ZT[_q][_n]) - set("RD"):
            SCRATCH["z%d%d" % (_n, _q)] = ("sbuf", [128, 2048], "bfloat16")
    for _n, _w, _d in (("ab", 2048, "bfloat16"), ("Dp", 128, "float32"), ("Hh", 144, "bfloat16"), ("fl", 128, "bfloat16"),
                       ("TR", 256, "bfloat16"), ("ov", 128, "bfloat16"), ("fi", 128, "bfloat16"), ("PG", 128, "float16"),
                       ("Pe", 128, "float16"), ("Pd", 128, "float32"), ("ru", 128, "bfloat16"), ("mo", 128, "float16"),
                       ("mz", 512, "float16"), ("pr", 128, "float32"), ("lz", 512, "uint16"), ("lx", 128, "uint16"),
                       ("ah", 128, "float16"), ("rp", 128, "float16"), ("xi", 128, "int32"), ("cf", 144, "float32"), ("cb", 80, "bfloat16"),
                       ("ch", 8, "bfloat16"), ("oD", 128, "float32"), ("oH", 128, "float32"), ("oA", 4, "float32")):
        SCRATCH["%s%d" % (_n, _q)] = ("sbuf", [128, _w], _d)
    for _n in ("pA", "pZ", "pN", "pS"):
        SCRATCH["%s%d" % (_n, _q)] = ("psum", [128, 512], "float32")

SEMAPHORES = ["sv", "ss", "sp", "sg", "out", "ldD", "ldH", "ldE", "ldI", "ldt", "ldA", "lxa", "lxb"]
SEMAPHORES += ["lb%d" % k for k in range(6)] + ["lc%d" % k for k in range(4)] + ["loc%d" % t for t in range(RO)]
SEMAPHORES += ["ar%d%d%d" % (t, q, h) for t in range(RO) for q in range(2) for h in range(XP)]
SEMAPHORES += ["ac%d%d%d" % (q, n, h) for q in range(2) for n in range(4) for h in range(4) if ZT[q][n][h] == "D"]

GD = 2
GDMA = 1000.0
DMA = 600.0
ACC = 2000.0
CY = 0.86
GC = 1.56
HOP = 230.0
OWN = 230.0
ARR = 3200.0
XLAT = 7000.0
PASSES = 2
LEAD = 1.5
LATE = -0.5
LOADS = (0, 1, 2, 3, 4, 5, 6, 7)
CPL = 1300.0
CPH = 1
ZL = None
FEW = 1
FROM = 1
BEAT = ("pr3 -mz2 -mz3 ru lz0_2 -sc lz1_0 -mut mo -df -f0 -f1 -f2 -f3 -m0 -m1 -m2 -m3 -Dp -m -a +xi +xi' lz2_0 +lx flg +x0 +x1 d1_0 lz3_0 +fl d1_1 +Z2 d1_2 r1_0 +ah d2_0 r1_1 d1_3 mz0 d2_1 r1_2 r1_3 d2_2 +ov d2_3 mz1 r2_1 +Pe +PG +Pd r2_0 r2_2 +rnd r2_3 +rem +dd +lz0_0 +lz0_1 +pr1 +pr2 +pr0", "d0_0 d0_1 d0_2 r0_0 d0_3 +Hh +w r0_1 +x2 +TR +x3 r0_2 r0_3 d3_0 d3_1 d3_2 +ab0 +ab2 +ab1 +ab3 d3_3 r3_0 r3_1 +fi r3_2 r3_3")
LOOK = 500.0
TOL = 50.0
WAIT = 0.0
NOISE = 0.0
SEED = 1
SERIAL = False
BIAS = 1000000.0
SLACK = 100.0


def schedule(ops):
    n = len(ops)
    succ = [[] for _ in range(n)]
    for i, o in enumerate(ops):
        for j in o["hard"] | o["order"]:
            succ[j].append(i)
    prio = [0.0] * n
    for i in range(n - 1, -1, -1):
        prio[i] = ops[i]["cost"] + ops[i]["lat"] + max([prio[j] + HOP for j in succ[i]], default=0.0)
    for i in range(n):
        prio[i] -= BIAS * ops[i]["ch"] + NOISE * ((i * SEED * 0.6180339887) % 1.0)
    for i in range(n - 1, -1, -1):
        prio[i] = max([prio[i]] + [prio[j] + 1.0 for j in succ[i]])
    if SERIAL:
        return sorted(range(n), key=lambda i: -prio[i])
    left = [len(o["hard"] | o["order"]) for o in ops]
    ready = [0.0] * n
    avail = {}
    pend = {}
    for i in range(n):
        if left[i] == 0:
            pend.setdefault(ops[i]["q"], []).append(i)
    done = []
    while len(done) < n:
        best = None
        for q, lst in pend.items():
            if not lst:
                continue
            av = avail.get(q, 0.0)
            m = min(max(av, ready[i]) for i in lst)
            c = max((i for i in lst if max(av, ready[i]) <= m + SLACK), key=lambda i: prio[i])
            if q in ("V", "S"):
                soon = [(ready[i], i) for i in lst if m + SLACK < ready[i] <= m + LOOK and prio[i] > prio[c] + BIAS / 4]
                far = []
                for k in pend.get("P", ()):
                    e = max(avail.get("P", 0.0), ready[k]) + ops[k]["cost"] + HOP
                    far += [e for j in succ[k] if ops[j]["q"] == q and left[j] == 1 and m < e <= m + LOOK and prio[j] > prio[c] + BIAS / 4]
                if soon or far:
                    when = min([x[0] for x in soon] + far)
                    fit = [i for i in lst if max(av, ready[i]) + ops[i]["cost"] <= when + TOL]
                    if fit:
                        c = max(fit, key=lambda i: prio[i])
                    elif soon and min(soon)[0] == when:
                        c = min(soon)[1]
                    elif when - m <= WAIT and pend.get("P"):
                        continue
            st = max(av, ready[c])
            if best is None or st < best[0]:
                best = (st, c)
        st, c = best
        o = ops[c]
        pend[o["q"]].remove(c)
        avail[o["q"]] = st + o["cost"]
        end = st + o["cost"] + o["lat"]
        done.append(c)
        for j in succ[c]:
            hop = 0.0 if c not in ops[j]["hard"] else (OWN if ops[j]["q"] == o["q"] else HOP)
            ready[j] = max(ready[j], (end if c in ops[j]["hard"] else st) + hop)
            left[j] -= 1
            if left[j] == 0:
                pend.setdefault(ops[j]["q"], []).append(j)
    return done


def place(ops, seq, before):
    st = [0.0] * len(ops)
    taken = {}
    for i in seq:
        t = max([st[j] + d for j, d in before[i]], default=0.0)
        c = ops[i]["cost"]
        lst = taken.setdefault(ops[i]["q"], [])
        k = len(lst)
        while k > 0 and lst[k - 1][1] > t:
            k -= 1
        while k < len(lst) and lst[k][0] < t + c:
            t = max(t, lst[k][1])
            k += 1
        lst.insert(k, (t, t + c))
        st[i] = t
    return st


def tighten(ops, seq):
    n = len(ops)
    fwd = [[] for _ in range(n)]
    bwd = [[] for _ in range(n)]
    for j, o in enumerate(ops):
        for i in o["hard"] | o["order"]:
            same = ops[i]["q"] == o["q"]
            if i in o["hard"]:
                gap = ops[i]["lat"] + (OWN if same else HOP)
            else:
                gap = 0.0 if same else -ops[i]["cost"]
            fwd[j].append((i, ops[i]["cost"] + gap))
            bwd[i].append((j, o["cost"] + gap))
    best = None
    for _ in range(PASSES):
        st = place(ops, seq, fwd)
        span = max(st[i] + ops[i]["cost"] + ops[i]["lat"] for i in range(n))
        pos = {i: k for k, i in enumerate(seq)}
        seq = sorted(range(n), key=lambda i: (st[i], pos[i]))
        if best is None or span < best[0]:
            best = (span, seq)
        pos = {i: k for k, i in enumerate(seq)}
        back = sorted(range(n), key=lambda i: (-st[i] - ops[i]["cost"], -pos[i]))
        back = topo_fix(back, bwd)
        sb = place(ops, back, bwd)
        pos = {i: k for k, i in enumerate(back)}
        seq = topo_fix(sorted(range(n), key=lambda i: (-sb[i] - ops[i]["cost"], -pos[i])), fwd)
    return best[1]


def topo_fix(seq, before):
    out, seen = [], set()
    for i in seq:
        stack = [i]
        while stack:
            k = stack[-1]
            if k in seen:
                stack.pop()
                continue
            miss = [j for j, d in before[k] if j not in seen]
            if miss:
                stack.extend(miss)
            else:
                seen.add(k)
                out.append(k)
                stack.pop()
    return out


PLAN = {}


def rank_program(g, core, T, topo):
    rank = T.rank_of(core)
    if rank is None:
        return
    n_ranks = len(T.cores)
    ops = []
    lastw, readers, bankacc = {}, {}, {}
    chunk = [0]
    sent = [0]
    left = [0] * RO
    named = {}
    where = [None, "start", 0]

    def op(q, cost, fn, R=(), W=(), banks=(), lat=0.0, sem=None, inc=1):
        i = len(ops)
        hard, order = set(), set()
        for k in R:
            if k in lastw:
                hard.add(lastw[k])
        for k in W:
            if k in lastw:
                hard.add(lastw[k])
            hard.update(readers.get(k, ()))
        for b in banks:
            d = bankacc.setdefault(b, {})
            for e, j in d.items():
                if e == q:
                    order.add(j)
                else:
                    hard.add(j)
            d[q] = i
        for k in R:
            readers.setdefault(k, []).append(i)
        for k in W:
            lastw[k] = i
            readers[k] = []
        hard.discard(i)
        ops.append({"q": q, "cost": cost, "fn": fn, "hard": hard, "order": order - hard, "lat": lat, "sem": sem, "inc": inc, "ch": chunk[0],
                    "at": tuple(where)})
        where[2] += 1
        if q in ("V", "S") and where[0] is not None:
            nm = W[0]
            nm = "x" + nm[-1] if nm[0] == "x" and "_" in nm else (nm[:-3] if nm.endswith("u0") else nm[:-1])
            while (where[0], nm) in named:
                nm += "'"
            named[where[0], nm] = i
        return i

    V, S, P = g.vector, g.scalar, g.tensor

    def cyc(n):
        return max(n, 64) * CY

    def tt(out, a, b, o, R, W, n, banks=()):
        op("V", cyc(n if banks else 2 * n), lambda: [V.tensor_tensor(out, a, b, o)], R, W, banks)

    def ts(out, a, s1, s2, o0, o1, R, W, n, banks=(), half=False):
        def f():
            if o1 is None:
                return [V.tensor_scalar(out, a, s1, None, o0)]
            return [V.tensor_scalar(out, a, s1, s2, o0, o1)]
        op("V", cyc(n / 2 if half else n), f, R, W, banks)

    def cp(out, a, R, W, n, banks=(), half=False):
        op("V", cyc(n / 2 if half else n), lambda: [V.tensor_copy(out, a)], R, W, banks)

    def act(out, a, fn, R, W, n, banks=(), scale=None):
        def f():
            if scale is None:
                return [S.activation(out, a, fn)]
            return [S.activation(out, a, fn, 0.0, scale)]
        op("S", cyc(n), f, R, W, banks)

    def mms(lst, R, W, banks, start=True, stop=True):
        def f():
            return [P.matmul(o, l, r, start and i == 0, stop and i == len(lst) - 1) for i, (o, l, r, c) in enumerate(lst)]
        i = op("P", sum(x[3] for x in lst) * PEC, f, R, W, banks)
        if not start:
            same = {j for j in ops[i]["hard"] if ops[j]["q"] == "P"}
            ops[i]["hard"] -= same
            ops[i]["order"] |= same

    def gather(q, run, lo, hi, make, R, W):
        for k, a in enumerate(range(lo, hi, UW[q])):
            i = op(q, UO + UW[q] * GC * CY, None, R, [w + "u%d" % k for w in W])
            ops[i]["run"] = (run, a, a + UW[q], make)
            if run in lastw:
                ops[i]["order"].add(lastw[run])
            lastw[run] = i
        return [w + "u%d" % k for w in W for k in range((hi - lo) // UW[q])]

    def load(out, in_, sem, W, lat, R=()):
        return op("Y", 60.0, lambda: g.sync.dma_start(out, in_), R, W, (), lat, sem, 16)

    def fill(ap, val, W, n=64):
        op("V", cyc(n), lambda: [V.memset(ap, val)], (), W)

    def sfill(ap, like, val, W):
        act(ap, like, F.Copy, ["ones"], W, 64, (), val)

    def sel(out, in_, pat, cmp, base, cm, R, W, n):
        op("G", 200.0 + 2 * n * CY, lambda: [g.affine_select(out, in_, pat, cmp, 0.0, base, cm)], R, W)

    def I(k):
        return T.Is[:, 128 * IS[k]:128 * IS[k] + 128]

    loads = [load(T.Dl[:, 0:128], T.D[:, 0:128], "ldD", ["Dl0"], 2400.0),
             load(T.Hl[:, 0:128], T.H[:, 0:128], "ldH", ["Hl0"], 2700.0),
             load(T.Xw[:, 6451:10240], T.X[:, 0:3789], "lxa", ["Xa"], XLAT),
             load(T.Xw[:, 6144:6451], T.X[:, 3789:4096], "lxb", ["Xb"], XLAT),
             load(T.Dl[:, 128:256], T.D[:, 128:256], "ldE", ["Dl1"], XLAT + 300.0),
             load(T.Hl[:, 128:256], T.H[:, 128:256], "ldI", ["Hl1"], XLAT + 600.0),
             load(T.tl[:], T.th[:], "ldt", ["tl"], XLAT + 600.0),
             load(T.Al[:], T.A[:], "ldA", ["Al"], XLAT + 600.0)]
    loads = [loads[k] for k in LOADS]
    for k, i in enumerate(loads):
        ops[i]["lat"] = 2400.0 + 300.0 * k if k < LOADS.index(2) else XLAT + 200.0 * k
    for a, b in zip(loads, loads[1:]):
        ops[b]["order"].add(a)
    X0 = ["Xa", "Xb"]

    fill(T.ones[:], 1.0, ["ones"])
    sel(I(1), T.ones[:], [[-1, 128]], A.is_equal, 0, 1, ["ones"], ["I1"], 128)
    sel(T.selt[:], T.ones[:, 0:8], [[-16, 8]], A.is_ge, 0, 1, ["ones"], ["selt"], 8)
    sel(T.sel[:, 0:8], T.selt[:], [[16, 8]], A.is_ge, 15, -1, ["selt"], ["sel"], 8)
    sel(T.Bt[:], T.ones[:], [[-32, 4], [0, 32]], A.is_ge, 0, 1, ["ones"], ["Bt"], 128)
    sel(T.Bb[:], T.Bt[:], [[32, 4], [0, 32]], A.is_ge, 31, -1, ["Bt"], ["Bb"], 128)
    sel(T.Ss[:], T.Bb[:], [[1, 128]], A.is_ge, -1, -1, ["Bb"], ["Ss"], 128)
    sel(T.Bi[:], T.ones[:], [[-1, 4], [0, 32]], A.not_equal, 0, 1, ["ones"], ["Bi"], 128)
    sel(T.Bi[:], T.Bi[:], [[-1, 4], [0, 32]], A.not_equal, -4, 1, ["Bi"], ["Bi"], 128)
    sel(T.Bi[:], T.Bi[:], [[-1, 4], [0, 32]], A.not_equal, -8, 1, ["Bi"], ["Bi"], 128)
    ts(T.Bi[:], T.Bi[:], -1.0, 1.0, A.mult, A.add, ["Bi"], ["Bi"], 128, half=True)
    for c0, rep, w in ((0, 3, 5), (60, 2, 1), (68, 3, 5)):
        cs = slice(c0, c0 + 4 * rep * w)
        sel(T.Bt[:, cs], T.ones[:, cs], [[0, rep], [-32, 4], [0, w]], A.is_ge, 0, 1, ["ones"], ["Bt"], 64)
        sel(T.Bp[:, cs], T.Bt[:, cs], [[0, rep], [32, 4], [0, w]], A.is_ge, 31, -1, ["Bt"], ["Bp%d" % c0], 64)

    for q in range(2):
        c0 = slice(128 * q, 128 * q + 128)
        ts(T["Dp%d" % q][:], T.Dl[:, c0], FR, None, A.add, None, ["Dl%d" % q], ["Dp%d" % q], 128)
        ts(T["Hh%d" % q][:, 16:144], T.Hl[:, c0], 0.5, None, A.add, None, ["Hl%d" % q], ["Hh%d" % q], 128)

    def konst():
        for k in IS:
            if k != 1 and (k != 4096 or MZ_ON == "S"):
                ts(I(k), I(1), float(k), None, A.mult, None, ["I1"], ["I%d" % k], 128, half=True)
        ts(T.nIh[:], I(1), -1.0, None, A.mult, None, ["I1"], ["nIh"], 128, half=True)
        cp(T.If[:], I(1), ["I1"], ["If"], 128)
        for n in (1, 2, 3):
            ts(T.I4[:, 128 * n - 128:128 * n], I(1), 4.0 * n, None, A.mult, None, ["I1"], ["J%d" % n], 128, half=True)
        cp(T.sel[:, 8:16], T.sel[:, 0:8], ["sel"], ["selb"], 8)
        ts(T.sel2[:], T.sel[:, 0:8], 2.0, None, A.mult, None, ["sel"], ["sel2"], 8)
        ts(T.seln[:], T.sel[:, 0:8], -1.0, None, A.mult, None, ["sel"], ["seln"], 8)
        tt(T.V1[:], I(1), T.Ss[:], A.subtract, ["I1", "Ss"], ["V1"], 128)
        ts(T.V1[:], T.V1[:], 0.5, None, A.mult, None, ["V1"], ["V1"], 128, half=True)
        fill(T.bias[:, 0:1], -2040.5, ["bias"])
        fill(T.bias[:, 1:2], -31.5, ["bias"])
        fill(T.bias[:, 2:3], M1K, ["bias"])
        fill(T.bias[:, 3:4], -M1K, ["bias"])
        for o in (0, 4) if MZ_ON == "S" else ():
            fill(T.rowb[0:1, :], -4096.0, ["rowb"])
            ts(T.B256f[:, o:o + 4], T.Bb[:, 0:128:32], 256.0, None, A.mult, None, ["Bb"], ["B256f"], 4)
            ts(T.Bneg[:, o:o + 4], T.Bb[:, 0:128:32], -2040.0 * 256, None, A.mult, None, ["Bb"], ["Bneg"], 4)
        tt(T.Tri[:], I(1), T.Ss[:], A.add, ["I1", "Ss"], ["Tri"], 128)
        tt(T.nSl[:], T.Tri[:], T.Bb[:], A.subtract, ["Tri", "Bb"], ["nSl"], 128)
        ts(T.nTri[:], T.Tri[:], -16.0, None, A.mult, None, ["Tri"], ["nTri"], 128, half=True)
        ts(T.Tri[:], T.Tri[:], 16.0, None, A.mult, None, ["Tri"], ["Tri"], 128, half=True)
        cp(T.Bh[:], T.Bb[:], ["Bb"], ["Bh"], 128, half=True)
        ts(T.B256[:, 0:4], T.Bb[:, 0:128:32], 256.0, None, A.mult, None, ["Bb"], ["B256"], 4)
        ts(T.B256[:, 4:8], T.Bb[:, 0:128:32], 256.0, None, A.mult, None, ["Bb"], ["B256"], 4)
        ts(T.Bd[:, 0:4], T.Bb[:, 0:128:32], 13.0 / 1024, None, A.mult, None, ["Bb"], ["Bd0"], 4)
        ts(T.Bd[:, 4:8], T.Bb[:, 0:128:32], 12.0 / 1024, None, A.mult, None, ["Bb"], ["Bd1"], 4)
        def cols(buf, rows, cs, v):
            sfill(T[buf][rows, cs], T.ones[rows, cs], v, [buf])
        every, first, both = slice(0, 128), slice(0, 1), slice(0, 2)
        cols("Ce", every, every, 1.0)
        cols("Cg", every, every, 0.0)
        cols("rowp", both, every, 0.0)
        cols("Ce", every, slice(60, 68), 1.0 / 1024)
        for c in (0, 68):
            cols("Ce", every, slice(c + 24, c + 40, 5), 0.0)
            cols("Ce", every, slice(c + 40, c + 60), 0.0)
            cols("Cg", every, slice(c, c + 20), 1.0)
            cols("Cg", every, slice(c + 40, c + 60), 0.25)
            cols("Cg", every, slice(c + 4, c + 60, 5), 0.0)
            cols("Cg", every, slice(c + 24, c + 40, 5), -0.25)
        Bp = ["Bp0", "Bp60", "Bp68"]
        tt(T.Be[:], T.Bp[:], T.Ce[:], A.mult, Bp + ["Ce"], ["Be"], 128)
        tt(T.Bg[:], T.Bp[:], T.Cg[:], A.mult, Bp + ["Cg"], ["Bg"], 128)
        cols("rowp", both, slice(64, 68), 11.625 / 1024)
        for cs, v in ((slice(0, 20), -1.0), (slice(20, 40), -1.5), (slice(40, 60), -1.9375), (slice(4, 20, 5), -1.5),
                      (slice(24, 40, 5), 1.9375), (slice(44, 60, 5), 0.0), (slice(60, 64), 215.0 / 1024),
                      (slice(64, 68), 2864.0 / 1024), (slice(68, 88), 1.0), (slice(72, 88, 5), 0.0)):
            cols("rowp", first, cs, v)
        fill(T.rowm[0:1, :], -2040.0, ["rowm"])
        for n in range(5):
            cols("rowk", first, slice(n, 20, 5), 0.5 - 4 * (n + 1) if n < 4 else 0.0)
            cols("rowk", first, slice(20 + n, 40, 5), 32.0 + 36 * n if n < 4 else 1.0)
            cols("rowk", first, slice(40 + n, 60, 5), 32.0 + 32 * n if n < 4 else 0.0)
        fill(T.rs[:], 0.0, ["rs"])
        fill(T.rs[:, 0:40:5], 1e9, ["rs"])
        ts(T.thf[:, 0:8], T.tl[:], -1.0, 2056.0 if TH_ON == "S" else 2040.0, A.mult, A.add, ["tl"], ["thf"], 8)
        ts(T.thf[:, 8:16], T.thf[:, 0:8], M32, -M32, A.add, A.add, ["thf"], ["thg"], 8)
        fill(T.thm[:], 0.0, ["thm"])
        for q in range(2):
            cp(T.thm[:, 12 * q + 4:12 * q + 8], T.thf[:, 8 + 4 * q:12 + 4 * q], ["thg"], ["thm"], 4)
            tt(T.thm[:, 12 * q + 8:12 * q + 12], T.thf[:, 4 * q:4 * q + 4], T.thf[:, 8 + 4 * q:12 + 4 * q], A.subtract, ["thf", "thg"], ["thm"], 4)
        ts(T.Am[:], T.Al[:], 31, None, A.bitwise_and, None, ["Al"], ["Am"], 8)
        tt(T.Ab[:], T.Al[:], T.Am[:], A.subtract, ["Al", "Am"], ["Ab"], 8)
        for q in range(2):
            cp(T["ch%d" % q][:, 0:4], T.Am[:, 4 * q:4 * q + 4], ["Am"], ["a%d" % q], 4)
            fill(T["Hh%d" % q][:, 0:16], 0.0, ["H0%d" % q])
            fill(T["TR%d" % q][0:12, 128:256], 0.0, ["TRc%d" % q])
            fill(T["TR%d" % q][0:4, 128:256], -2040.0, ["TRc%d" % q])
            for n in range(4):
                if "z%d%d" % (n, q) in SCRATCH:
                    for h in range(4):
                        if ZT[q][n][h] not in "RD":
                            fill(T["d%d%d" % (n, q)][:, 512 * h:512 * h + 512], 0.0, ["d%d_%d%d" % (n, h, q)], 256)

    def xpart(t, q):
        K = lambda s: "%s%d" % (s, q)
        xb = "x%d" % (t % 3)
        if t == 0 or not HCOPY:
            tt(T[K("xi")][:], T[K("Dp")][:], T[K("Hh")][:, 16:144], A.mult, [K("Dp"), K("Hh")], [K("xi")], 128)
        else:
            pN = T[K("pN")]
            tt(T[K("xi")][:], pN[:, 128:256], T[K("Dp")][:], A.mult, [K("Dp"), K("m")], [K("xi")], 128, [K("pN")])
            act(T[K("Hh")][:, 16:144], pN[:, 128:256], F.Copy, [K("m")], [K("Hh")], 128, [K("pN")])
        ts(T[K("xi")][:], T[K("xi")][:], 4095, None, A.bitwise_and, None, [K("xi")], [K("xi")], 128)
        cp(T[K("lx")][:], T[K("xi")][:], [K("xi")], [K("lx")], 128)
        w = 2048 // XP
        dst = T.cores[(rank - DIST[t % 3]) % n_ranks]
        rid, pid = topo.addr(dst)[:2]
        for h in range(XP):
            cs = slice(2048 * q + w * h, 2048 * q + w * h + w)
            src = T.Xw[:, 6144:10240].indirect(T[K("lx")][:, (w // 16) * h:(w // 16) * (h + 1)])
            R, W = X0 + [K("lx")] + (["loc%d" % (t - 3)] if t >= 3 else []), ["%s_%d%d" % (xb, q, h)]
            if (XT if t else XT0)[q][h] == "V":
                op("V", 60.0 + w * GC * CY, lambda src=src, cs=cs: [V.tensor_copy(T[xb][:, cs], src)], R, W)
            else:
                op("S", 80.0 + w * GC * CY, lambda src=src, cs=cs: [S.activation(T[xb][:, cs], src, F.Copy)], R, W)
            ar = "ar%d%d%d" % (t, q, h)
            eng = topo.engines(core, dst)[::FEW if (t, q) == (0, 0) else 1]
            left[t] += len(eng)
            i = op("G", ISSUE, lambda cs=cs, ar=ar, eng=eng: g.remote_dma(T["y%d" % t][:, cs], T[xb][:, cs], T.sem[ar], T.sem["loc%d" % t],
                                                                           pid, rid, sum(1 << e for e in eng)),
                   ["%s_%d%d" % (xb, q, h)], [], (), 0.0, None, 0)
            a = op("D", DMA, None, (), ["y%d_%d%d" % (t, q, h)], (), ARR - ISSUE - DMA - HOP, ar, len(eng))
            ops[a]["hard"].add(i)
            sent[0] = i

    def gpart(t, q):
        K = lambda s: "%s%d" % (s, q)
        pA, pZ, A_, Z_ = T[K("pA")], T[K("pZ")], K("pA"), K("pZ")
        Hh, ch = T[K("Hh")], T[K("ch")]
        if t == 0:
            mms([(pZ[0:12, 384:512], T.thm[:, 12 * q:12 * q + 12], I(1), 128)], ["thm", "I1"], [K("Z3")], [Z_])
            cp(T[K("TR")][0:12, 0:128], pZ[0:12, 384:512], [K("Z3")], [K("TR")], 128, [Z_])
        if TH_ON == "S":
            op("S", cyc(64), lambda: [S.activation(ch[:, 4:8], ch[:, 0:4], F.Sign, T.bias[:, 1:2])], [K("a"), "bias"], [K("w")])
        else:
            ts(ch[:, 4:8], ch[:, 0:4], 31.5, 2.0, A.is_gt, A.mult, [K("a")], [K("w")], 4)
        mms([(pZ[0:4, 128:256], ch[:, 0:4], I(-1), 128), (pZ[0:4, 128:256], ch[:, 4:8], I(16), 128)],
            ["I-1", "I16", K("a"), K("w")], [K("Z1")], [Z_])
        mms([(pZ[:, 0:128], Hh[:, 16:144], I(1), 128), (pZ[:, 0:128], Hh[:, 15:143], I(-1), 128)],
            ["I1", "I-1", K("Hh"), K("H0")], [K("Z0")], [Z_])
        if TR_ON == "S":
            act(T[K("TR")][0:4, 0:128], pZ[0:4, 128:256], F.Copy, [K("Z1")], [K("TR")], 128, [Z_])
        else:
            cp(T[K("TR")][0:4, 0:128], pZ[0:4, 128:256], [K("Z1")], [K("TR")], 128, [Z_])
        if FL_ON == "S":
            act(T[K("fs")][:], pZ[:, 0:128], F.Sign, [K("Z0")], [K("fs")], 128, [Z_])
            act(T[K("fl")][:], T[K("fs")][:], F.Abs, [K("fs")], [K("fl")], 128)
        else:
            ts(T[K("fl")][:], pZ[:, 0:128], 0.0, None, A.not_equal, None, [K("Z0")], [K("fl")], 128, [Z_])
        if R_ON == "S":
            op("S", cyc(128), lambda: [S.activation(T[K("rm")][:], T[K("Dp")][:], F.Identity, T.bias[:, 2:3])], [K("Dp"), "bias"], [K("rm")])
            op("S", cyc(128), lambda: [S.activation(pZ[:, 256:384], T[K("rm")][:], F.Identity, T.bias[:, 3:4])], [K("rm"), "bias"], [K("Z2")], [Z_])
        else:
            ts(pZ[:, 256:384], T[K("Dp")][:], M1K, -M1K, A.add, A.add, [K("Dp")], [K("Z2")], 128, [Z_])
        tt(T[K("ah")][:], T[K("Dp")][:], pZ[:, 256:384], A.subtract, [K("Dp"), K("Z2")], [K("ah")], 128, [Z_])
        mms([(pA[:, 384:512], T[K("Dp")][:], T.If[:], 512)], [K("Dp"), "If"], [K("DT")], [A_])
        mms([(pA[:, 256:384], Hh[:, 16:144], I(1), 128), (pA[:, 256:384], T.Tri[:], T[K("fl")][:], 128)],
            [K("Hh"), K("fl"), "I1", "Tri"], [K("G1")], [A_])

    def epart(t, q):
        K = lambda s: "%s%d" % (s, q)
        pA, pN, pZ, A_, N_, Z_ = T[K("pA")], T[K("pN")], T[K("pZ")], K("pA"), K("pN"), K("pZ")
        xb, yb, ab = T["x%d" % (t % 3)], T["y%d" % t], T[K("ab")]
        cf, cb, Hh = T[K("cf")], T[K("cb")], T[K("Hh")]
        NK = [K("G2"), K("m"), K("FI"), K("pk")]
        for s in range(4):
            cs = slice(2048 * q + 512 * s, 2048 * q + 512 * s + 512)
            h = s * XP // 4
            bk = K("p" + EB[s])
            ks = {"S": [K("sub")], "N": NK, "Z": [K("Z%d" % k) for k in range(4)]}[EB[s]]
            mms([(T[bk][:], I(1), xb[:, cs], 512), (T[bk][:], I(-1), yb[:, cs], 512)],
                ["I1", "I-1", "x%d_%d%d" % (t % 3, q, h), "y%d_%d%d" % (t, q, h)], ks, [bk])
            act(ab[:, 512 * s:512 * s + 512], T[bk][:], F.Abs, ks, [K("ab%d" % s)], 512, [bk])
        mms([(pA[:, 0:256], T.Bi[0:12, :], T[K("TR")][0:12, :], 256)], ["Bi", K("TR"), K("TRc")], [K("e1"), K("e0")], [A_], True, False)
        if ETAIL:
            mms([(pA[0:96, i:256:16], ab[:, i:1536:16], T.sel[:], 64) for i in range(16)],
                ["sel", "selb"] + [K("ab%d" % s) for s in range(3)], [], [A_], False, False)
            mms([(pA[96:128, i:256:16], ab[:, 1536 + i:2048:16], T.sel[:], 32) for i in range(16)],
                ["sel", "selb", K("ab3")], [K("e1"), K("e0")], [A_], False, True)
        else:
            mms([(pA[:, i:256:16], ab[:, i:2048:16], T.sel[:], 64) for i in range(16)],
                ["sel", "selb"] + [K("ab%d" % s) for s in range(4)], [K("e1"), K("e0")], [A_], False, True)
        if OV_ON == "V":
            ts(T[K("ov")][:], pA[:, 0:128], 2040.0, 2.0, A.is_gt, A.mult, [K("e1")], [K("ov")], 128, [A_])
            mms([(pA[:, 0:128], T.V1[:], T[K("ov")][:], 128)], ["V1", K("ov")], [K("e1")], [A_])
        else:
            op("S", cyc(128), lambda: [S.activation(T[K("ov")][:], pA[:, 0:128], F.Sign, T.bias[:, 0:1])], [K("e1"), "bias"], [K("ov")], [A_])
            mms([(pA[:, 0:128], T.V1[:], T.ones[:], 128), (pA[:, 0:128], T.V1[:], T[K("ov")][:], 128)], ["V1", "ones", K("ov")], [K("e1")], [A_])
        if FI_ON == "V":
            ts(T[K("fi")][:], pA[:, 0:128], 0.0, None, A.max, None, [K("e1")], [K("fi")], 128, [A_])
        else:
            act(T[K("fi")][:], pA[:, 0:128], F.Relu, [K("e1")], [K("fi")], 128, [A_])
        tt(T[K("Pe")][:], pA[:, 128:256], T[K("fi")][:], A.mult, [K("e0"), K("fi")], [K("Pe")], 128, [A_])
        tt(T[K("PG")][:], pA[:, 256:384], T[K("fi")][:], A.mult, [K("G1"), K("fi")], [K("PG")], 128, [A_])
        if not PDSEP:
            tt(T[K("Pd")][:], pA[:, 384:512], T[K("fi")][:], A.mult, [K("DT"), K("fi")], [K("Pd")], 128, [A_])
        mms([(pN[:, 384:512], T.ones[0:2, :], T.rowp[0:2, :], 128)], ["ones", "rowp"], [K("pk")], [N_], True, False)
        mms([(pN[:, 384:512], T[K("Pe")][:], T.Be[:], 128)], [K("Pe"), "Be"], [], [N_], False, False)
        mms([(pN[:, 384:512], T[K("PG")][:], T.Bg[:], 128)], [K("PG"), "Bg"], [K("pk")], [N_], False, PDSEP)
        if not PDSEP:
            mms([(pN[:, 444:452], T[K("Pd")][:], T.Bd[:], 256)], [K("Pd"), "Bd0", "Bd1"], [K("pk")], [N_], False, True)
        ts(cf[:, 0:64], pN[:, 384:448], M4, -M4, A.add, A.add, [K("pk")], [K("rnd")], 64, [N_])
        tt(cb[:, 0:60], pN[:, 452:512], cf[:, 0:60], A.subtract, [K("pk"), K("rnd")], [K("rem")], 60, [N_])
        prk = [K("pr%d" % b) for b in range(4)]
        for b in range(L0 if t >= DIRECT else 0):
            bs = slice(32 * b, 32 * b + 32)
            ts(T[K("lz")][:, bs], T[K("Dp")][:, bs], cb[:, 5 * b:5 * b + 1], None, A.mult, None, [K("Dp"), K("rem")], [K("lz0_%d" % b)], 32)
        for b in range(4):
            bs = slice(32 * b, 32 * b + 32)
            ts(T[K("pr")][:, bs], T[K("Dp")][:, bs], cb[:, 5 * b:5 * b + 1], 2048.5, A.mult, A.add, [K("Dp"), K("rem")], [prk[b]], 32)
        near = t < DIRECT
        if near:
            ts(T[K("rp")][:], T[K("pr")][:], M4K, -M4K - 8192.0, A.add, A.add, prk, [K("rp")], 128)
        for n in ORDER:
            ns = slice(128 * n, 128 * n + 128)
            if n == 0 and t >= DIRECT:
                if L0 < 4:
                    ts(T[K("lz")][:, 32 * L0:128], T[K("pr")][:, 32 * L0:128], -2048.5, None, A.add, None, prk,
                       [K("lz0_%d" % b) for b in range(L0, 4)], 128 - 32 * L0)
                continue
            mms([(pZ[:, ns], T.If[:], T[K("pr")][:], 512)] + ([(pZ[:, ns], T.nIh[:], T[K("rp")][:], 128)] if near else [])
                + ([(pZ[:, ns], T.I4[:, 128 * n - 128:128 * n], T[K("ah")][:], 128)] if n else []),
                [K("ah"), "If", "nIh", "J1", "J2", "J3"] + prk + ([K("rp")] if near else []), [K("Z%d" % n)], [Z_])
            ts(T[K("lz")][:, ns], pZ[:, ns], -0.5 - WIN[n][0] if near else FAR[n][2] - 0.5 - FAR[n][0], None, A.add, None, [K("Z%d" % n)],
               [K("lz%d_%d" % (n, b)) for b in range(4)], 128, [Z_])
        chunk[0] = 2 * t + q
        if PDSEP:
            tt(T[K("Pd")][:], pA[:, 384:512], T[K("fi")][:], A.mult, [K("DT"), K("fi")], [K("Pd")], 128, [A_])
            mms([(pN[:, 444:452], T.ones[0:2, :], T.rowp[0:2, 60:68], 64), (pN[:, 444:452], T[K("Pe")][:], T.Be[:, 60:68], 64),
                 (pN[:, 444:452], T[K("Pd")][:], T.Bd[:], 256)], [K("Pe"), K("Pd"), "Bd0", "Bd1"], [K("pk")], [N_])
            ts(cf[:, 60:64], pN[:, 444:448], M4, -M4, A.add, A.add, [K("pk")], [K("rnd")], 4, [N_])
        tt(cf[:, 64:68], pN[:, 448:452], cf[:, 60:64], A.subtract, [K("pk"), K("rnd")], [K("dd")], 4, [N_])
        mms([(pN[:, 0:128], T.Bh[:], T[K("PG")][:], 128), (pN[:, 0:128], Hh[:, 16:144], I(-1), 128),
             (pN[:, 0:128], T.nTri[:], T[K("fl")][:], 128)], ["Bh", K("PG"), K("Hh"), "I-1", "nTri", K("fl")], [K("G2")], [N_])
        if RU_ON == "S":
            act(T[K("rm")][:], pN[:, 0:128], F.Abs, [K("G2")], [K("ra")], 128, [N_])
            op("S", cyc(128), lambda: [S.activation(T[K("ru")][:], T[K("rm")][:], F.Relu, 1.0, -2.0)], [K("ra")], [K("ru")])
        else:
            ts(T[K("ru")][:], pN[:, 0:128], 0.0, None, A.is_equal, None, [K("G2")], [K("ru")], 128, [N_])
        tt(T[K("mo")][:], pA[:, 128:256], T[K("ru")][:], A.mult, [K("e0"), K("ru")], [K("mo")], 128, [A_])
        mms([(pN[:, 0:20], T.ones[0:1, :], T.rowk[0:1, 0:20], 64), (pN[:, 0:20], I(1), cb[:, 20:40], 64),
             (pN[:, 0:20], I(4), cb[:, 40:60], 64)], ["ones", "rowk", "I1", "I4", K("rem")], [K("G2")], [N_])
        mms([(pN[:, 128:256], T[K("ru")][:], I(2), 128),  (pN[:, 128:256], T[K("fi")][:], T.nSl[:], 128)],
            [K("ru"), K("fi"), "I2", "nSl"], [K("m")], [N_])
        mms([(pN[:, 256:384], T[K("fi")][:], I(1024), 128)], [K("fi"), "I1024"], [K("FI")], [N_])
        ts(cb[:, 60:80], pN[:, 0:20], 0.0, None, A.is_ge, None, [K("G2")], [K("flg")], 20, [N_])
        mms([(pN[:, 32:72], T.ones[0:1, :], T.rowk[0:1, 20:60], 64), (pN[:, 32:52], I(1), cb[:, 0:20], 64),
             (pN[:, 32:52], I(-4), cb[:, 40:60], 64), (pN[:, 32:52], I(128), cb[:, 60:80], 64), (pN[:, 52:72], I(128), cb[:, 60:80], 64),
             (pN[:, 36:52:5], I(112), cb[:, 63:80:5], 64), (pN[:, 56:72:5], I(128), cb[:, 63:80:5], 64),
             (pN[:, 36:72:5], T[K("mo")][:], T.B256[:], 64)],
            ["ones", "rowk", "I1", "I-4", "I128", "I112", "B256", K("rem"), K("flg"), K("mo")], [K("key"), K("G2")], [N_], True, False)

    def zpart(t, q):
        K = lambda s: "%s%d" % (s, q)
        pZ, Z_, pN, N_ = T[K("pZ")], K("pZ"), T[K("pN")], K("pN")
        yb = T["y%d" % t]
        subs = [0]
        held = []
        sizes = []
        later = {}

        def joined():
            ZK = [K("Z2"), K("Z3")]
            if MZ_ON == "V":
                mms([(pZ[:, 256:512], T.ones[0:1, :], T.rowm[0:1, :], 256)], ["ones", "rowm"], ZK, [Z_], True, False)
            else:
                mms([(pZ[:, 256:512], T.ones[0:1, :], T.rowb[0:1, :], 256), (pZ[:, 256:384], I(4096), T[K("ru")][:], 128),
                     (pZ[:, 384:512], I(4096), T[K("ru")][:], 128)], ["ones", "rowb", "I4096", K("ru")], ZK, [Z_], True, False)
                mms([(pN[:, 32 + k:72:5], T[K("ru")][:], T.Bneg[:], 64) for k in (2, 3)], ["Bneg", K("ru")], [], [N_], False, False)
            for l, dk, rk, tw in held:
                if tw:
                    mms(l[1:9], ["seln"] + dk, [], [Z_], False, False)
                    mms(l[9:17], ["seln"] + dk, [], [Z_], False, False)
            for k in JOIN:
                l, dk, rk, tw = held[k]
                mms(l[-16:-8], ["sel", "sel2"] + rk, [], [Z_], False, False)
                mms(l[-8:], ["sel", "sel2"] + rk, ZK if k == JOIN[-1] else [], [Z_], False, k == JOIN[-1])
            if MZ_ON == "S":
                act(T[K("mf")][:], pZ[:, 256:512], F.Relu, ZK, [K("mf")], 256, [Z_])
                mms([(pN[:, 32 + k:72:5], T[K("mf")][:, 128 * k - 256:128 * k - 128], T.B256f[:], 256) for k in (2, 3)],
                    ["B256f", K("mf")], [K("key")], [N_], False, True)
                return
            for k in (2, 3):
                ks = slice(128 * k, 128 * k + 128)
                tt(T[K("mz")][:, ks], pZ[:, ks], T[K("ru")][:], A.mult, ZK + [K("ru")], [K("mz%d" % k)], 128, [Z_])
                mms([(pN[:, 32 + k:72:5], T[K("mz")][:, ks], T.B256[:], 64)], ["B256", K("mz%d" % k)], [K("key")] if k == 3 else [], [N_],
                    False, k == 3)

        for n in ORDER:
            win = T.Xw[:, WIN[n][0]:WIN[n][1]]
            wk = X0 + ["X%d" % k for k in range(2 * n)]
            if t >= DIRECT:
                win = T.Xw[:, FAR[n][0]:FAR[n][1]]
                wk = X0 + ["X%d" % k for k in range(FAR[n][3])]
            d, r = T["d%d%d" % (n, q)], T["r%d%d" % (n, q)]
            two = "R" in ZT[q][n] or "D" in ZT[q][n]
            dks = []
            pend = []
            for h in range(4):
                ty = ZT[q][n][h]
                cs = slice(512 * h, 512 * h + 512)
                ys = slice(2048 * q + cs.start, 2048 * q + cs.stop)
                yk = "y%d_%d%d" % (t, q, h * XP // 4)
                nm = "z" if two and ty not in "RD" else "d"
                z, zk, rk = T["%s%d%d" % (nm, n, q)], K("%s%d_%d" % (nm, n, h)), K("r%d_%d" % (n, h))
                sc = 0.5 if two else None
                lk = K("lz%d_%d" % (n, h))

                def src(a, b, n=n, win=win):
                    return win.indirect(T[K("lz")][:, 128 * n + a // 16:128 * n + b // 16])
                if ty == "D":
                    zk = gather("S", (t, q, n, nm, "S"), cs.start, cs.stop,
                                lambda a, b, z=z, src=src: [S.activation(z[:, a:b], src(a, b), F.Copy, 0.0, -1.0)], wk + [lk], [zk])
                    pend.append((h, zk, yk, rk))
                    if len(pend) == GD or h == 3 or ZT[q][n][h + 1] != "D":
                        c2 = slice(512 * pend[0][0], cs.stop)
                        zs = [k for p in pend for k in p[1]]
                        i = op("G", GDMA, lambda c2=c2, z=z: g.dma_start(z[:, c2], yb[:, 2048 * q + c2.start:2048 * q + c2.stop], accum_op=A.add),
                               zs + [p[2] for p in pend], zs, (), 0.0, "ac%d%d%d" % (q, n, h), 16)
                        op("D", 2 * DMA * len(pend), None, zs, zs, (), ACC)
                        ops[-1]["same"] = i
                        for p in pend:
                            c5 = slice(512 * p[0], 512 * p[0] + 512)
                            ts(r[:, c5], z[:, c5], 0.0, None, A.max, None, p[1], [p[3]], 512, half=True)
                        pend = []
                elif ty == "S":
                    zk = gather("S", (t, q, n, nm, "S"), cs.start, cs.stop,
                                lambda a, b, z=z, src=src: [S.activation(z[:, a:b], src(a, b), F.Copy)], wk + [lk], [zk])
                    if len(sizes) >= LAG:
                        ops[lastw[zk[0]]]["order"].add(sizes[-LAG])
                    subs[0] += 1
                    other = subs[0] > TWOB and subs[0] % 2 == 0
                    bk, ks = (K("pA"), [K("e1"), K("e0"), K("G1"), K("DT")]) if other else (K("pS"), [K("sub")])
                    mms([(T[bk][:], I(1), z[:, cs], 512), (T[bk][:], I(-1), yb[:, ys], 512)], ["I1", "I-1", yk] + zk, ks, [bk])
                    act(r[:, cs], T[bk][:], F.Abs, ks, [rk], 512, [bk], sc)
                    sizes.append(len(ops) - 1)
                else:
                    zk = gather("V", (t, q, n, nm, "V"), cs.start, cs.stop,
                                lambda a, b, z=z, src=src: [V.tensor_tensor(z[:, a:b], src(a, b), yb[:, 2048 * q + a:2048 * q + b], A.subtract)],
                                wk + [yk, lk], [zk])
                    if ty == "R":
                        ts(r[:, cs], z[:, cs], 0.0, None, A.max, None, zk, [rk], 512, half=True)
                    else:
                        act(r[:, cs], z[:, cs], F.Abs, zk, [rk], 512, (), sc)
                dks += zk if ty in "RD" else [K("d%d_%d" % (n, h))]
            ns = slice(128 * n, 128 * n + 128)
            lst = [(pZ[:, ns], T.ones[0:1, :], T.rowm[0:1, 0:128], 128)]
            if two:
                lst += [(pZ[:, 128 * n + i:128 * n + 128:16], d[:, i:2048:16], T.seln[:], 64) for i in range(16)]
            lst += [(pZ[:, 128 * n + i:128 * n + 128:16], r[:, i:2048:16], T.sel2[:] if two else T.sel[:, 0:8], 64) for i in range(16)]
            if JOIN and n >= 2:
                held.append((lst, dks, [K("r%d_%d" % (n, s)) for s in range(4)], two))
                continue
            later[n] = (lst, dks, two)
        for n in SUMO:
            if n not in later:
                continue
            lst, dks, two = later[n]
            ns = slice(128 * n, 128 * n + 128)
            cuts = [0] + list(range(1 + PS, len(lst), PS)) + [len(lst)]
            for a, b in zip(cuts, cuts[1:]):
                R = (dks if two and a < 17 else []) + [K("r%d_%d" % (n, s)) for s in range(4) if b > 17 or not two]
                mms(lst[a:b], ["ones", "rowm", "sel", "sel2", "seln"] + R, [K("Z%d" % n)] if a == 0 or b == len(lst) else [], [Z_],
                    a == 0, b == len(lst))
            tt(T[K("mz")][:, ns], pZ[:, ns], T[K("ru")][:], A.mult, [K("Z%d" % n), K("ru")], [K("mz%d" % n)], 128, [Z_])
            mms([(pN[:, 32 + n:72:5], T[K("mz")][:, ns], T.B256[:], 64)], ["B256", K("mz%d" % n)], [K("key")], [N_], False, n == SUMO[3] and not JOIN)
        if JOIN:
            joined()

    def fin(t, q):
        K = lambda s: "%s%d" % (s, q)
        pN, N_ = T[K("pN")], K("pN")
        cf, ch, Hh, Dp = T[K("cf")], T[K("ch")], T[K("Hh")], T[K("Dp")]
        last = t == RO - 1
        if last:
            ts(T[K("oD")][:], Dp[:], -FR, None, A.add, None, [K("Dp")], [K("oD")], 128)
            ts(T[K("oH")][:], Hh[:, 16:144], -0.5, None, A.add, None, [K("Hh")], [K("oH")], 128)
            tt(T[K("oA")][:], T.Ab[:, 4 * q:4 * q + 4], ch[:, 0:4], A.add, ["Ab", K("a")], [K("oA")], 4)
        op("V", cyc(64), lambda: [V.tensor_tensor_scan(cf[:, 104:144], T.rs[:], pN[:, 32:72], 0.0, A.add, A.min)],
           [K("key"), "rs"], [K("sc")], [N_])
        tt(cf[:, 92:96], cf[:, 107:124:5], cf[:, 108:124:5], A.is_gt, [K("sc")], [K("mut")], 4)
        tt(cf[:, 100:104], cf[:, 108:124:5], cf[:, 128:144:5], A.subtract, [K("sc")], [K("df")], 4)
        fik = [K("f%d" % b) for b in range(4)]
        for b in range(4):
            ps = pN[:, 256 + 32 * b:288 + 32 * b]
            ts(ps, ps, cf[:, 92 + b:93 + b], cf[:, 64 + b:65 + b], A.mult, A.mult, [K("FI"), K("mut"), K("dd")], [fik[b]], 32, [N_])
        mk = [K("m%d" % b) for b in range(4)]
        for b in range(4):
            ps = pN[:, 128 + 32 * b:160 + 32 * b]
            ts(ps, ps, cf[:, 92 + b:93 + b], cf[:, 100 + b:101 + b], A.is_gt, A.mult, [K("m"), K("mut"), K("df")], [mk[b]], 32, [N_])
        if last:
            tt(T[K("oD")][:], pN[:, 256:384], T[K("oD")][:], A.add, fik + [K("oD")], [K("oD")], 128, [N_])
            tt(T[K("oH")][:], pN[:, 128:256], T[K("oH")][:], A.add, mk + [K("oH")], [K("oH")], 128, [N_])
            tt(T[K("oA")][:], T[K("oA")][:], cf[:, 92:96], A.add, [K("oA"), K("mut")], [K("oA")], 4)
            for nm, y, n in (("oD", T.yD, 128), ("oH", T.yH, 128), ("oA", T.yA, 4)):
                load(y[:, n * q:n * q + n], T[K(nm)][:], "out", [], 2000.0, [K(nm)])
            return
        tt(Dp[:], pN[:, 256:384], Dp[:], A.add, fik + [K("Dp")], [K("Dp"), K("FI")], 128, [N_])
        if HCOPY:
            tt(pN[:, 128:256], pN[:, 128:256], Hh[:, 16:144], A.add, mk + [K("Hh")], [K("m")], 128, [N_])
        else:
            tt(Hh[:, 16:144], pN[:, 128:256], Hh[:, 16:144], A.add, mk + [K("Hh")], [K("Hh"), K("m")], 128, [N_])
        tt(ch[:, 0:4], ch[:, 0:4], cf[:, 92:96], A.add, [K("a"), K("mut")], [K("a")], 4)

    for q in range(2):
        chunk[0] = q - LEAD
        xpart(0, q)
    chunk[0] = 2
    konst()
    for k in range(6):
        a = 4096 - 2048 * (k // 2) if k % 2 == 0 else 10240 + 2048 * (k // 2)
        c = 6144 + (a - 6144) % 4096
        out, src = T.Xw[:, a:a + 2048], T.Xw[:, c:c + 2048]
        if COPY[k] == "V":
            for o in range(0, 2048, CW):
                cp(T.Xw[:, a + o:a + o + CW], T.Xw[:, c + o:c + o + CW], X0, ["X%d" % k], CW, half=True)
        elif COPY[k] == "S":
            for o in range(0, 2048, CW // 2):
                act(T.Xw[:, a + o:a + o + CW // 2], T.Xw[:, c + o:c + o + CW // 2], F.Copy, X0, ["X%d" % k], CW // 2)
        else:
            load(out, src, "lb%d" % k, ["X%d" % k], 3500.0 + CPL * k, X0 + ["y0_0%d" % CPH])
    for t in range(RO):
        for q in range(2):
            chunk[0] = 2 * t + q - LEAD
            if t:
                where[:] = [2 * t + q, "x", 0]
                xpart(t, q)
            where[:] = [2 * t + q, "g" if t else "g0", 0]
            gpart(t, q)
            where[:] = [2 * t + q, "e" if t else "e0", 0]
            if (t, q) == (0, 1):
                chunk[0] = LATE
            epart(t, q)
            chunk[0] = 2 * t + q
            where[:] = [2 * t + q, "z", 0]
            zpart(t, q)
            chunk[0] = 2 * t + q + 2 - LEAD
            where[:] = [2 * t + q, "f" if t < RO - 1 else "f9", 0]
            fin(t, q)
        where[:] = [None, "end%d" % t, 0]
        if t < RO - 1:
            op("loc%d" % t, 0.0, None, (), ["loc%d" % t], (), 1000.0, "loc%d" % t, left[t])
            ops[-1]["order"].add(sent[0])
        if t == 0:
            for k, (a, b, c) in enumerate(((16384, 18432, 8192), (18432, 22528, 6144), (22528, 26624, 6144), (26624, XW, 6144))):
                if MORE[k] == "Y":
                    load(T.Xw[:, a:b], T.Xw[:, c:c + b - a], "lc%d" % k, ["X%d" % (6 + k)], 5000.0 + 4000.0 * k, X0 + ["loc0"])
                else:
                    for o in range(0, b - a, CW):
                        e = min(o + CW, b - a)
                        cp(T.Xw[:, a + o:a + e], T.Xw[:, c + o:c + e], X0, ["X%d" % (6 + k)], e - o, half=True)

    for beat in BEAT:
        prev = None
        for h in range(FROM, 2 * RO + 1):
            for w in beat.split():
                i = named.get((h + {"-": -1, "+": 1}.get(w[0], 0), w.lstrip("+-")))
                if i is not None:
                    if prev is not None:
                        ops[i]["order"].add(prev)
                    prev = i
    if "seq" not in PLAN:
        PLAN["seq"] = tighten(ops, schedule(ops))
    seq = PLAN["seq"]
    SEM = {"V": "sv", "S": "ss", "P": "sp", "G": "sg"}
    ENG = {"V": g.vector, "S": g.scalar, "P": g.tensor, "G": g, "Y": g.sync}
    count = {"sv": 0, "ss": 0, "sp": 0, "sg": 0, "out": 0}
    val = {}
    clock = {q: {} for q in ENG}
    tail = {q: {} for q in ENG}
    fin_clock = {}
    after, prev = {}, {}
    for i in seq:
        q = ops[i]["q"]
        after[prev.get(q)] = i
        prev[q] = i
    for i in seq:
        o = ops[i]
        q = o["q"]
        if i in val:
            continue
        if "same" in o:
            val[i], fin_clock[i] = val[o["same"]], fin_clock[o["same"]]
            continue
        if q not in ENG:
            val[i] = (o["sem"], o["inc"])
            fin_clock[i] = {o["sem"]: o["inc"]}
            continue
        parts = [i]
        if "run" in o:
            run, lo, hi, make = o["run"]
            j = after.get(i)
            while (j is not None and "run" in ops[j] and ops[j]["run"][0] == run and ops[j]["run"][1] == hi and hi - lo < UMAX
                   and all(k in val for k in ops[j]["hard"])):
                parts.append(j)
                hi = ops[j]["run"][2]
                j = after.get(j)
            o["fn"] = lambda: make(lo, hi)
        cur = clock[q]
        need = {}
        for j in set().union(*[ops[k]["hard"] for k in parts]):
            if j in val:
                s, v = val[j]
                if cur.get(s, 0) < v and need.get(s, (0, 0))[0] < v:
                    need[s] = (v, j)
        for s in sorted(need, key=lambda s: -need[s][1]):
            v, j = need[s]
            if cur.get(s, 0) < v:
                ENG[q].wait_ge(T.sem[s], v)
                for a, b in fin_clock[j].items():
                    if cur.get(a, 0) < b:
                        cur[a] = b
        r = o["fn"]()
        if o["sem"]:
            r.then_inc(T.sem[o["sem"]], 16)
            count[o["sem"]] = count.get(o["sem"], 0) + 16
            val[i] = (o["sem"], count[o["sem"]])
            fin_clock[i] = dict(cur)
            fin_clock[i][o["sem"]] = count[o["sem"]]
        elif o["inc"]:
            s = SEM[q]
            for x in r:
                x.then_inc(T.sem[s], 1)
            count[s] += len(r)
            val[i] = (s, count[s])
            d = tail[q]
            for a, b in cur.items():
                if d.get(a, 0) < b:
                    d[a] = b
            d[s] = count[s]
            fin_clock[i] = dict(d)
            for k in parts[1:]:
                val[k], fin_clock[k] = val[i], fin_clock[i]
    g.sync.wait_ge(T.sem.out, count["out"])
    for s in ("sv", "ss", "sp", "sg"):
        g.wait_ge(T.sem[s], count[s])
    for t in range(RO):
        g.wait_ge(T.sem["loc%d" % t], left[t])
